import numpy as np, ml_dtypes
CORES = [51,54,179,182]
N = 4
BF = ml_dtypes.bfloat16
def gentries(a):
    return np.ascontiguousarray(a.reshape(8, 16, -1).transpose(0, 2, 1)).reshape(8, -1)
def gtable(e):
    e = np.asarray(e); return np.ascontiguousarray(e.reshape(8, -1, 16).transpose(0, 2, 1)).reshape(128, -1).astype(np.int32)
W, C, M, V, E = 2048, 256, 8, 6, 2
def parts(rng):
    u = rng.random((N, 8, 16, W), dtype=np.float32); z = rng.random((N, 8, 16, W), dtype=np.float32); ty = rng.integers(0, 3, (N, 8, 1, W))
    u = np.where(ty == 0, np.minimum(u, z), np.where(ty == 1, u, np.maximum(u, z)))
    here = rng.random((N, 8, 16, W)) < 0.35 + 0.65 * rng.random((N, 8, 1, W))
    x = np.where(here, np.minimum(1 + (255 * u).astype(np.int64), 255), 0)
    L = rng.integers(0, W, (N, 8, C, 16)); k = (rng.random((N, 8, C, 16)) < 0.25).astype(np.int64)
    o = np.argsort(rng.random((N, 8, W)), axis=-1)[..., :M * C]
    t = rng.integers(0, 256, (N, 8, 16, C)); w = rng.integers(0, 4096, (N, 8, 16)); th = rng.integers(3, 10, (N, 8, V))
    return x, L, k, np.ascontiguousarray(o), t, w, th
def deep(rng, x, L, k, o, th, g):
    n = C // 4; z = n * (M // 4); slots = np.concatenate([np.array([0]), 1 + rng.permutation(C - 2)[:n - 2], np.array([C - 1])])
    p = rng.permutation(W); u, d, full, none, half = p[:3], p[3:6], p[6:10], p[10:12], p[12:14]; used = p[14:14 + N * z].reshape(N, z)
    y = x[:, g]; y[..., u] = 1; y[..., used.reshape(-1)] = 1; y[..., full] = 255; y[..., none] = 0
    y[..., d] = np.where(np.argsort(rng.random((N, 16, 3)), axis=1) < 2, 255, 1)
    y[..., half] = np.where(np.argsort(rng.random((N, 16, 2)), axis=1) < 8, 255, 1)
    for r in range(N):
        a = np.zeros((C, M), np.int64); rest = np.ones((C, M), bool); rest[slots, ::4] = False
        a[~rest] = rng.permutation(used[r]); a[rest] = rng.permutation(np.setdiff1d(p, used[r]))[:M * C - z]
        o[r, g] = a.reshape(-1)
    kind = rng.integers(0, 3, (N, C, 1)); ff = rng.choice(full, (N, C, 16)); fe = rng.choice(np.concatenate([full, none]), (N, C, 16))
    a = np.where(kind < 2, fe, ff); a[..., 0] = np.where(kind[..., 0] == 2, rng.choice(u, (N, C)), a[..., 0]); b = np.where(kind < 2, rng.integers(0, 2, (N, C, 16)), 0)
    q = ff[:, slots]; q[..., 0] = rng.choice(u, (N, n)); q[..., 1:3] = rng.choice(d, (N, n, 2)); q[..., 3] = rng.choice(half, (N, n)); a[:, slots] = q; b[:, slots] = 1
    L[:, g] = a; k[:, g] = b; th[:, g] = rng.choice(np.array([8, 15]), (N, V)); th[:, g, :2] = 1
    if g == 7:
        th[:, g, 2:5] = 15; th[:, g, 5:] = 8
def pack(x, L, k, o, t, w, th):
    return {"dep": np.ascontiguousarray(x.reshape(N, 128, W)).astype(np.float32).astype(BF), "nam": np.stack([gtable(a.reshape(8, -1)) for a in L]), "mrk": np.stack([gtable(a.reshape(8, -1)) for a in k]),
            "own": np.stack([gtable(a) for a in o]), "pic": np.ascontiguousarray(t.reshape(N, 128, C)).astype(np.float32).astype(BF), "wt": w.reshape(N, 128, 1).astype(np.int32), "thr": np.ascontiguousarray(th).astype(np.int32)}
def setup_inputs(rng):
    return pack(*parts(rng))
def setup_inputs_spread(rng):
    x, L, k, o, t, w, th = parts(rng)
    x = np.minimum(np.exp2(8 * np.sqrt(rng.random((N, 8, 1, W))) * rng.random((N, 8, 16, W))).astype(np.int64) - 1, 255)
    t = np.minimum(np.exp2(8 * rng.random((N, 8, 16, C))).astype(np.int64) - 1, 255); w = np.minimum(np.exp2(12 * rng.random((N, 8, 16))).astype(np.int64) - 1, 4095)
    L = np.minimum((W * rng.random((N, 8, C, 16)) ** 3).astype(np.int64), W - 1); k = (rng.random((N, 8, C, 16)) < rng.random((N, 8, C, 1))).astype(np.int64)
    th = 1 + (14 * rng.random((N, 8, V)) ** 2).astype(np.int64)
    return pack(x, L, k, o, t, w, th)
def setup_inputs_ends(rng):
    x, L, k, o, t, w, th = parts(rng); lane = np.arange(16)[:, None]
    b = 255 * rng.integers(0, 2, (N, 8, 16, W)); q = rng.random((N, 8, 1, W))
    x = np.where(q < 0.2, b, np.where(q < 0.42, 255, np.where(q < 0.65, 1, np.where(q < 0.75, np.maximum(b, 1), np.where(q < 0.9, np.where(lane == 15, 1, 255), 0)))))
    for g in range(8):
        if g % 2 == 0 or g == 7:
            x[:, g, :, 0] = 1; x[:, g, :, W - 1] = 255
        else:
            x[:, g, :, 0] = 255; x[:, g, 15, 0] = 1; x[:, g, :, W - 1] = 1
    u = rng.random((N, 8, C, 16)); L = np.where(u < 0.36, 0, np.where(u < 0.72, W - 1, L)); k = rng.integers(0, 2, (N, 8, C, 16))
    L[:, 7, 0] = W - 1; L[:, 7, C - 1] = W - 1
    L[:, 7, 1] = 0; L[:, 7, C - 2] = 0; L[:, 7, 1, 15] = W - 1; L[:, 7, C - 2, 15] = W - 1; k[:, 7, 1] = 0; k[:, 7, C - 2] = 1
    h = (M * C) // 2; mid = np.concatenate([np.arange(1, M * C - h), np.arange(W - h, W - 1)]); c = (C - 1) * M
    for r in range(N):
        for g in range(8):
            p = rng.permutation(mid); o[r, g] = np.concatenate([p[:c], np.array([0]), p[c:c + M // 2 - 1], np.array([W - 1]), p[c + M // 2 - 1:]])
    t = 255 * rng.integers(0, 2, (N, 8, 16, C)); t[:, 7] = 255; w = 4095 * rng.integers(0, 2, (N, 8, 16)); w[:, 7] = 4095; w[:, 6, 0] = 4095; w[:, 3] = 0
    th = np.where(rng.random((N, 8, V)) < 0.6, 1, 15)
    return pack(x, L, k, o, t, w, th)
def setup_inputs_corners(rng):
    x, L, k, o, t, w, th = parts(rng); lane = np.arange(16)
    pal = [np.full(16, 100), np.full(16, 255), np.where(lane < 8, 200, 50), np.where((lane >= 8) & (lane < 8 + E), 10, 0), np.where((lane >= 8) & (lane < 7 + E), 10, 0),
           np.zeros(16, np.int64), np.full(16, 1), np.where(lane < 8, 101, 100), np.where(lane < 7, 101, 100), np.full(16, 200)]
    f = rng.choice(np.array([0, 5]), (N, 8, C, 16)); f[..., 0] = 0
    s = (np.arange(C) + rng.integers(0, 12, (N, 8, 1))) % 12
    f[s == 1, 15] = 2
    f[s == 2, 1] = 2
    f[s == 3, 1] = 2; f[s == 3, 15] = 3
    f[s == 4, 15] = 2; f[s == 4, 14] = 3; f[s == 4, 13] = 4
    f[s == 5, 2] = 2; f[s == 5, 1] = 3
    f[s == 6] = 3; f[s == 6, 0] = 0; f[s == 6, 1] = 2
    f[s == 7, 1] = 8; f[s == 7, 2] = 7; f[s == 7, 3] = 1
    f[s == 8, 0] = 5; f[s == 8, 1] = 1
    f[s == 9] = 1; f[s == 9, 0] = 6
    f[s == 10] = 0
    f[s == 11] = rng.integers(0, 10, (int(np.count_nonzero(s == 11)), 16))
    for g in range(8):
        if g == 3 or g == 6: continue
        q = rng.permutation(W)[:10]
        for i in range(10): x[:, g, :, int(q[i])] = pal[i]
        L[:, g] = q[f[:, g]]
    m = rng.integers(0, 3, (N, 8, C, 1)); k = np.where(m == 0, 1, np.where(m == 1, 0, k))
    th = rng.choice(np.array([1, 7, 8, 8, 9, 15]), (N, 8, V)); th[..., 0] = np.array([8, 7, 8, 1, 8, 7, 15, 8])
    k[:, 3] = 1; th[:, 3] = 1; k[:, 6] = 0; th[:, 6] = 15
    t[:, 0] = 0; t[:, 6] = 255; t[:, 2, :, ::2] = 255; w[:, 5] = 4095; w[:, 0, ::2] = 0
    deep(rng, x, L, k, o, th, 4); deep(rng, x, L, k, o, th, 7)
    return pack(x, L, k, o, t, w, th)
def setup_inputs_crowd(rng):
    x, L, k, o, t, w, th = parts(rng); lane = np.arange(16)
    pal = [np.full(16, 1), np.full(16, 255), np.where(lane == 15, 1, 255), np.where(lane < 8, 200, 120), np.where(lane < 8, 1, 0), np.full(16, 150)]
    for g in range(8):
        z = rng.permutation(W)[:6]
        for i in range(6): x[:, g, :, int(z[i])] = pal[i]
        if g % 4 == 0:
            odd = rng.integers(0, 16, (N, C, 1)) == np.arange(16); L[:, g] = np.where(odd, z[rng.integers(1, 3, (N, C, 1))], z[0])
        elif g % 4 == 1: L[:, g] = z[rng.integers(0, 6, (N, C, 16))]
        elif g % 4 == 2:
            L[:, g] = z[rng.integers(0, 6, (1, 1, 16))]; L[:, g, :, 0] = z[0]; L[:, g, :, 9] = z[2]
        else: L[:, g] = z[3]
        rest = np.setdiff1d(np.arange(W), z)
        for r in range(N): o[r, g] = rng.permutation(np.concatenate([z, rng.permutation(rest)[:M * C - 6]]))
    k = (rng.random((N, 8, C, 16)) < 0.5).astype(np.int64); th = rng.choice(np.array([1, 8, 14, 15]), (N, 8, V)); th[:, 1, 0] = 14; th[:, 5, 0] = 15; th[:, 0, 0] = 15; th[:, 2, 0] = 1
    return pack(x, L, k, o, t, w, th)
def setup_inputs_ranks(rng):
    x, L, k, o, t, w, th = parts(rng); q = rng.permutation(N)
    for i in (0, 2, 3):
        r = int(q[i]); th[r, :, 0] = 1; k[r] = 0 if i == 3 else 1
        for g in range(8):
            z = rng.permutation(W)[:2]; x[r, g, :, int(z[0])] = 1; x[r, g, :, int(z[1])] = 255
            a = L[r, g]; a[:, 0] = z[0]; a[np.arange(C), rng.integers(1, 16, C)] = z[1]
    k[int(q[2]), 7, C - 1] = 0; k[int(q[3]), 7, C - 1] = 1
    b = int(q[1]); th[b] = 15
    for g in range(8):
        e = rng.permutation(16)[:2]; y = x[b, g]; y[e] = rng.integers(1, 256, (2, 1))
        if g == 2 or g == 7:
            y[int(e[0])] = 2 * (2 * int(rng.integers(0, 64)) + 1); w[b, g] = 0; w[b, g, int(e[0])] = W // 2
    return pack(x, L, k, o, t, w, th)
def check_inputs(d):
    bad = []
    for a, lo, hi in (("dep", 0, 255), ("nam", 0, W - 1), ("mrk", 0, 1), ("own", 0, W - 1), ("pic", 0, 255), ("wt", 0, 4095), ("thr", 1, 15)):
        v = np.asarray(d[a]).astype(np.float64)
        if not (np.min(v) >= lo and np.max(v) <= hi): bad.append("range of " + a)
        elif np.any(v != np.floor(v)): bad.append("whole numbers of " + a)
    s = np.sort(np.stack([gentries(np.asarray(a)) for a in d["own"]]), axis=-1)
    if np.any(s[..., 1:] == s[..., :-1]): bad.append("distinct numbers of own")
    return bad
def reference(dep, nam, mrk, own, pic, wt, thr):
    X = dep.astype(np.float32).astype(np.int32).reshape(N, 8, 16, W)
    L = np.stack([gentries(a) for a in nam]).astype(np.int64).reshape(N, 8, C, 16); K = np.stack([gentries(a) for a in mrk]).astype(np.int64).reshape(N, 8, C, 16)
    O = np.stack([gentries(a) for a in own]).astype(np.int64).reshape(N, 8, C, M)
    T = pic.astype(np.float32).astype(np.int64).reshape(N, 8, 16, C); A = np.zeros((N, 8, C), np.int64); wv = wt.astype(np.int64).reshape(N, 8, 16, 1)
    row = np.arange(16)
    for v in range(V):
        G = np.take_along_axis(X, L.reshape(N, 8, 1, 16 * C), 3).reshape(N, 8, 16, C, 16)
        P = G[..., 0]
        cnt = np.add.reduce((P > 0)[..., None] & (G > P[..., None]), axis=2, dtype=np.int64)
        clash = cnt >= (thr[:, :, v].astype(np.int64)[..., None] + (A & 1))[..., None]
        some = np.any(clash, axis=3); k = np.argmax(clash, axis=3)
        km = np.take_along_axis(K, k[..., None], 3)[..., 0]
        none = ~some; turn = some & (km == 0); cut = some & (km == 1)
        T = np.where(none[:, :, None, :] & (P > 0), P, T)
        h = np.add.reduce(wv * T, axis=2) & (W - 1)
        xk = np.take_along_axis(G, k[:, :, None, :, None], 4)[..., 0]
        n = np.add.reduce(xk, axis=2, dtype=np.int64) & (M - 1)
        na = np.take_along_axis(O, n[..., None], 3)[..., 0]; nb = np.take_along_axis(O, (n ^ (M // 2))[..., None], 3)[..., 0]
        far = np.where(xk > P, xk, 0); near = np.where(xk <= P, xk, 0)
        enter = np.add.reduce((G > 0) & (G < near[..., None]), axis=2, dtype=np.int64) >= E
        j = np.where(np.any(enter, axis=3), np.argmax(enter, axis=3), 16)
        isk = row == k[..., None]; key = np.broadcast_to(4 * row, (N, 8, C, 16))
        key = np.where(none[..., None] & (row == 0), 999, key); key = np.where(turn[..., None] & isk, -1, key); key = np.where(cut[..., None] & isk, 999, key)
        ka = np.where(none, 100, np.where(cut, -1, 999)); kb = np.where(cut, 4 * j - 1, 999)
        order = np.argsort(np.concatenate([key, ka[..., None], kb[..., None]], axis=3), axis=3, kind="stable")[..., :16]
        L = np.take_along_axis(np.concatenate([L, np.where(none, h, na)[..., None], nb[..., None]], axis=3), order, 3)
        K = np.take_along_axis(np.concatenate([np.where(turn[..., None] & isk, 1, K), np.zeros((N, 8, C, 2), np.int64)], axis=3), order, 3)
        A = A + cut
        for r in range(N):
            for g in range(8):
                i = np.flatnonzero(cut[r, g])
                X[r, g][:, na[r, g, i]] = far[r, g][:, i]; X[r, g][:, nb[r, g, i]] = near[r, g][:, i]
        if v < V - 1: L, K, T, A = np.roll(L, 1, axis=0), np.roll(K, 1, axis=0), np.roll(T, 1, axis=0), np.roll(A, 1, axis=0)
    return {"ydep": X.reshape(N, 128, W).astype(np.float32).astype(BF), "ynam": np.stack([gtable(a.reshape(8, -1)) for a in L]).astype(np.float32), "ymrk": np.stack([gtable(a.reshape(8, -1)) for a in K]).astype(np.float32),
            "ypic": T.reshape(N, 128, C).astype(np.float32).astype(BF), "ycut": A.astype(np.float32)}

@@ -1,0 +1,676 @@
+import numpy as np
+from concourse.bass import DstId, RemoteDMATransfer
+from concourse.mybir import AluOpType, ActivationFunctionType
+
+W, C, NV = 2048, 256, 6
+CHUNKS = [64, 64, 64, 64]
+SGROUPS = [[0, 1, 2], [3]]
+ASUB = 16
+BGROUPS = [[0, 1, 2, 3]]
+SEED, NOISE, ROUNDS = 0, 60.0, 12
+SEARCH, DB = [], []
+OFFS = {'T': 16093, 'g0': 480, 'c0': -589, 'h0': 423, 'o0': 2826, 'f0': 6082, 'm0': -1422, 'b0': 6545, 'l0': 9588, 'e0': 3410,
+        't0': 11120, 's0': 9900, 'g1': -1383, 'c1': 1383, 'h1': 4034, 'o1': 6007, 'f1': 6781, 'm1': 3148, 'b1': 6655, 'l1': 6783,
+        'e1': 6407, 't1': 12453, 's1': 15980, 'g2': 2416, 'c2': 6176, 'h2': 8526, 'o2': 585, 'f2': 6920, 'm2': 6205, 'b2': 13554,
+        'l2': 1749, 'e2': 11308, 't2': 13370, 's2': 8916, 'g3': 5505, 'c3': 5737, 'h3': 6239, 'o3': 8427, 'f3': 8646, 'm3': 7045,
+        'b3': 10709, 'l3': 19177, 'e3': 13382, 't3': 17145, 's3': 11632}
+MODELS = [{}, {"ga": 0.7, "sc": 0.5, "xsend": 1.2}, {"ga": 1.3, "sc": 1.5, "xsend": 0.7}, {"p": 1.5, "xc": 1.5},
+          {"ga": 1.3, "sc": 0.6, "xc": 0.6}, {"ga": 0.75, "sc": 1.4, "xc": 2.0, "send": 1.5}]
+GSUB = 32
+KB = 5
+MKP = True
+VG, VG0 = [96, 160], [160]
+WIN = W + 512
+GATH, SCAT, PEC, LAT, DMAL, COMM = 1.56, 3.8, 0.5, 90.0, 2400.0, 2500.0
+SENDC = 700.0
+
+BF, HF, F4, I4, U2 = "bfloat16", "float16", "float32", "int32", "uint16"
+SB = {
+    "y": (WIN, BF), "x0": (W, BF), "z0": (W, BF), "yo": (W, BF),
+    "nami": (C, I4), "mrki": (C, I4), "owni": (C // 2, I4), "picb": (C, BF), "wti": (4, I4), "thri": (8, I4),
+    "G": (16 * C, BF), "Gp": (16 * C, BF), "c1": (16 * C, BF), "c2": (16 * C, BF),
+    "nm": (NV * C, U2), "Z": (NV * C, HF), "Tp": (NV * C, HF), "S": (NV * C, BF),
+    "nmo": (NV * C, U2), "Zo": (NV * C, HF), "Tpo": (NV * C, HF), "So": (NV * C, BF),
+    "cl": (C, BF), "isk": (C, BF), "Zk": (C, HF), "Za": (C, HF), "Zs": (C, HF), "nc": (C, BF), "xk": (2 * C, BF),
+    "FB": (2 * C, BF), "t1": (C, HF), "q": (C, I4), "J": (C, HF), "A1": (C, HF), "pr": (C, HF), "e": (C, BF),
+    "X": (C, BF), "Q": (C, F4), "aZ": (C, F4), "a128": (16, BF), "WS": (144, BF), "offk": (128, U2), "a8": (32, BF),
+    "offs": (32, U2), "cix": (C, BF), "W2": (144, BF), "WC": (144, HF), "OwnT": (C, HF), "owe": (C // 2, HF), "owo": (C // 2, HF),
+    "onm": (C, F4), "omk": (C, F4), "opc": (C, BF), "oct": (C, F4),
+    "ta": (C, F4), "tb": (C, F4), "thb": (8, BF), "thc": (8, F4), "wm": (4, I4), "wc": (4, F4),
+    "pi": (4, I4), "si": (4, I4), "col": (48, F4), "jj": (16, F4), "MK": (16, F4), "OH": (16, F4),
+    "m4": (128, BF), "m5": (128, BF), "E1": (128, BF), "E": (128, BF), "Rr": (128, BF), "m1": (128, BF), "m2": (128, BF), "m3": (128, BF),
+    "u0": (144, BF), "Wd": (144, BF), "Wh": (144, HF), "WA": (144, HF), "WB": (144, HF), "Eg": (128, BF), "Eg0": (128, BF),
+    "one": (128, BF),
+}
+for _m in ("I", "nI", "N2", "D14", "Is", "ON", "GT", "LT", "Mr", "Mv", "Mpar", "B2", "nB2", "Mx", "Mnc", "Msm", "Msg"):
+    SB[_m] = (128, BF)
+for _m in ("Ih", "ONh", "Sm", "ISm", "SI", "IR", "Pm", "Pm2", "M15", "Mw", "Mpr", "Mdi", "h1", "h2"):
+    SB[_m] = (128, HF)
+SB["SI4"] = (128, F4)
+SCRATCH = {k: ("sbuf", [128, n], d) for k, (n, d) in SB.items()}
+for _b in range(8):
+    SCRATCH["ps%d" % _b] = ("psum", [128, 512], F4)
+NCH = len(CHUNKS)
+LOADS = ["nam", "dep0", "dep1", "mrk", "thr", "pic", "own", "wt"]
+SEMAPHORES = (["qv", "qa", "qp", "qg", "sent", "stored"] + ["ld_" + k for k in LOADS]
+              + ["r%s%d_%d" % (k, v, c) for k in "ab" for v in range(1, NV) for c in range(NCH)])
+AL, AF = AluOpType, ActivationFunctionType
+
+
+def V(name, lo, hi, step=1, p=None):
+    return (name, lo, hi, step, p)
+
+
+def ap(T, v):
+    name, lo, hi, step, p = v
+    rows = slice(0, 128) if p is None else slice(p[0], p[1])
+    return T[name][rows, lo:hi] if step == 1 else T[name][rows, lo:hi:step]
+
+
+def nel(v):
+    return len(range(v[1], v[2], v[3]))
+
+
+def isv(x):
+    return isinstance(x, tuple)
+
+
+def two(*vs):
+    return all(v[0] in SB and SB[v[0]][1] in (BF, HF, U2) for v in vs)
+
+
+def regions():
+    out = []
+    for ci, n in enumerate(CHUNKS):
+        if NCH == 2:
+            b = [2 + 3 * ci, 3 + 3 * ci, 4 + 3 * ci]
+            t = {"Pp": (0, 0), "Bp": (0, 1), "Sp": (0, 2), "oT": (0, 3), "R": (1, 0), "D": (1, 0), "val": (1, 0), "mk": (1, 1),
+                 "Wp": (1, 1), "ma": (1, 2), "Tab": (2, 1), "ms": (1, 3), "u": (1, 3), "Zsum": (2, 0), "L1": (2, 0),
+                 "ZT": (2, 1), "U": (2, 2), "new": (2, 2), "nU": (2, 3)}
+            out.append({k: V("ps%d" % b[i], 128 * s, 128 * s + n) for k, (i, s) in t.items()})
+        elif NCH == 3:
+            ob, mb = 2 + 2 * ci, 3 + 2 * ci
+            t = {"Pp": (ob, 0), "Bp": (ob, 1), "Sp": (ob, 2), "oT": (ob, 4), "R": (mb, 0), "D": (mb, 0), "val": (mb, 0),
+                 "mk": (ob, 3), "Wp": (ob, 3), "ma": (ob, 3), "Tab": (mb, 3), "ms": (mb, 1), "u": (mb, 1), "Zsum": (mb, 2),
+                 "L1": (mb, 2), "ZT": (mb, 3), "U": (mb, 4), "new": (mb, 4), "nU": (ob, 2)}
+            out.append({k: V("ps%d" % b, 96 * s, 96 * s + n) for k, (b, s) in t.items()})
+        else:
+            ob, mb, h = 2 + ci % 2, 4 + ci, 4 * (ci // 2)
+            t = {"Pp": (ob, h), "Bp": (ob, h + 1), "Sp": (ob, h + 2), "oT": (ob, h + 3), "R": (mb, 0), "D": (mb, 0), "val": (mb, 0),
+                 "mk": (mb, 1), "Wp": (mb, 1), "ma": (mb, 2), "Tab": (mb, 5), "ms": (mb, 3), "u": (mb, 3), "Zsum": (mb, 4),
+                 "L1": (mb, 4), "ZT": (mb, 5), "U": (mb, 6), "new": (mb, 6), "nU": (mb, 7)}
+            out.append({k: V("ps%d" % b, 64 * s, 64 * s + n) for k, (b, s) in t.items()})
+    return out
+
+
+def build():
+    ops = []
+    tag = [None]
+
+    def add(eng, cost, reads, writes, fn, kind="c", sem=None, after=None, ck=None):
+        ops.append({"e": eng, "cost": cost, "r": [r for r in reads if isv(r)], "w": writes, "fn": fn, "kind": kind, "sem": sem,
+                    "after": after, "ck": ck or (kind if kind != "c" else eng), "tag": tag[0], "cont": False})
+        return len(ops) - 1
+
+    def a_(T, x):
+        return ap(T, x) if isv(x) else x
+
+    def ts(out, in0, s1, op0, s2=None, op1=None):
+        n = nel(in0) * (0.5 if two(out, in0) else 1.0)
+        if op1 is None:
+            f = lambda g, T: g.vector.tensor_scalar(ap(T, out), ap(T, in0), a_(T, s1), None, op0)
+        else:
+            f = lambda g, T: g.vector.tensor_scalar(ap(T, out), ap(T, in0), a_(T, s1), a_(T, s2), op0, op1)
+        add("v", max(64, n), [in0, s1, s2], [out], f)
+
+    def cp(out, in0):
+        n = nel(in0) * (0.5 if two(out, in0) else 1.0)
+        add("v", max(64, n), [in0], [out], lambda g, T: g.vector.tensor_copy(ap(T, out), ap(T, in0)))
+
+    def tt(out, in0, in1, op):
+        n = nel(in0) * (2.0 if in0[0] in SB and in1[0] in SB else 1.0)
+        add("v", max(64, n), [in0, in1], [out], lambda g, T: g.vector.tensor_tensor(ap(T, out), ap(T, in0), ap(T, in1), op))
+
+    def ms(out, c):
+        add("v", max(64, nel(out) * (0.5 if two(out) else 1.0)), [], [out], lambda g, T: g.vector.memset(ap(T, out), c))
+
+    def act(out, in0, func, bias=0.0, scale=1.0):
+        add("a", max(80, nel(in0)), [in0, bias], [out],
+            lambda g, T: g.scalar.activation(ap(T, out), ap(T, in0), func, bias=a_(T, bias), scale=scale))
+
+    def gather(out, off, win=V("y", 0, W), vec=False):
+        if vec:
+            return add("v", 60 + GATH * nel(out), [win, off], [out],
+                       lambda g, T: g.vector.tensor_copy(ap(T, out), ap(T, win).indirect(ap(T, off))), ck="ga")
+        add("a", 80 + GATH * nel(out), [win, off], [out],
+            lambda g, T: g.scalar.activation(ap(T, out), ap(T, win).indirect(ap(T, off)), AF.Identity), ck="ga")
+
+    def mm(out, terms, first=True, last=True, whole=None):
+        cost = sum(max(64, nel(r)) * (4 if SB[r[0]][1] == F4 else 1) for l, r in terms) * PEC + 20
+
+        def f(g, T):
+            ins = None
+            for i, (l, r) in enumerate(terms):
+                ins = g.tensor.matmul(ap(T, out), ap(T, l), ap(T, r), first and i == 0, last and i == len(terms) - 1)
+            return ins
+        i = add("p", cost, [x for t in terms for x in t], [whole or out], f)
+        ops[i]["cont"] = not first
+
+    def iota(out, pat, base, cm):
+        if SB[out[0]][1] == I4:
+            f = lambda g, T: g.iota(ap(T, out), pat, base, cm)
+        else:
+            f = lambda g, T: g.iota(ap(T, out), pat, base, cm, allow_small_or_imprecise_dtypes=True)
+        add("g", 160 + 2 * nel(out), [], [out], f)
+
+    def asel(out, in0, pat, op, fill, base, cm):
+        add("g", 210 + 2 * nel(out), [in0], [out], lambda g, T: g.affine_select(ap(T, out), ap(T, in0), pat, op, fill, base, cm))
+
+    def load(name, out, src, eng="s"):
+        if eng == "g":
+            f = lambda g, T: g.dma_start(ap(T, out), src(T), allow_slow_non_contiguous=True)
+        else:
+            f = lambda g, T: g.sync.dma_start(ap(T, out), src(T))
+        add(eng, 100, [], [out], f, "dma", "ld_" + name)
+
+    def store(dst, src):
+        add("s", 100, [src], [], lambda g, T: g.sync.dma_start(dst(T), ap(T, src)), "dma", "stored")
+
+    M = lambda k: V(k, 0, 128)
+    sel = lambda k, r: V(k, 15 - r, 143 - r)
+    sel2 = lambda k, b: V(k, 14 - 2 * b, 142 - 2 * b)
+    names = {}
+
+    def col(k):
+        if k not in names:
+            names[k] = len(names)
+        return V("col", names[k], names[k] + 1)
+    MK = lambda j: V("MK", j, j + 1)
+    OH = lambda j: V("OH", j, j + 1)
+
+    load("nam", V("nami", 0, C), lambda T: T.nam[:])
+    load("dep0", V("x0", 0, W // 2), lambda T: T.dep[:, 0:W // 2])
+    load("dep1", V("x0", W // 2, W), lambda T: T.dep[:, W // 2:W])
+    load("mrk", V("mrki", 0, C), lambda T: T.mrk[:])
+    load("thr", V("thri", 0, NV, 1, (0, 8)), lambda T: T.thr[:])
+    load("pic", V("picb", 0, C), lambda T: T.pic[:])
+    load("own", V("owni", 0, C // 2), lambda T: T.own[:])
+    E0 = V("u0", 15, 143)
+    iota(V("u0", 0, 144), [[1, 144]], -15, -1)
+    iota(V("pi", 0, 1), [[0, 1]], 0, 1)
+    asel(M("E1"), E0, [[16, 8], [0, 16]], AL.is_ge, 200.0, 15, -1)
+    asel(M("E"), M("E1"), [[-16, 8], [0, 16]], AL.is_ge, 200.0, 0, 1)
+    cp(col("p"), V("pi", 0, 1))
+    ts(V("jj", 0, 16), V("u0", 15, 31), col("p"), AL.add)
+    ms(M("one"), 1.0)
+    asel(V("Eg0", 0, 128, 1, (0, 8)), V("one", 0, 128, 1, (0, 8)), [[1, 128]], AL.is_ge, 0.0, 0, -16)
+    asel(V("Eg", 0, 128, 1, (0, 8)), V("Eg0", 0, 128, 1, (0, 8)), [[-1, 128]], AL.is_ge, 0.0, 15, 16)
+    ts(V("a8", 0, 32), V("u0", 15, 47), col("p"), AL.add, 8.0, AL.mult)
+    ts(V("cix", 0, 128), E0, col("p"), AL.add, 1.0, AL.add)
+    ts(V("cix", 128, 256), E0, col("p"), AL.add, 129.0, AL.add)
+    load("wt", V("wti", 0, 1), lambda T: T.wt[:], "g")
+    ts(M("nI"), E0, 0.0, AL.is_equal, -1.0, AL.mult)
+    ts(M("Is"), E0, 0.0, AL.is_equal, 1.0 / 256, AL.mult)
+    ts(M("I"), E0, 0.0, AL.is_equal)
+    ts(M("Ih"), E0, 0.0, AL.is_equal)
+    ts(V("si", 0, 1), V("pi", 0, 1), 15, AL.bitwise_and)
+    s = col("s")
+    cp(s, V("si", 0, 1))
+    ts(col("ns"), s, -1.0, AL.mult)
+    ts(V("Wd", 0, 144), V("u0", 0, 144), col("ns"), AL.is_equal)
+    ts(V("Wh", 0, 144), V("u0", 0, 144), col("ns"), AL.is_equal)
+    tt(V("W2", 0, 142), V("Wd", 0, 142), V("Wd", 1, 143), AL.add)
+    ts(V("WS", 0, 142), V("W2", 0, 142), s, AL.mult)
+    ts(V("si", 1, 2), V("si", 0, 1), 1, AL.arith_shift_right)
+    cp(col("s2"), V("si", 1, 2))
+    ts(col("s16"), col("s2"), 16.0, AL.mult)
+    ts(V("a128", 0, 16), V("jj", 0, 16), 128.0, AL.mult)
+    ts(V("MK", 0, 16), V("jj", 0, 16), s, AL.is_le)
+    ts(V("OH", 0, 16), V("jj", 0, 16), s, AL.is_equal)
+    ts(M("ON"), M("E"), 100.0, AL.is_lt)
+    ts(M("ONh"), M("E"), 100.0, AL.is_lt)
+    ts(M("GT"), M("E"), 0.0, AL.is_lt)
+    ts(M("B2"), M("E"), 100.0, AL.is_lt, 2.0, AL.mult)
+    ts(M("nB2"), M("E"), 100.0, AL.is_lt, -2.0, AL.mult)
+    ts(M("m1"), M("E"), 0.5, AL.is_lt)
+    tt(M("LT"), M("ON"), M("m1"), AL.subtract)
+    tt(M("m2"), M("I"), M("LT"), AL.subtract)
+    ts(M("Mr"), M("m2"), 0.5, AL.mult)
+    tt(M("Mv"), M("Mr"), M("LT"), AL.max)
+    ts(col("np"), OH(0), -1.0, AL.mult)
+    ts(M("Mpar"), M("ON"), col("np"), AL.mult)
+    ts(col("isk"), s, -0.5, AL.mult, 0.5, AL.add)
+    ts(col("x"), s, -1.0, AL.mult, 1.5, AL.add)
+    ts(col("sg"), OH(0), OH(1), AL.subtract, 0.5, AL.mult)
+    ts(col("nsg"), col("sg"), -1.0, AL.mult)
+    ts(M("Msg"), M("I"), col("sg"), AL.mult)
+    ts(col("ncb"), OH(15), 8192.0, AL.mult, 0.5, AL.add)
+    ts(M("N2"), M("B2"), OH(0), AL.mult)
+    ts(col("cn"), OH(15), -1.0 / 32, AL.mult, 1.0 / 32, AL.add)
+    ts(col("bq"), OH(15), -0.5 - 2.0 ** -12, AL.mult)
+    ts(M("Msm"), sel("Wd", 15), 1.5 * 2 ** 25, AL.mult)
+    ts(M("Rr"), M("E"), s, AL.add)
+    ts(M("m4"), M("Rr"), 8.0, AL.is_lt, 32.0, AL.mult)
+    ts(M("m5"), M("Rr"), 12.0, AL.is_lt, 64.0, AL.mult)
+    tt(M("Mx"), M("m5"), M("m4"), AL.subtract)
+    tt(M("m1"), M("Mx"), M("Rr"), AL.mult)
+    ts(M("m2"), M("ON"), 8.0, AL.mult)
+    ts(V("m2", 15, 128, 16), V("ON", 15, 128, 16), 0.125, AL.mult)
+    tt(M("m3"), M("m2"), M("m1"), AL.subtract)
+    ts(M("m1"), M("m3"), OH(15), AL.mult, 1.0 / 256, AL.mult)
+    ts(M("m2"), M("I"), col("cn"), AL.mult)
+    tt(M("Mnc"), M("m1"), M("m2"), AL.add)
+    ts(col("lo8"), MK(8), -1.0, AL.mult, 1.0, AL.add)
+    ts(M("Sm"), M("E"), -1.0, AL.is_equal)
+    tt(M("ISm"), M("Ih"), M("Sm"), AL.subtract)
+    ts(M("h1"), M("E"), 1.0, AL.is_equal)
+    tt(M("SI"), M("h1"), M("Ih"), AL.subtract)
+    cp(M("SI4"), M("SI"))
+    ts(M("h2"), sel("Wh", 0), -1.0, AL.mult)
+    tt(M("IR"), M("h2"), M("Ih"), AL.subtract)
+    ts(col("a"), col("lo8"), OH(13), AL.add)
+    ts(M("Pm"), sel("Wh", 0), col("a"), AL.mult)
+    ts(col("n1"), MK(8), 2.0, AL.mult, -1.0, AL.add)
+    ts(col("lo13"), MK(13), -1.0, AL.mult, 1.0, AL.add)
+    ts(col("nb"), col("n1"), col("lo13"), AL.mult)
+    ts(M("h1"), M("ONh"), col("nb"), AL.mult)
+    tt(M("Pm2"), M("Pm"), M("h1"), AL.subtract)
+    ts(col("wa"), col("lo8"), OH(12), AL.subtract, OH(14), AL.subtract)
+    ts(col("w9"), OH(12), -1.125, AL.mult, col("nb"), AL.add)
+    ts(col("wb"), col("w9"), OH(14), AL.subtract)
+    ts(V("WB", 0, 142), V("Wh", 1, 143), col("wa"), AL.mult)
+    ts(V("WC", 0, 142), V("Wh", 0, 142), col("wb"), AL.mult)
+    tt(V("WA", 0, 142), V("WB", 0, 142), V("WC", 0, 142), AL.add)
+    ts(M("M15"), M("Ih"), OH(15), AL.mult, 2048.0, AL.mult)
+    ts(M("D14"), M("I"), OH(14), AL.mult)
+    ts(col("c1"), col("s2"), -511.0, AL.mult, 2048.0, AL.add)
+    ts(col("oc"), s, 256.0, AL.mult, col("c1"), AL.add)
+    ts(V("wm", 0, 1), V("wti", 0, 1), W - 1, AL.bitwise_and)
+    ts(V("wc", 0, 1), V("wm", 0, 1), 0.125, AL.mult)
+    ts(M("Mw"), sel("Wh", 15), V("wc", 0, 1), AL.mult)
+    ts(col("d1"), MK(4), MK(8), AL.add, MK(12), AL.add)
+    ts(col("d2"), col("d1"), -4.0, AL.mult, 8.0, AL.add)
+    ts(M("Mpr"), M("E"), col("d2"), AL.is_equal)
+    ts(col("d3"), MK(8), -8.0, AL.mult)
+    ts(M("Mdi"), M("E"), col("d3"), AL.is_equal)
+    ts(V("owe", 0, 128), V("owni", 0, 128), 1.0, AL.add, col("lo8"), AL.mult)
+    ts(V("owo", 0, 128), V("owni", 0, 128), 1.0, AL.add, MK(8), AL.mult)
+    ts(col("o1"), MK(12), MK(8), AL.subtract, OH(12), AL.add)
+    ts(col("o2"), col("o1"), 2048.0, AL.mult)
+    mm(V("ps1", 128, 256), [(M("Mpr"), V("owe", 0, 128)), (M("Mdi"), V("owe", 0, 128)), (M("D14"), V("cix", 0, C, 2))])
+    mm(V("ps1", 256, 384), [(M("Mpr"), V("owo", 0, 128)), (M("Mdi"), V("owo", 0, 128)), (M("D14"), V("cix", 1, C, 2))])
+    ts(V("OwnT", 0, C, 2), V("ps1", 128, 256), col("o2"), AL.add)
+    ts(V("OwnT", 1, C, 2), V("ps1", 256, 384), col("o2"), AL.add)
+    cp(V("thb", 0, NV, 1, (0, 8)), V("thri", 0, NV, 1, (0, 8)))
+    mm(V("ps1", 0, NV), [(V("Eg", 0, 128, 1, (0, 8)), V("thb", 0, NV, 1, (0, 8)))])
+    ts(V("thc", 0, NV), V("ps1", 0, NV), -1.0, AL.mult, 0.5, AL.add)
+    cp(V("nm", 0, C), V("nami", 0, C))
+    ts(V("ta", 0, C), V("mrki", 0, C), -2.0, AL.mult, 1.0, AL.add)
+    ts(V("tb", 0, C), V("nami", 0, C), 1.0, AL.add)
+    tt(V("Z", 0, C), V("ta", 0, C), V("tb", 0, C), AL.mult)
+    ts(V("Tp", 0, C), V("picb", 0, C), 1.0 / 256, AL.mult)
+    ms(V("S", 0, C), 0.0)
+    ms(V("y", W, WIN), 0.0)
+    for b in range(4):
+        lo, hi, pb = 512 * b, 512 * b + 512, V("ps%d" % (4 + b), 0, 512)
+        ts(V("z0", lo, hi), V("x0", lo, hi), 0.0, AL.is_equal)
+        mm(pb, [(M("Is"), V("x0", lo, hi)), (M("nI"), V("z0", lo, hi))])
+        if b == 3:
+            cp(V("y", lo, hi), pb)
+        else:
+            act(V("y", lo, hi), pb, AF.Identity)
+
+    reg = regions()
+    c0s = [sum(CHUNKS[:i]) for i in range(NCH)]
+
+    def span(ci):
+        grp = [x for x in SGROUPS if ci in x][0]
+        return c0s[grp[0]], c0s[grp[-1]] + CHUNKS[grp[-1]]
+
+    def send(kind, v, ci, pairs):
+        sem = "r%s%d_%d" % (kind, v + 1, ci)
+        i = add("g", SENDC, [a for a, b in pairs], [], pairs, "send", sem)
+        add("n", 0, [], [b for a, b in pairs], None, "recv", sem, i)
+
+    def passes(ci, src, dst, opnd, op, bank, extra):
+        n, c0 = CHUNKS[ci], c0s[ci]
+        cnt, whole = V(bank, 0, n), V(bank, 0, 512)
+        ks = list(range(1, 16))
+        first = True
+        for i in range(0, 15, KB):
+            terms = []
+            for k in ks[i:i + KB]:
+                o = V(dst, 16 * c0 + k * n, 16 * c0 + (k + 1) * n)
+                tt(o, V(src, 16 * c0 + k, 16 * (c0 + n), 16), opnd, op)
+                terms.append((sel("Wd", k), o))
+            if i + KB >= 15:
+                terms = terms + extra
+            mm(cnt, terms, first, i + KB >= 15, whole)
+            first = False
+        return cnt
+
+    for v in range(NV):
+        last = v == NV - 1
+        for ci in range(NCH):
+            n, c0, R = CHUNKS[ci], c0s[ci], reg[ci]
+            t = lambda k: V(k, c0, c0 + n)
+            st = lambda k: V(k, v * C + c0, v * C + c0 + n)
+            tag[0] = (v, "g%d" % ci)
+            for a in range(c0, c0 + n, GSUB):
+                b = min(a + GSUB, c0 + n)
+                gather(V("G", 16 * a, 16 * b), V("nm", v * C + a, v * C + b), vec=a in (VG if v else VG0))
+            P = V("G", 16 * c0, 16 * (c0 + n), 16)
+            tag[0] = (v, "c%d" % ci)
+            act(R["Pp"], P, AF.Abs)
+            cnt = passes(ci, "G", "c1", R["Pp"], AL.is_gt, "ps0", [(M("Mpar"), st("S"))] if v else [])
+            tag[0] = (v, "h%d" % ci)
+            act(t("cl"), cnt, AF.Sign, V("thc", v, v + 1))
+            mm(R["R"], [(M("Mr"), t("cl"))])
+            act(t("isk"), R["R"], AF.Relu, col("isk"))
+            zt = V(R["ZT"][0], R["ZT"][1], R["ZT"][1] + n // 8)
+            mm(zt, [(M("I"), V("a128", 0, n // 8))] + [(sel2("WS", b), V("isk", c0 + b, c0 + n, 8)) for b in range(8)])
+            ok = V("offk", 16 * ci, 16 * ci + n // 8)
+            ts(ok, zt, col("s16"), AL.add)
+            gather(V("xk", 2 * c0, 2 * (c0 + n)), ok, V("G", 16 * c0, 16 * (c0 + n)))
+            xk = V("xk", 2 * c0, 2 * (c0 + n), 2)
+            if MKP:
+                mm(R["mk"], [(M("I"), t("isk"))])
+                tt(t("Zk"), st("Z"), R["mk"], AL.mult)
+            else:
+                tt(t("Zk"), st("Z"), t("isk"), AL.mult)
+            mm(R["Zsum"], [(M("ONh"), t("Zk"))])
+            act(t("nc"), R["Zsum"], AF.Sign, col("ncb"))
+            mm(R["Tab"], [(M("Ih"), t("OwnT")), (sel("Wh", 13), t("Zk"))])
+            tag[0] = (v, "o%d" % ci)
+            mm(R["ma"], [(M("GT"), t("isk"))])
+            mm(R["ms"], [(M("ON"), t("isk"))])
+            tt(t("Za"), st("Z"), R["ma"], AL.mult)
+            tt(t("Zs"), st("Z"), R["ms"], AL.mult)
+            mm(R["U"], [(M("I"), P), (M("nB2"), t("isk"))])
+            mm(R["nU"], [(M("nI"), P), (M("B2"), t("isk"))])
+            tt(t("t1"), st("Tp"), R["nU"], AL.min)
+            tt(st("Tpo"), t("t1"), R["U"], AL.max)
+            mm(R["Sp"], [(M("I"), st("S")), (M("Msg"), t("nc"))])
+            act(t("oct") if last else st("So"), R["Sp"], AF.Abs, col("nsg"))
+            if not last:
+                for grp in BGROUPS:
+                    if grp[-1] == ci:
+                        bv = lambda k, u: V(k, u * C + c0s[grp[0]], u * C + c0 + n)
+                        send("b", v, ci, [(bv("Tpo", v), bv("Tp", v + 1)), (bv("So", v), bv("S", v + 1))])
+            else:
+                ts(t("opc"), st("Tpo"), 256.0, AL.mult)
+            tag[0] = (v, "f%d" % ci)
+            mm(R["D"], [(M("nI"), P), (M("N2"), t("nc")), (M("I"), xk)])
+            act(R["Wp"], R["D"], AF.Sign, 2.0 - 1.0 / 512)
+            Fv, Bv = V("FB", 2 * c0, 2 * (c0 + n), 2), V("FB", 2 * c0 + 1, 2 * (c0 + n), 2)
+            tt(Fv, xk, R["Wp"], AL.min)
+            mm(R["Bp"], [(M("I"), xk), (M("nI"), V("one", 0, n)), (M("nI"), Fv)])
+            act(Bv, R["Bp"], AF.Identity)
+            tag[0] = (v, "m%d" % ci)
+            mm(R["u"], [(M("Mw"), st("Tpo")), (M("Msm"), t("isk")), (M("Mnc"), t("nc")), (M("Mx"), xk)])
+            ts(t("q"), R["u"], col("bq"), AL.add)
+            tt(t("A1"), t("q"), R["u"], AL.is_equal)
+            tt(t("pr"), t("A1"), R["Tab"], AL.mult)
+            tag[0] = (v, "l%d" % ci)
+            tt(t("J"), R["u"], t("q"), AL.subtract)
+            tag[0] = (v, "b%d" % ci)
+            for a in range(c0, c0 + n, ASUB):
+                b = min(a + ASUB, c0 + n)
+                act(V("Gp", 16 * a, 16 * b), V("G", 16 * a, 16 * b), AF.Abs)
+        for grp in SGROUPS:
+            tag[0] = (v, "s%d" % grp[-1])
+            g0, g1 = span(grp[0])
+            oT = reg[grp[-1]]["oT"]
+            oa = V(oT[0], oT[1], oT[1] + (g1 - g0) // 8)
+            mm(oa, [(M("I"), V("a8", g0 // 8, g1 // 8))] + [(sel2("WA", b), V("pr", g0 + b, g1, 8)) for b in range(8)])
+            off = V("offs", g0 // 8, g1 // 8)
+            ts(off, oa, col("oc"), AL.add)
+            win, fb = V("y", 0, WIN), V("FB", 2 * g0, 2 * g1)
+            add("v", 60 + SCAT * nel(fb), [off, fb], [win],
+                lambda g, T, win=win, off=off, fb=fb: g.vector.tensor_copy(ap(T, win).indirect(ap(T, off)), ap(T, fb)), ck="sc")
+        if last:
+            for b in range(4):
+                lo, hi = 512 * b, 512 * b + 512
+                if b % 2:
+                    ts(V("yo", lo, hi), V("y", lo, hi), 0.0, AL.max, 256.0, AL.mult)
+                else:
+                    act(V("yo", lo, hi), V("y", lo, hi), AF.Relu, 0.0, 256.0)
+            store(lambda T: T.ydep[:], V("yo", 0, W))
+            store(lambda T: T.ypic[:], V("opc", 0, C))
+            for gi in range(8):
+                store(lambda T, gi=gi: T.ycut[gi:gi + 1, :], V("oct", 0, C, 1, (16 * gi + 1, 16 * gi + 2)))
+        for ci in range(NCH):
+            n, c0, R = CHUNKS[ci], c0s[ci], reg[ci]
+            t = lambda k: V(k, c0, c0 + n)
+            st = lambda k: V(k, v * C + c0, v * C + c0 + n)
+            base = [(M("Sm"), st("Z")), (M("ISm"), t("Zs")), (M("SI"), t("Za")), (M("IR"), t("Zk"))]
+            tag[0] = (v, "l%d" % ci)
+            mm(R["L1"], base + [(M("Pm2"), t("pr"))])
+            tag[0] = (v, "e%d" % ci)
+            cnt = passes(ci, "Gp", "c2", R["Bp"], AL.is_lt, "ps1", [])
+            tag[0] = (v, "t%d" % ci)
+            act(t("e"), cnt, AF.Sign, -1.5)
+            mm(R["val"], [(M("LT"), t("isk")), (M("Mv"), t("e"))])
+            ts(t("X"), R["val"], col("x"), AL.is_ge)
+            tt(t("Q"), t("X"), R["L1"], AL.mult)
+            mm(R["new"], base + [(M("Pm"), t("pr")), (M("M15"), t("J")), (M("SI4"), t("Q"))])
+            act(t("aZ"), R["new"], AF.Abs)
+            if not last:
+                ts(st("nmo"), t("aZ"), -1.0, AL.add)
+                cp(st("Zo"), R["new"])
+                nx = lambda k: V(k, (v + 1) * C + c0, (v + 1) * C + c0 + n)
+                send("a", v, ci, [(st("nmo"), nx("nm")), (st("Zo"), nx("Z"))])
+            else:
+                ts(t("onm"), t("aZ"), -1.0, AL.add)
+                ts(t("omk"), R["new"], 0.0, AL.is_lt)
+                store(lambda T, c0=c0, n=n: T.ynam[:, c0:c0 + n], t("onm"))
+                store(lambda T, c0=c0, n=n: T.ymrk[:, c0:c0 + n], t("omk"))
+    return ops
+
+
+def plan():
+    ops = build()
+    n = len(ops)
+    deps = [set() for _ in range(n)]
+    hist = {}
+    for i, o in enumerate(ops):
+        if o["after"] is not None:
+            deps[i].add(o["after"])
+        for x, wr in [(x, False) for x in o["r"]] + [(x, True) for x in o["w"]]:
+            for (lo, hi, j, w2) in hist.get(x[0], []):
+                if j != i and (wr or w2) and lo < x[2] and x[1] < hi:
+                    deps[i].add(j)
+        for x in o["w"]:
+            hist[x[0]] = [h for h in hist.get(x[0], []) if not (x[1] <= h[0] and h[1] <= x[2] and x[3] == 1 and x[4] is None)]
+        for x, wr in [(x, False) for x in o["r"]] + [(x, True) for x in o["w"]]:
+            hist.setdefault(x[0], []).append((x[1], x[2], i, wr))
+    extra = [DMAL if o["kind"] == "dma" else COMM if o["kind"] == "send" else LAT for o in ops]
+    succ = [[] for _ in range(n)]
+    for i in range(n):
+        for j in deps[i]:
+            succ[j].append(i)
+    cost = [o["cost"] for o in ops]
+    eng = [o["e"] for o in ops]
+    banks = [sorted(set(x[0] for x in o["r"] + o["w"] if x[0] not in SB)) for o in ops]
+    pred = [sorted(d) for d in deps]
+
+    def place(key, back):
+        before = succ if back else pred
+        start = [0.0] * n
+        lines = {}
+        for i in sorted(range(n), key=lambda i: (key[i], -i if back else i)):
+            t0 = 0.0
+            for j in before[i]:
+                a, b = (i, j) if back else (j, i)
+                t0 = max(t0, start[j] + cost[j] + (0.0 if ops[b]["cont"] and eng[a] == "p" else extra[a]))
+            if back and not before[i]:
+                t0 = extra[i]
+            e, c = eng[i], cost[i]
+            if e != "n":
+                res = [(lines.setdefault(e, ([], [])), 0.0)] + [(lines.setdefault(b, ([], [])), LAT) for b in banks[i]]
+                moved = True
+                while moved:
+                    moved = False
+                    for (ss, jj), gap in res:
+                        x = max(0, find(ss, t0) - (1 if gap == 0.0 else 4))
+                        while x < len(ss) and ss[x] < t0 + c + gap:
+                            j = jj[x]
+                            if (gap == 0.0 or eng[j] != e) and ss[x] + cost[j] + gap > t0:
+                                t0 = ss[x] + cost[j] + gap
+                                moved = True
+                            x += 1
+                for (ss, jj), gap in res:
+                    x = find(ss, t0)
+                    ss.insert(x, t0)
+                    jj.insert(x, i)
+            start[i] = t0
+        end = max(start[i] + cost[i] + (0.0 if back else extra[i]) for i in range(n))
+        return start, end
+
+    def find(ss, t0):
+        lo, hi = 0, len(ss)
+        while lo < hi:
+            m = (lo + hi) // 2
+            if ss[m] <= t0:
+                lo = m + 1
+            else:
+                hi = m
+        return lo
+
+    def finish(start):
+        order = sorted(range(n), key=lambda i: (start[i], i))
+        dp = [set(d) for d in deps]
+        lastuse = {}
+        for i in order:
+            for b in banks[i]:
+                for e2, j in lastuse.get(b, {}).items():
+                    if e2 != eng[i]:
+                        dp[i].add(j)
+                lastuse.setdefault(b, {})[eng[i]] = i
+        return order, dp
+
+    def replay(order, dp, m):
+        fin = [0.0] * n
+        free = {}
+        for i in order:
+            o = ops[i]
+            t0 = max([free.get(eng[i], 0.0)] + [fin[j] for j in dp[i] if not (o["cont"] and eng[j] == "p")])
+            t1 = t0 + cost[i] * m.get(o["ck"], 1.0)
+            if eng[i] != "n":
+                free[eng[i]] = t1
+            fin[i] = t1 + extra[i] * m.get("x" + o["kind"], 1.0)
+        return max(fin)
+
+    rng = np.random.default_rng(SEED)
+    tail = [0.0] * n
+    for i in range(n - 1, -1, -1):
+        tail[i] = cost[i] + extra[i] + max([tail[j] for j in succ[i]] + [0.0])
+    top = max(tail)
+    rel, run = [], {}
+    for i in range(n):
+        tg = ops[i]["tag"]
+        rel.append(run.get(tg, 0.0))
+        run[tg] = rel[i] + 0.6 * cost[i]
+
+    def keys(off):
+        key = [0.0] * n
+        for i in range(n - 1, -1, -1):
+            tg = ops[i]["tag"]
+            if tg is None:
+                key[i] = min([key[j] - cost[i] - extra[i] for j in succ[i]] + [1e9])
+            else:
+                key[i] = tg[0] * off["T"] + off[tg[1]] + rel[i] + off.get(tg[1] + ("a" if tg[0] == 0 else "z" if tg[0] == NV - 1 else "m"), 0)
+        for i in range(n):
+            key[i] = max([key[i]] + [key[j] + 1e-3 for j in pred[i]])
+        return key
+    if SEARCH:
+        DB[:] = [[cost[i] + extra[i] for i in range(n)], cost, sorted(set(o["tag"][1] + x for o in ops if o["tag"] for x in "az"))]
+        return SEARCH[0](keys, place, finish, replay)
+    best = None
+    key = keys(OFFS)
+    for it in range(ROUNDS):
+        start, end = place(key, False)
+        order, dp = finish(start)
+        score = [replay(order, dp, m) for m in MODELS]
+        if best is None or sum(score) < best[0]:
+            best = (sum(score), start, order, dp, score)
+        src = best[1] if it % 4 == 3 else start
+        rs, end = place([-(src[i] + cost[i] + extra[i]) for i in range(n)], True)
+        key = [-(rs[i] + cost[i]) for i in range(n)]
+        noise = NOISE * rng.random(n)
+        for i in range(n):
+            key[i] = max([key[i] + float(noise[i])] + [key[j] + 1e-3 for j in pred[i]])
+    start, order, deps = best[1], best[2], best[3]
+    done = [start[i] + cost[i] + extra[i] for i in range(n)]
+    count = {}
+    token = [None] * n
+    clock = [None] * n
+    know = {e: {} for e in "vapgs"}
+    steps = []
+    for i in order:
+        o = ops[i]
+        e = o["e"]
+        if o["kind"] == "recv":
+            token[i], clock[i] = (o["sem"], 1), {o["sem"]: 1}
+            continue
+        waits = {}
+        k = know[e]
+        for j in sorted(deps[i], key=lambda j: -done[j]):
+            s, c = token[j]
+            if o["cont"] and ops[j]["e"] == "p":
+                continue
+            if k.get(s, 0) < c:
+                waits[s] = max(waits.get(s, 0), c)
+                for s2, c2 in clock[j].items():
+                    if k.get(s2, 0) < c2:
+                        k[s2] = c2
+        s = o["sem"] if o["kind"] == "dma" else "sent" if o["kind"] == "send" else "q" + e
+        count[s] = count.get(s, 0) + 1
+        token[i] = (s, count[s])
+        clock[i] = dict(k)
+        clock[i][s] = count[s]
+        steps.append((i, sorted(waits.items())))
+    return {"ops": ops, "steps": steps, "count": count, "span": max(done), "done": done, "order": order, "score": best[4]}
+
+
+PLAN = {}
+
+
+def rank_program(g, core, T, topo):
+    rank = T.rank_of(core)
+    if rank is None:
+        return
+    if "p" not in PLAN:
+        PLAN["p"] = plan()
+    p = PLAN["p"]
+    nr = len(T.cores)
+    nxt, prv = T.cores[(rank + 1) % nr], T.cores[(rank - 1) % nr]
+
+    def masks(a, b):
+        eng = topo.engines(a, b)
+        eng = eng[::max(1, len(eng) // 8)]
+        h = len(eng) // 2
+        return [sum(1 << x for x in eng[:h]), sum(1 << x for x in eng[h:2 * h])], 2 * h
+    mk, nout = masks(core, nxt)
+    nin = masks(prv, core)[1]
+    rid, pid = topo.addr(nxt, core)
+    queue = {"v": g.vector, "a": g.scalar, "p": g.tensor, "g": g, "s": g.sync}
+
+    def unit(s):
+        return 1 if s[0] == "q" else nin if s[0] == "r" else nout if s == "sent" else 16
+    for i, waits in p["steps"]:
+        o = p["ops"][i]
+        q = queue[o["e"]]
+        for s, c in waits:
+            q.wait_ge(T.sem[s], c * unit(s))
+        if o["kind"] == "send":
+            g.remote_dma_fused([RemoteDMATransfer(dst_ids=[DstId(rid=rid, pnc=pid)], dma_engine_mask=mk[j], remote_sem=T.sem[o["sem"]],
+                                                  src=ap(T, a), dst=ap(T, b)) for j, (a, b) in enumerate(o["fn"])],
+                               local_sem=T.sem["sent"])
+        elif o["kind"] == "dma":
+            o["fn"](g, T).then_inc(T.sem[o["sem"]], 16)
+        else:
+            o["fn"](g, T).then_inc(T.sem["q" + o["e"]], 1)
+    for s, c in sorted(p["count"].items()):
+        if not s.startswith("ld_"):
+            g.wait_ge(T.sem[s], c * unit(s))

@@ -4,25 +4,65 @@ from concourse.mybir import AluOpType, ActivationFunctionType
 
 W, C, NV = 2048, 256, 6
 CHUNKS = [64, 64, 64, 64]
-SGROUPS = [[0, 1, 2], [3]]
+SGROUPS = [[0, 1, 2, 3]]
 ASUB = 16
 BGROUPS = [[0, 1, 2, 3]]
 SEED, NOISE, ROUNDS = 0, 60.0, 12
 SEARCH, DB = [], []
-OFFS = {'T': 16093, 'g0': 480, 'c0': -589, 'h0': 423, 'o0': 2826, 'f0': 6082, 'm0': -1422, 'b0': 6545, 'l0': 9588, 'e0': 3410,
-        't0': 11120, 's0': 9900, 'g1': -1383, 'c1': 1383, 'h1': 4034, 'o1': 6007, 'f1': 6781, 'm1': 3148, 'b1': 6655, 'l1': 6783,
-        'e1': 6407, 't1': 12453, 's1': 15980, 'g2': 2416, 'c2': 6176, 'h2': 8526, 'o2': 585, 'f2': 6920, 'm2': 6205, 'b2': 13554,
-        'l2': 1749, 'e2': 11308, 't2': 13370, 's2': 8916, 'g3': 5505, 'c3': 5737, 'h3': 6239, 'o3': 8427, 'f3': 8646, 'm3': 7045,
-        'b3': 10709, 'l3': 19177, 'e3': 13382, 't3': 17145, 's3': 11632}
-MODELS = [{}, {"ga": 0.7, "sc": 0.5, "xsend": 1.2}, {"ga": 1.3, "sc": 1.5, "xsend": 0.7}, {"p": 1.5, "xc": 1.5},
-          {"ga": 1.3, "sc": 0.6, "xc": 0.6}, {"ga": 0.75, "sc": 1.4, "xc": 2.0, "send": 1.5}]
+OFFS = {'T': 17874, 'g0': 648, 'c0': 412, 'h0': -533, 'o0': 3347, 'f0': 4937, 'm0': -1076, 'b0': 6503, 'l0': 9126, 'e0': 1097,
+        't0': 10429, 's0': 16550, 'g1': -1103, 'c1': -1759, 'h1': 3848, 'o1': 6245, 'f1': 7762, 'm1': 3316, 'b1': 5204, 'l1': 7857,
+        'e1': 5315, 't1': 12711, 's1': 14996, 'g2': 1904, 'c2': 6101, 'h2': 8577, 'o2': -888, 'f2': 4061, 'm2': 6449, 'b2': 12828,
+        'l2': 121, 'e2': 10801, 't2': 13284, 's2': 7049, 'g3': 5232, 'c3': 4432, 'h3': 4939, 'o3': 8168, 'f3': 8646, 'm3': 8814,
+        'b3': 14869, 'l3': 18755, 'e3': 16067, 't3': 20886, 's3': 12001, 'e0a': -1321, 'c1a': -1104, 't2a': 3201, 'l0z': 2561,
+        'b1a': -1806, 'e0z': -1253, 'e2a': 4389, 't0z': 652, 's3z': -331, 'm0z': 3344, 'o1z': 364, 'b3a': -3636, 'c2a': 1042,
+        'b0a': -1799, 'f2z': 1887, 'g1a': 362, 't1a': -1354, 'm2z': 159, 'h2a': 633, 'o0a': -521, 'l1z': 185, 'g1z': -2257,
+        'c1z': -547, 'b3z': -2654, 'o2z': -3090, 'g3z': -222, 'f1a': -882, 'c3a': 1546, 't0a': 239, 'm2a': 1668, 'g2a': 238,
+        'f0a': 2291, 'm1z': 2114, 'e3a': 1447, 'g2z': 1057, 'e1a': 589, 's3a': -1271, 'h3z': -3444, 't1z': 5509, 'l3a': -342,
+        't3a': 121, 'l3z': -855, 'm3a': -311, 'b2z': 1273, 't3z': 2215, 'h3a': 209, 'o2a': -2212, 'g0z': -1586, 'e3z': -287,
+        'g0a': 566, 'b2a': -2410, 't2z': 373, 'b1z': -1705, 'o3z': -892, 'h1a': 574, 'l2z': 373, 'c3z': 228, 'o0z': 299,
+        'c0a': -3977, 'g3a': -1733, 'l1a': -117, 'm0a': -248, 'o1a': 2473, 'e1z': 1063, 'h0z': 226, 'f2a': -129, 'l2a': 1877,
+        'f1z': -243, 'h0a': 638, 'o3a': -302, 'e2z': 167}
+CHUNKS, SGROUPS, BGROUPS, ROUNDS = [128, 128], [[0, 1]], [[0, 1]], 2
+ASUB = 32
+OFFS = {'T': 13610, 'g0': -4370, 'c0': 4450, 'h0': 6380, 'o0': -860, 'f0': -180, 'm0': 7360, 'b0': 16400, 'l0': -3160, 'e0': 9000,
+        't0': 7840, 's0': 14120, 'g1': 4490, 'c1': 6360, 'h1': -490, 'o1': 8050, 'f1': -1930, 'm1': -2110, 'b1': 7550, 'l1': 5580,
+        'e1': 17250, 't1': 11790, 's1': 12330, 't0a': 4850, 'b0z': 9480, 'o1a': 240, 'h1a': -4840, 'm1a': 1400, 'b1z': 7670,
+        'e0a': -9540, 'l0a': -2760, 'm1z': 220, 'e1a': 1050, 't1a': 2160, 's1z': 1540, 'f0z': -4360, 't1z': 5960, 'e1z': -1060,
+        's1a': 5650, 'o0a': -2470, 'l1z': 1050, 'f0a': 4400, 'l0z': 5580, 'g1z': -8710, 'g0a': -8180, 't0z': -6830, 'o0z': 3320,
+        'f1a': 10010, 'g0z': 9710, 'h0a': -3700, 'g1a': -1410, 'h1z': 6780, 'm0z': -6270, 'f1z': -5160, 'l1a': -7300,
+        'b1a': -2830, 'c0a': -2900, 'e0z': 880, 'b0a': -3230, 'm0a': 1460, 'c1z': -80}
+_L, _C = 0.5, 3000.0 / 5500
+MODELS = [{"xc": _L, "xsend": _C}, {"ga": 0.7, "sc": 0.5, "xc": _L, "xsend": _C * 1.4}, {"ga": 1.33, "sc": 1.5, "xc": _L, "xsend": _C * .7},
+          {"xc": 1.8 * _L, "xsend": 2 * _C}, {"ga": 1.33, "sc": 0.6, "xc": _L, "xsend": 1.5 * _C},
+          {"ga": 0.75, "sc": 1.4, "xc": 1.5 * _L, "xsend": _C, "send": 1.5}]
 GSUB = 32
-KB = 5
-MKP = True
-VG, VG0 = [96, 160], [160]
+KB = 3
+MKP, UV, DUP, BV, LV, ONE = True, 0, 2, False, False, False
+PAIR, NACT = [1, 1], 40
+FV, FA = 48.0, 48.0
+VG, VG0 = [32, 96, 160], [32]
 WIN = W + 512
-GATH, SCAT, PEC, LAT, DMAL, COMM = 1.56, 3.8, 0.5, 90.0, 2400.0, 2500.0
-SENDC = 700.0
+GATH, SCAT, PEC, LAT, DMAL, COMM = 1.56, 3.8, 0.5, 200.0, 2400.0, 5500.0
+SENDC = 1000.0
+CHUNKS, SGROUPS, BGROUPS, ASUB, PAIR, NACT = [64] * 4, [[0, 1, 2], [3]], [[0, 1, 2, 3]], 16, [0, 0], 20
+FV, FA, VG, VG0, LAT, COMM = 0.0, 0.0, [96, 160], [160], 310.0, 3000.0
+_L = 250.0 / 310
+MODELS = [{"xc": _L}, {"ga": 0.7, "sc": 0.5, "xc": _L, "xsend": 1.4}, {"ga": 1.33, "sc": 1.5, "xc": _L, "xsend": .8},
+          {"xc": 1.6 * _L, "xsend": 1.6}, {"ga": 1.33, "sc": 0.6, "xc": .75 * _L, "xsend": 1.2},
+          {"ga": 0.75, "sc": 1.4, "xc": 1.3 * _L, "send": 1.5}]
+OFFS = {'T': 15630, 'g0': 560, 'c0': -810, 'h0': 480, 'o0': 4730, 'f0': 6080, 'm0': -3540, 'b0': 7160, 'l0': 8180, 'e0': 7500,
+        't0': 11120, 's0': 10070, 'g1': 1020, 'c1': 1510, 'h1': 4930, 'o1': 6010, 'f1': 6570, 'm1': 5360, 'b1': 6770, 'l1': 6950,
+        'e1': 3050, 't1': 11910, 's1': 16240, 'g2': 2630, 'c2': 6440, 'h2': 11060, 'o2': -1740, 'f2': 8500, 'm2': 8910,
+        'b2': 13550, 'l2': 2820, 'e2': 11860, 't2': 13170, 's2': 7040, 'g3': 3380, 'c3': 5760, 'h3': 6580, 'o3': 7460, 'f3': 9530,
+        'm3': 5290, 'b3': 11490, 'l3': 20880, 'e3': 13310, 't3': 16780, 's3': 12210, 't0z': 2240, 'b1a': -320, 'c2a': 350,
+        'm2a': -580, 'e0z': -1100, 'l0z': 1960, 'e2a': 3230, 't2z': 2330, 't0a': 460, 'f2a': 2360, 'l1a': 4520, 'c1a': 5760,
+        'h1a': 2180, 'o1z': -70, 'l3a': -2280, 'b0z': 2480, 'e1z': -2090, 'l3z': 510, 'c0a': 2900, 'm1a': 770, 'h0a': 490,
+        'f0a': 400, 'c0z': -1060, 'm3a': -1210, 't1z': -810, 'c3z': 1530, 'e2z': 200, 'f1a': -6200, 'b2z': -90, 'f3a': -1130,
+        'o2z': -700, 'h3a': 6230, 'e3z': -620, 't2a': -420, 'g2a': -120, 'c2z': 1320, 'g2z': -5230, 'l0a': -690, 'e1a': -520,
+        't3z': 2610, 's3a': 1730, 'b3z': -230, 'f0z': 2290, 'g3a': -770, 'h2z': -1410, 'b0a': 470, 'o1a': 650, 'h2a': 3630,
+        'b3a': 3280, 'o2a': -620, 'o3z': -7330, 'c3a': -4120, 'l1z': 2820, 'm0z': 970, 'c1z': -650, 't1a': -710, 'o0z': 140,
+        'm1z': -2430, 's3z': 1510, 'h3z': 140, 'm0a': -160, 'f2z': 1180, 'o3a': -390, 'l2z': -500, 'f1z': 80, 'g1a': 1150,
+        'h1z': 1040}
 
 BF, HF, F4, I4, U2 = "bfloat16", "float16", "float32", "int32", "uint16"
 SB = {
@@ -31,7 +71,7 @@ SB = {
     "G": (16 * C, BF), "Gp": (16 * C, BF), "c1": (16 * C, BF), "c2": (16 * C, BF),
     "nm": (NV * C, U2), "Z": (NV * C, HF), "Tp": (NV * C, HF), "S": (NV * C, BF),
     "nmo": (NV * C, U2), "Zo": (NV * C, HF), "Tpo": (NV * C, HF), "So": (NV * C, BF),
-    "cl": (C, BF), "isk": (C, BF), "Zk": (C, HF), "Za": (C, HF), "Zs": (C, HF), "nc": (C, BF), "xk": (2 * C, BF),
+    "cl": (C, BF), "isk": (C, BF), "Zk": (C, HF), "Za": (C, HF), "Zs": (C, HF), "nc": (C, BF), "xk": (4 * C, BF), "L1s": (C, F4), "nz": (NV * C, F4), "Zf": (NV * C, F4), "W4": (144, BF),
     "FB": (2 * C, BF), "t1": (C, HF), "q": (C, I4), "J": (C, HF), "A1": (C, HF), "pr": (C, HF), "e": (C, BF),
     "X": (C, BF), "Q": (C, F4), "aZ": (C, F4), "a128": (16, BF), "WS": (144, BF), "offk": (128, U2), "a8": (32, BF),
     "offs": (32, U2), "cix": (C, BF), "W2": (144, BF), "WC": (144, HF), "OwnT": (C, HF), "owe": (C // 2, HF), "owo": (C // 2, HF),
@@ -44,7 +84,7 @@ SB = {
 }
 for _m in ("I", "nI", "N2", "D14", "Is", "ON", "GT", "LT", "Mr", "Mv", "Mpar", "B2", "nB2", "Mx", "Mnc", "Msm", "Msg"):
     SB[_m] = (128, BF)
-for _m in ("Ih", "ONh", "Sm", "ISm", "SI", "IR", "Pm", "Pm2", "M15", "Mw", "Mpr", "Mdi", "h1", "h2"):
+for _m in ("Ih", "ONh", "Sm", "ISm", "SI", "IR", "Pm", "Pm2", "NBm", "M15", "Mw", "Mpr", "Mdi", "h1", "h2"):
     SB[_m] = (128, HF)
 SB["SI4"] = (128, F4)
 SCRATCH = {k: ("sbuf", [128, n], d) for k, (n, d) in SB.items()}
@@ -53,7 +93,7 @@ for _b in range(8):
 NCH = len(CHUNKS)
 LOADS = ["nam", "dep0", "dep1", "mrk", "thr", "pic", "own", "wt"]
 SEMAPHORES = (["qv", "qa", "qp", "qg", "sent", "stored"] + ["ld_" + k for k in LOADS]
-              + ["r%s%d_%d" % (k, v, c) for k in "ab" for v in range(1, NV) for c in range(NCH)])
+              + ["r%s%d_%d" % (k, v, c) for k in "abz" for v in range(1, NV) for c in range(NCH)])
 AL, AF = AluOpType, ActivationFunctionType
 
 
@@ -86,8 +126,13 @@ def regions():
             b = [2 + 3 * ci, 3 + 3 * ci, 4 + 3 * ci]
             t = {"Pp": (0, 0), "Bp": (0, 1), "Sp": (0, 2), "oT": (0, 3), "R": (1, 0), "D": (1, 0), "val": (1, 0), "mk": (1, 1),
                  "Wp": (1, 1), "ma": (1, 2), "Tab": (2, 1), "ms": (1, 3), "u": (1, 3), "Zsum": (2, 0), "L1": (2, 0),
-                 "ZT": (2, 1), "U": (2, 2), "new": (2, 2), "nU": (2, 3)}
+                 "ZT": (2, 1), "U": (2, 2), "new": (2, 2), "nU": (2, 3), "nW": (1, 2)}
+            t.update({"Sp": (1, 2), "Bp": (2, 3), "oT": (1, 1)})
             out.append({k: V("ps%d" % b[i], 128 * s, 128 * s + n) for k, (i, s) in t.items()})
+            out[-1].update({"P2": V("ps%d" % b[0], 0, 2 * n, 2 - PAIR[0]), "B2": V("ps%d" % b[0], 256, 256 + 2 * n, 2 - PAIR[1])})
+            if not PAIR[1]:
+                out[-1]["B2"] = V("ps%d" % b[0], 256, 256 + n, 2)
+                out[-1]["Bp"] = V("ps%d" % b[0], 256, 256 + n)
         elif NCH == 3:
             ob, mb = 2 + 2 * ci, 3 + 2 * ci
             t = {"Pp": (ob, 0), "Bp": (ob, 1), "Sp": (ob, 2), "oT": (ob, 4), "R": (mb, 0), "D": (mb, 0), "val": (mb, 0),
@@ -98,17 +143,19 @@ def regions():
             ob, mb, h = 2 + ci % 2, 4 + ci, 4 * (ci // 2)
             t = {"Pp": (ob, h), "Bp": (ob, h + 1), "Sp": (ob, h + 2), "oT": (ob, h + 3), "R": (mb, 0), "D": (mb, 0), "val": (mb, 0),
                  "mk": (mb, 1), "Wp": (mb, 1), "ma": (mb, 2), "Tab": (mb, 5), "ms": (mb, 3), "u": (mb, 3), "Zsum": (mb, 4),
-                 "L1": (mb, 4), "ZT": (mb, 5), "U": (mb, 6), "new": (mb, 6), "nU": (mb, 7)}
+                 "L1": (mb, 4), "ZT": (mb, 5), "U": (mb, 6), "new": (mb, 6), "nU": (mb, 7), "nW": (mb, 2)}
             out.append({k: V("ps%d" % b, 64 * s, 64 * s + n) for k, (b, s) in t.items()})
+            out[-1].update({"P2": out[-1]["Pp"], "B2": out[-1]["Bp"]})
     return out
 
 
 def build():
     ops = []
     tag = [None]
+    moved = []
 
     def add(eng, cost, reads, writes, fn, kind="c", sem=None, after=None, ck=None):
-        ops.append({"e": eng, "cost": cost, "r": [r for r in reads if isv(r)], "w": writes, "fn": fn, "kind": kind, "sem": sem,
+        ops.append({"e": eng, "cost": cost + (FV if eng == "v" else FA if eng == "a" else 0.0), "r": [r for r in reads if isv(r)], "w": writes, "fn": fn, "kind": kind, "sem": sem,
                     "after": after, "ck": ck or (kind if kind != "c" else eng), "tag": tag[0], "cont": False})
         return len(ops) - 1
 
@@ -116,6 +163,10 @@ def build():
         return ap(T, x) if isv(x) else x
 
     def ts(out, in0, s1, op0, s2=None, op1=None):
+        if (tag[0] is None and len(moved) < NACT and op0 == AL.mult and (op1 is None or op1 == AL.add)
+                and SB[out[0]][1] in (BF, F4) and in0[0] in SB and SB[in0[0]][1] in (BF, F4)):
+            moved.append(out)
+            return act(out, in0, AF.Identity, 0.0 if s2 is None else s2, s1)
         n = nel(in0) * (0.5 if two(out, in0) else 1.0)
         if op1 is None:
             f = lambda g, T: g.vector.tensor_scalar(ap(T, out), ap(T, in0), a_(T, s1), None, op0)
@@ -135,8 +186,8 @@ def build():
         add("v", max(64, nel(out) * (0.5 if two(out) else 1.0)), [], [out], lambda g, T: g.vector.memset(ap(T, out), c))
 
     def act(out, in0, func, bias=0.0, scale=1.0):
-        add("a", max(80, nel(in0)), [in0, bias], [out],
-            lambda g, T: g.scalar.activation(ap(T, out), ap(T, in0), func, bias=a_(T, bias), scale=scale))
+        add("a", max(80, nel(in0)), [in0, bias, scale], [out],
+            lambda g, T: g.scalar.activation(ap(T, out), ap(T, in0), func, bias=a_(T, bias), scale=a_(T, scale)))
 
     def gather(out, off, win=V("y", 0, W), vec=False):
         if vec:
@@ -219,12 +270,16 @@ def build():
     ts(col("ns"), s, -1.0, AL.mult)
     ts(V("Wd", 0, 144), V("u0", 0, 144), col("ns"), AL.is_equal)
     ts(V("Wh", 0, 144), V("u0", 0, 144), col("ns"), AL.is_equal)
-    tt(V("W2", 0, 142), V("Wd", 0, 142), V("Wd", 1, 143), AL.add)
-    ts(V("WS", 0, 142), V("W2", 0, 142), s, AL.mult)
+    NB = 16 // DUP
+    tt(V("W2", 0, 143), V("Wd", 0, 143), V("Wd", 1, 144), AL.add)
+    if DUP == 4:
+        tt(V("W4", 0, 141), V("W2", 0, 141), V("W2", 2, 143), AL.add)
+    ts(V("WS", 0, 145 - DUP), V("W4" if DUP == 4 else "W2", 0, 145 - DUP), s, AL.mult)
     ts(V("si", 1, 2), V("si", 0, 1), 1, AL.arith_shift_right)
     cp(col("s2"), V("si", 1, 2))
-    ts(col("s16"), col("s2"), 16.0, AL.mult)
-    ts(V("a128", 0, 16), V("jj", 0, 16), 128.0, AL.mult)
+    ts(V("si", 2, 3), V("si", 0, 1), DUP // 2, AL.arith_shift_right)
+    ts(col("s16"), V("si", 2, 3), 16.0, AL.mult)
+    ts(V("a128", 0, 16), V("jj", 0, 16), 16.0 * NB, AL.mult)
     ts(V("MK", 0, 16), V("jj", 0, 16), s, AL.is_le)
     ts(V("OH", 0, 16), V("jj", 0, 16), s, AL.is_equal)
     ts(M("ON"), M("E"), 100.0, AL.is_lt)
@@ -262,7 +317,8 @@ def build():
     tt(M("Mnc"), M("m1"), M("m2"), AL.add)
     ts(col("lo8"), MK(8), -1.0, AL.mult, 1.0, AL.add)
     ts(M("Sm"), M("E"), -1.0, AL.is_equal)
-    tt(M("ISm"), M("Ih"), M("Sm"), AL.subtract)
+    tt(M("h2"), M("Ih"), M("Sm"), AL.subtract)
+    ts(M("ISm"), M("h2"), 0.5, AL.mult)
     ts(M("h1"), M("E"), 1.0, AL.is_equal)
     tt(M("SI"), M("h1"), M("Ih"), AL.subtract)
     cp(M("SI4"), M("SI"))
@@ -273,8 +329,8 @@ def build():
     ts(col("n1"), MK(8), 2.0, AL.mult, -1.0, AL.add)
     ts(col("lo13"), MK(13), -1.0, AL.mult, 1.0, AL.add)
     ts(col("nb"), col("n1"), col("lo13"), AL.mult)
-    ts(M("h1"), M("ONh"), col("nb"), AL.mult)
-    tt(M("Pm2"), M("Pm"), M("h1"), AL.subtract)
+    ts(M("NBm"), M("ONh"), col("nb"), AL.mult)
+    tt(M("Pm2"), M("Pm"), M("NBm"), AL.subtract)
     ts(col("wa"), col("lo8"), OH(12), AL.subtract, OH(14), AL.subtract)
     ts(col("w9"), OH(12), -1.125, AL.mult, col("nb"), AL.add)
     ts(col("wb"), col("w9"), OH(14), AL.subtract)
@@ -335,19 +391,43 @@ def build():
     def passes(ci, src, dst, opnd, op, bank, extra):
         n, c0 = CHUNKS[ci], c0s[ci]
         cnt, whole = V(bank, 0, n), V(bank, 0, 512)
-        ks = list(range(1, 16))
-        first = True
-        for i in range(0, 15, KB):
-            terms = []
-            for k in ks[i:i + KB]:
+        if nel(opnd) < n or NCH > 2:
+            return passes1(ci, src, dst, V(opnd[0], opnd[1], opnd[2]), op, cnt, whole, extra)
+        ks = list(range(1, 9))
+        for i, w in ((0, 3), (3, 2), (5, 2), (7, 1)):
+            terms = list(extra) if i == 3 else []
+            for k in ks[i:i + w]:
+                lo = 16 * c0 + 2 * (k - 1) * n
+                if k < 8 and opnd[3] == 2:
+                    for j in range(2):
+                        o = V(dst, lo + j * n, lo + (j + 1) * n)
+                        tt(o, V(src, 16 * c0 + k + 8 * j, 16 * (c0 + n), 16), opnd, op)
+                        terms.append((sel("Wd", k + 8 * j), o))
+                elif k < 8:
+                    tt(V(dst, lo, lo + 2 * n), V(src, 16 * c0 + k, 16 * (c0 + n), 8), opnd, op)
+                    terms += [(sel("Wd", k), V(dst, lo, lo + 2 * n, 2)), (sel("Wd", k + 8), V(dst, lo + 1, lo + 2 * n, 2))]
+                else:
+                    tt(V(dst, lo, lo + n), V(src, 16 * c0 + k, 16 * (c0 + n), 16), V(opnd[0], opnd[1], opnd[2], 2), op)
+                    terms.append((sel("Wd", k), V(dst, lo, lo + n)))
+            mm(cnt, terms, i == 0, i == 7, whole)
+        return cnt
+
+    def passes1(ci, src, dst, opnd, op, cnt, whole, extra):
+        n, c0 = CHUNKS[ci], c0s[ci]
+        for i, w in ((1, 7), (8, 6), (14, 2)):
+            terms = list(extra) if i == 8 else []
+            for k in range(i, i + w):
                 o = V(dst, 16 * c0 + k * n, 16 * c0 + (k + 1) * n)
                 tt(o, V(src, 16 * c0 + k, 16 * (c0 + n), 16), opnd, op)
                 terms.append((sel("Wd", k), o))
-            if i + KB >= 15:
-                terms = terms + extra
-            mm(cnt, terms, first, i + KB >= 15, whole)
-            first = False
+            mm(cnt, terms, i == 1, i == 14, whole)
         return cnt
+
+    def twice(out, src, func):
+        if NCH > 2:
+            return act(out, src, func)
+        for j in range(2 if out[3] == 1 else 1):
+            act(V(out[0], out[1] + j, out[2], 2), src, func)
 
     for v in range(NV):
         last = v == NV - 1
@@ -361,18 +441,19 @@ def build():
                 gather(V("G", 16 * a, 16 * b), V("nm", v * C + a, v * C + b), vec=a in (VG if v else VG0))
             P = V("G", 16 * c0, 16 * (c0 + n), 16)
             tag[0] = (v, "c%d" % ci)
-            act(R["Pp"], P, AF.Abs)
-            cnt = passes(ci, "G", "c1", R["Pp"], AL.is_gt, "ps0", [(M("Mpar"), st("S"))] if v else [])
+            twice(R["P2"], P, AF.Abs)
+            cnt = passes(ci, "G", "c1", R["P2"], AL.is_gt, "ps0", [(M("Mpar"), st("S"))] if v else [])
             tag[0] = (v, "h%d" % ci)
             act(t("cl"), cnt, AF.Sign, V("thc", v, v + 1))
             mm(R["R"], [(M("Mr"), t("cl"))])
             act(t("isk"), R["R"], AF.Relu, col("isk"))
-            zt = V(R["ZT"][0], R["ZT"][1], R["ZT"][1] + n // 8)
-            mm(zt, [(M("I"), V("a128", 0, n // 8))] + [(sel2("WS", b), V("isk", c0 + b, c0 + n, 8)) for b in range(8)])
-            ok = V("offk", 16 * ci, 16 * ci + n // 8)
+            zt = V(R["ZT"][0], R["ZT"][1], R["ZT"][1] + n // NB)
+            mm(zt, [(M("I"), V("a128", 0, n // NB))]
+               + [(V("WS", 16 - DUP * (b + 1), 144 - DUP * (b + 1)), V("isk", c0 + b, c0 + n, NB)) for b in range(NB)])
+            ok = V("offk", 32 * ci, 32 * ci + n // NB)
             ts(ok, zt, col("s16"), AL.add)
-            gather(V("xk", 2 * c0, 2 * (c0 + n)), ok, V("G", 16 * c0, 16 * (c0 + n)))
-            xk = V("xk", 2 * c0, 2 * (c0 + n), 2)
+            gather(V("xk", DUP * c0, DUP * (c0 + n)), ok, V("G", 16 * c0, 16 * (c0 + n)))
+            xk = V("xk", DUP * c0, DUP * (c0 + n), DUP)
             if MKP:
                 mm(R["mk"], [(M("I"), t("isk"))])
                 tt(t("Zk"), st("Z"), R["mk"], AL.mult)
@@ -383,11 +464,17 @@ def build():
             mm(R["Tab"], [(M("Ih"), t("OwnT")), (sel("Wh", 13), t("Zk"))])
             tag[0] = (v, "o%d" % ci)
             mm(R["ma"], [(M("GT"), t("isk"))])
-            mm(R["ms"], [(M("ON"), t("isk"))])
+            mm(R["ms"], [(M("B2"), t("isk"))])
             tt(t("Za"), st("Z"), R["ma"], AL.mult)
             tt(t("Zs"), st("Z"), R["ms"], AL.mult)
-            mm(R["U"], [(M("I"), P), (M("nB2"), t("isk"))])
-            mm(R["nU"], [(M("nI"), P), (M("B2"), t("isk"))])
+            if UV >= 1:
+                tt(R["nU"], R["ms"], P, AL.subtract)
+            else:
+                mm(R["nU"], [(M("nI"), P), (M("B2"), t("isk"))])
+            if UV >= 2:
+                tt(R["U"], P, R["ms"], AL.subtract)
+            else:
+                mm(R["U"], [(M("I"), P), (M("nB2"), t("isk"))])
             tt(t("t1"), st("Tp"), R["nU"], AL.min)
             tt(st("Tpo"), t("t1"), R["U"], AL.max)
             mm(R["Sp"], [(M("I"), st("S")), (M("Msg"), t("nc"))])
@@ -403,8 +490,14 @@ def build():
             mm(R["D"], [(M("nI"), P), (M("N2"), t("nc")), (M("I"), xk)])
             act(R["Wp"], R["D"], AF.Sign, 2.0 - 1.0 / 512)
             Fv, Bv = V("FB", 2 * c0, 2 * (c0 + n), 2), V("FB", 2 * c0 + 1, 2 * (c0 + n), 2)
+            if BV:
+                act(R["nW"], R["D"], AF.Sign, 1.0 / 512 - 2.0, -1.0)
+                tt(R["Bp"], xk, R["nW"], AL.min)
             tt(Fv, xk, R["Wp"], AL.min)
-            mm(R["Bp"], [(M("I"), xk), (M("nI"), V("one", 0, n)), (M("nI"), Fv)])
+            if not BV:
+                mm(R["Bp"], [(M("I"), xk), (M("nI"), V("one", 0, n)), (M("nI"), Fv)])
+            if PAIR[1]:
+                twice(R["B2"], R["Bp"], AF.Identity)
             act(Bv, R["Bp"], AF.Identity)
             tag[0] = (v, "m%d" % ci)
             mm(R["u"], [(M("Mw"), st("Tpo")), (M("Msm"), t("isk")), (M("Mnc"), t("nc")), (M("Mx"), xk)])
@@ -446,23 +539,42 @@ def build():
             base = [(M("Sm"), st("Z")), (M("ISm"), t("Zs")), (M("SI"), t("Za")), (M("IR"), t("Zk"))]
             tag[0] = (v, "l%d" % ci)
             mm(R["L1"], base + [(M("Pm2"), t("pr"))])
+            if LV:
+                act(t("L1s"), R["L1"], AF.Identity)
             tag[0] = (v, "e%d" % ci)
-            cnt = passes(ci, "Gp", "c2", R["Bp"], AL.is_lt, "ps1", [])
+            cnt = passes(ci, "Gp", "c2", R["B2"], AL.is_lt, "ps1", [])
             tag[0] = (v, "t%d" % ci)
             act(t("e"), cnt, AF.Sign, -1.5)
             mm(R["val"], [(M("LT"), t("isk")), (M("Mv"), t("e"))])
             ts(t("X"), R["val"], col("x"), AL.is_ge)
             tt(t("Q"), t("X"), R["L1"], AL.mult)
-            mm(R["new"], base + [(M("Pm"), t("pr")), (M("M15"), t("J")), (M("SI4"), t("Q"))])
-            act(t("aZ"), R["new"], AF.Abs)
+            nx = lambda k: V(k, (v + 1) * C + c0, (v + 1) * C + c0 + n)
+            one = ONE and not last
+            if LV:
+                nz = st("nz")
+                mm(R["new"], [(M("NBm"), t("pr")), (M("M15"), t("J")), (M("SI4"), t("Q"))])
+                tt(nz, t("L1s"), R["new"], AL.add)
+            else:
+                nz = R["new"]
+                mm(nz, base + [(M("Pm"), t("pr")), (M("M15"), t("J")), (M("SI4"), t("Q"))])
+                if one:
+                    act(st("nz"), nz, AF.Identity)
+            if one:
+                send("a", v, ci, [(st("nz"), nx("Zf"))])
+                tag[0] = (v + 1, "r%d" % ci)
+                act(t("aZ"), nx("Zf"), AF.Abs)
+                ts(nx("nm"), t("aZ"), -1.0, AL.add)
+                cp(nx("Z"), nx("Zf"))
+                continue
+            act(t("aZ"), nz, AF.Abs)
             if not last:
                 ts(st("nmo"), t("aZ"), -1.0, AL.add)
-                cp(st("Zo"), R["new"])
-                nx = lambda k: V(k, (v + 1) * C + c0, (v + 1) * C + c0 + n)
-                send("a", v, ci, [(st("nmo"), nx("nm")), (st("Zo"), nx("Z"))])
+                send("a", v, ci, [(st("nmo"), nx("nm"))])
+                cp(st("Zo"), nz)
+                send("z", v, ci, [(st("Zo"), nx("Z"))])
             else:
                 ts(t("onm"), t("aZ"), -1.0, AL.add)
-                ts(t("omk"), R["new"], 0.0, AL.is_lt)
+                ts(t("omk"), nz, 0.0, AL.is_lt)
                 store(lambda T, c0=c0, n=n: T.ynam[:, c0:c0 + n], t("onm"))
                 store(lambda T, c0=c0, n=n: T.ymrk[:, c0:c0 + n], t("omk"))
     return ops
@@ -579,7 +691,7 @@ def plan():
             if tg is None:
                 key[i] = min([key[j] - cost[i] - extra[i] for j in succ[i]] + [1e9])
             else:
-                key[i] = tg[0] * off["T"] + off[tg[1]] + rel[i] + off.get(tg[1] + ("a" if tg[0] == 0 else "z" if tg[0] == NV - 1 else "m"), 0)
+                key[i] = tg[0] * off["T"] + off.get(tg[1], -9000) + rel[i] + off.get(tg[1] + ("a" if tg[0] == 0 else "z" if tg[0] == NV - 1 else "m"), 0)
         for i in range(n):
             key[i] = max([key[i]] + [key[j] + 1e-3 for j in pred[i]])
         return key
@@ -664,7 +776,7 @@ def rank_program(g, core, T, topo):
         for s, c in waits:
             q.wait_ge(T.sem[s], c * unit(s))
         if o["kind"] == "send":
-            g.remote_dma_fused([RemoteDMATransfer(dst_ids=[DstId(rid=rid, pnc=pid)], dma_engine_mask=mk[j], remote_sem=T.sem[o["sem"]],
+            g.remote_dma_fused([RemoteDMATransfer(dst_ids=[DstId(rid=rid, pnc=pid)], dma_engine_mask=mk[j] if len(o["fn"]) > 1 else mk[0] | mk[1], remote_sem=T.sem[o["sem"]],
                                                   src=ap(T, a), dst=ap(T, b)) for j, (a, b) in enumerate(o["fn"])],
                                local_sem=T.sem["sent"])
         elif o["kind"] == "dma":

@@ -1,99 +1,55 @@
 import numpy as np
-from concourse.bass import DstId, RemoteDMATransfer
 from concourse.mybir import AluOpType, ActivationFunctionType
 
 W, C, NV = 2048, 256, 6
-CHUNKS = [64, 64, 64, 64]
-SGROUPS = [[0, 1, 2, 3]]
-ASUB = 16
+NB, BN = 4, 64
+GW = 16 * BN + 16
+SGROUPS = [[0, 1], [2, 3]]
+ZGROUPS = [[0], [1], [2], [3]]
 BGROUPS = [[0, 1, 2, 3]]
-SEED, NOISE, ROUNDS = 0, 60.0, 12
-SEARCH, DB = [], []
-OFFS = {'T': 17874, 'g0': 648, 'c0': 412, 'h0': -533, 'o0': 3347, 'f0': 4937, 'm0': -1076, 'b0': 6503, 'l0': 9126, 'e0': 1097,
-        't0': 10429, 's0': 16550, 'g1': -1103, 'c1': -1759, 'h1': 3848, 'o1': 6245, 'f1': 7762, 'm1': 3316, 'b1': 5204, 'l1': 7857,
-        'e1': 5315, 't1': 12711, 's1': 14996, 'g2': 1904, 'c2': 6101, 'h2': 8577, 'o2': -888, 'f2': 4061, 'm2': 6449, 'b2': 12828,
-        'l2': 121, 'e2': 10801, 't2': 13284, 's2': 7049, 'g3': 5232, 'c3': 4432, 'h3': 4939, 'o3': 8168, 'f3': 8646, 'm3': 8814,
-        'b3': 14869, 'l3': 18755, 'e3': 16067, 't3': 20886, 's3': 12001, 'e0a': -1321, 'c1a': -1104, 't2a': 3201, 'l0z': 2561,
-        'b1a': -1806, 'e0z': -1253, 'e2a': 4389, 't0z': 652, 's3z': -331, 'm0z': 3344, 'o1z': 364, 'b3a': -3636, 'c2a': 1042,
-        'b0a': -1799, 'f2z': 1887, 'g1a': 362, 't1a': -1354, 'm2z': 159, 'h2a': 633, 'o0a': -521, 'l1z': 185, 'g1z': -2257,
-        'c1z': -547, 'b3z': -2654, 'o2z': -3090, 'g3z': -222, 'f1a': -882, 'c3a': 1546, 't0a': 239, 'm2a': 1668, 'g2a': 238,
-        'f0a': 2291, 'm1z': 2114, 'e3a': 1447, 'g2z': 1057, 'e1a': 589, 's3a': -1271, 'h3z': -3444, 't1z': 5509, 'l3a': -342,
-        't3a': 121, 'l3z': -855, 'm3a': -311, 'b2z': 1273, 't3z': 2215, 'h3a': 209, 'o2a': -2212, 'g0z': -1586, 'e3z': -287,
-        'g0a': 566, 'b2a': -2410, 't2z': 373, 'b1z': -1705, 'o3z': -892, 'h1a': 574, 'l2z': 373, 'c3z': 228, 'o0z': 299,
-        'c0a': -3977, 'g3a': -1733, 'l1a': -117, 'm0a': -248, 'o1a': 2473, 'e1z': 1063, 'h0z': 226, 'f2a': -129, 'l2a': 1877,
-        'f1z': -243, 'h0a': 638, 'o3a': -302, 'e2z': 167}
-CHUNKS, SGROUPS, BGROUPS, ROUNDS = [128, 128], [[0, 1]], [[0, 1]], 2
-ASUB = 32
-OFFS = {'T': 13610, 'g0': -4370, 'c0': 4450, 'h0': 6380, 'o0': -860, 'f0': -180, 'm0': 7360, 'b0': 16400, 'l0': -3160, 'e0': 9000,
-        't0': 7840, 's0': 14120, 'g1': 4490, 'c1': 6360, 'h1': -490, 'o1': 8050, 'f1': -1930, 'm1': -2110, 'b1': 7550, 'l1': 5580,
-        'e1': 17250, 't1': 11790, 's1': 12330, 't0a': 4850, 'b0z': 9480, 'o1a': 240, 'h1a': -4840, 'm1a': 1400, 'b1z': 7670,
-        'e0a': -9540, 'l0a': -2760, 'm1z': 220, 'e1a': 1050, 't1a': 2160, 's1z': 1540, 'f0z': -4360, 't1z': 5960, 'e1z': -1060,
-        's1a': 5650, 'o0a': -2470, 'l1z': 1050, 'f0a': 4400, 'l0z': 5580, 'g1z': -8710, 'g0a': -8180, 't0z': -6830, 'o0z': 3320,
-        'f1a': 10010, 'g0z': 9710, 'h0a': -3700, 'g1a': -1410, 'h1z': 6780, 'm0z': -6270, 'f1z': -5160, 'l1a': -7300,
-        'b1a': -2830, 'c0a': -2900, 'e0z': 880, 'b0a': -3230, 'm0a': 1460, 'c1z': -80}
-_L, _C = 0.5, 3000.0 / 5500
-MODELS = [{"xc": _L, "xsend": _C}, {"ga": 0.7, "sc": 0.5, "xc": _L, "xsend": _C * 1.4}, {"ga": 1.33, "sc": 1.5, "xc": _L, "xsend": _C * .7},
-          {"xc": 1.8 * _L, "xsend": 2 * _C}, {"ga": 1.33, "sc": 0.6, "xc": _L, "xsend": 1.5 * _C},
-          {"ga": 0.75, "sc": 1.4, "xc": 1.5 * _L, "xsend": _C, "send": 1.5}]
-GSUB = 32
-KB = 3
-MKP, UV, DUP, BV, LV, ONE = True, 0, 2, False, False, False
-PAIR, NACT = [1, 1], 40
-FV, FA = 48.0, 48.0
-VG, VG0 = [32, 96, 160], [32]
-WIN = W + 512
-GATH, SCAT, PEC, LAT, DMAL, COMM = 1.56, 3.8, 0.5, 200.0, 2400.0, 5500.0
-SENDC = 1000.0
-CHUNKS, SGROUPS, BGROUPS, ASUB, PAIR, NACT = [64] * 4, [[0, 1, 2], [3]], [[0, 1, 2, 3]], 16, [0, 0], 20
-FV, FA, VG, VG0, LAT, COMM = 0.0, 0.0, [96, 160], [160], 310.0, 3000.0
-_L = 250.0 / 310
-MODELS = [{"xc": _L}, {"ga": 0.7, "sc": 0.5, "xc": _L, "xsend": 1.4}, {"ga": 1.33, "sc": 1.5, "xc": _L, "xsend": .8},
-          {"xc": 1.6 * _L, "xsend": 1.6}, {"ga": 1.33, "sc": 0.6, "xc": .75 * _L, "xsend": 1.2},
-          {"ga": 0.75, "sc": 1.4, "xc": 1.3 * _L, "send": 1.5}]
-OFFS = {'T': 15630, 'g0': 560, 'c0': -810, 'h0': 480, 'o0': 4730, 'f0': 6080, 'm0': -3540, 'b0': 7160, 'l0': 8180, 'e0': 7500,
-        't0': 11120, 's0': 10070, 'g1': 1020, 'c1': 1510, 'h1': 4930, 'o1': 6010, 'f1': 6570, 'm1': 5360, 'b1': 6770, 'l1': 6950,
-        'e1': 3050, 't1': 11910, 's1': 16240, 'g2': 2630, 'c2': 6440, 'h2': 11060, 'o2': -1740, 'f2': 8500, 'm2': 8910,
-        'b2': 13550, 'l2': 2820, 'e2': 11860, 't2': 13170, 's2': 7040, 'g3': 3380, 'c3': 5760, 'h3': 6580, 'o3': 7460, 'f3': 9530,
-        'm3': 5290, 'b3': 11490, 'l3': 20880, 'e3': 13310, 't3': 16780, 's3': 12210, 't0z': 2240, 'b1a': -320, 'c2a': 350,
-        'm2a': -580, 'e0z': -1100, 'l0z': 1960, 'e2a': 3230, 't2z': 2330, 't0a': 460, 'f2a': 2360, 'l1a': 4520, 'c1a': 5760,
-        'h1a': 2180, 'o1z': -70, 'l3a': -2280, 'b0z': 2480, 'e1z': -2090, 'l3z': 510, 'c0a': 2900, 'm1a': 770, 'h0a': 490,
-        'f0a': 400, 'c0z': -1060, 'm3a': -1210, 't1z': -810, 'c3z': 1530, 'e2z': 200, 'f1a': -6200, 'b2z': -90, 'f3a': -1130,
-        'o2z': -700, 'h3a': 6230, 'e3z': -620, 't2a': -420, 'g2a': -120, 'c2z': 1320, 'g2z': -5230, 'l0a': -690, 'e1a': -520,
-        't3z': 2610, 's3a': 1730, 'b3z': -230, 'f0z': 2290, 'g3a': -770, 'h2z': -1410, 'b0a': 470, 'o1a': 650, 'h2a': 3630,
-        'b3a': 3280, 'o2a': -620, 'o3z': -7330, 'c3a': -4120, 'l1z': 2820, 'm0z': 970, 'c1z': -650, 't1a': -710, 'o0z': 140,
-        'm1z': -2430, 's3z': 1510, 'h3z': 140, 'm0a': -160, 'f2z': 1180, 'o3a': -390, 'l2z': -500, 'f1z': 80, 'g1a': 1150,
-        'h1z': 1040}
+ABSB, ASUB = [1, 2, 3], 256
+BATCH = [6, 6, 3]
+GSUB, HSUB = 32, 5
+VG, VG0 = [32, 160], [32, 96]
+OPB = {"c": [2, 3, 2, 2], "e": [3, 3, 2, 3]}
+CNT = {"c": [0, 0, 0, 0], "e": [1, 1, 0, 1]}
+MKV, PV, NVEC = False, True, 12
+OM, ETA, KILL, CU, BIG = 2.0 ** 18, 2.0 ** -8, 2.0 ** 40, 4096.0, 8192.0
+WIN = 2 * W + 2 * C + 16
+GATH, SCAT, PEC, LAT, DMAL, COMM, SENDC = 1.56, 3.8, 0.5, 260.0, 2400.0, 3000.0, 1000.0
+MODELS = [{}, {"ga": 1.2, "sc": 1.2, "xc": 1.3, "xsend": 1.5}]
+CHECK = [{}, {"ga": 0.7, "sc": 0.5, "xsend": 1.4}, {"ga": 1.33, "sc": 1.5, "xsend": .8},
+         {"xc": 1.5, "xsend": 1.6}, {"ga": 1.33, "sc": 0.6, "xc": .7, "xsend": 1.2, "p": 1.2},
+         {"ga": 0.75, "sc": 1.4, "xc": 1.2, "send": 1.5}]
+TRIES, MOVES, BUMP, HEAT, COOL, SEED = 800, 5000, 500.0, 500.0, 100.0, 0
 
 BF, HF, F4, I4, U2 = "bfloat16", "float16", "float32", "int32", "uint16"
 SB = {
-    "y": (WIN, BF), "x0": (W, BF), "z0": (W, BF), "yo": (W, BF),
-    "nami": (C, I4), "mrki": (C, I4), "owni": (C // 2, I4), "picb": (C, BF), "wti": (4, I4), "thri": (8, I4),
-    "G": (16 * C, BF), "Gp": (16 * C, BF), "c1": (16 * C, BF), "c2": (16 * C, BF),
-    "nm": (NV * C, U2), "Z": (NV * C, HF), "Tp": (NV * C, HF), "S": (NV * C, BF),
-    "nmo": (NV * C, U2), "Zo": (NV * C, HF), "Tpo": (NV * C, HF), "So": (NV * C, BF),
-    "cl": (C, BF), "isk": (C, BF), "Zk": (C, HF), "Za": (C, HF), "Zs": (C, HF), "nc": (C, BF), "xk": (4 * C, BF), "L1s": (C, F4), "nz": (NV * C, F4), "Zf": (NV * C, F4), "W4": (144, BF),
-    "FB": (2 * C, BF), "t1": (C, HF), "q": (C, I4), "J": (C, HF), "A1": (C, HF), "pr": (C, HF), "e": (C, BF),
-    "X": (C, BF), "Q": (C, F4), "aZ": (C, F4), "a128": (16, BF), "WS": (144, BF), "offk": (128, U2), "a8": (32, BF),
-    "offs": (32, U2), "cix": (C, BF), "W2": (144, BF), "WC": (144, HF), "OwnT": (C, HF), "owe": (C // 2, HF), "owo": (C // 2, HF),
-    "onm": (C, F4), "omk": (C, F4), "opc": (C, BF), "oct": (C, F4),
+    "y": (WIN, BF), "yo": (WIN, BF), "x0": (W, BF), "z0": (W, BF),
+    "nami": (C, I4), "mrki": (C, I4), "owni": (C // 2, I4), "wti": (4, I4), "thri": (8, I4),
+    "G": (NB * GW, BF), "Gp": (NB * GW, BF), "c1": (16 * C, BF), "c2": (16 * C, BF),
+    "nm": (NV * C, U2), "nmo": (NV * C, U2), "Zi": (NV * C, HF), "Zo": (NV * C, HF), "Ti": (NV * 2 * C, BF), "To": (NV * 2 * C, BF),
+    "cl": (C, BF), "isk": (C, BF), "Zk": (C, HF), "xx": (2 * C, BF), "m": (C, BF), "FB": (2 * C, BF), "pr": (C, HF),
+    "L1": (C, HF), "e": (C, BF), "X": (C, BF), "aZ": (C, F4), "offk": (32, U2), "offs": (32, U2),
+    "a128": (16, BF), "cix": (C, BF), "OwnT": (C, HF), "owe": (C // 2, HF), "owo": (C // 2, HF),
+    "onm": (C, F4), "omk": (C, F4), "oct": (C, F4),
     "ta": (C, F4), "tb": (C, F4), "thb": (8, BF), "thc": (8, F4), "wm": (4, I4), "wc": (4, F4),
-    "pi": (4, I4), "si": (4, I4), "col": (48, F4), "jj": (16, F4), "MK": (16, F4), "OH": (16, F4),
-    "m4": (128, BF), "m5": (128, BF), "E1": (128, BF), "E": (128, BF), "Rr": (128, BF), "m1": (128, BF), "m2": (128, BF), "m3": (128, BF),
-    "u0": (144, BF), "Wd": (144, BF), "Wh": (144, HF), "WA": (144, HF), "WB": (144, HF), "Eg": (128, BF), "Eg0": (128, BF),
-    "one": (128, BF),
+    "pi": (4, I4), "si": (4, I4), "col": (64, F4), "jj": (16, F4), "MK": (16, F4), "OH": (16, F4),
+    "u0": (144, BF), "Wd": (144, BF), "W18": (144, BF), "WS": (144, BF), "WA": (144, BF), "ug": (128, BF), "Eg": (128, BF),
+    "one": (BN, BF), "Mc": (8, BF),
 }
-for _m in ("I", "nI", "N2", "D14", "Is", "ON", "GT", "LT", "Mr", "Mv", "Mpar", "B2", "nB2", "Mx", "Mnc", "Msm", "Msg"):
-    SB[_m] = (128, BF)
-for _m in ("Ih", "ONh", "Sm", "ISm", "SI", "IR", "Pm", "Pm2", "NBm", "M15", "Mw", "Mpr", "Mdi", "h1", "h2"):
-    SB[_m] = (128, HF)
-SB["SI4"] = (128, F4)
+MB = ["E1", "E", "Rr", "ON", "I", "nOm", "p2Om", "Ie", "Iem", "It", "pK", "nK", "pKS", "nKS", "pKON", "nKON", "pKGE", "nKGE",
+      "LT", "Mv", "nh", "Mr", "pA", "nA", "pR", "nR", "D14", "Sd", "nSd", "Sm", "SmI", "ISd", "Mpar", "nON", "Mt0", "Mt1", "Mth",
+      "Tc", "Doff", "Gm", "pNB", "nNB", "Gc", "Mpr", "Mdi"]
+MH = ["pMw", "nMw"]
+SB["MB"], SB["MH"] = (128 * len(MB), BF), (128 * len(MH), HF)
+MAT = {k: (b, 128 * i) for b, ks in (("MB", MB), ("MH", MH)) for i, k in enumerate(ks)}
 SCRATCH = {k: ("sbuf", [128, n], d) for k, (n, d) in SB.items()}
 for _b in range(8):
     SCRATCH["ps%d" % _b] = ("psum", [128, 512], F4)
-NCH = len(CHUNKS)
-LOADS = ["nam", "dep0", "dep1", "mrk", "thr", "pic", "own", "wt"]
+LOADS = ["nam", "dep0", "dep1", "mrk", "thr", "pic0", "pic1", "pic2", "pic3", "own", "wt"]
 SEMAPHORES = (["qv", "qa", "qp", "qg", "sent", "stored"] + ["ld_" + k for k in LOADS]
-              + ["r%s%d_%d" % (k, v, c) for k in "abz" for v in range(1, NV) for c in range(NCH)])
+              + ["r%s%d_%d" % (k, v, c) for k in "azb" for v in range(1, NV) for c in range(NB)])
 AL, AF = AluOpType, ActivationFunctionType
 
 
@@ -119,60 +75,40 @@ def two(*vs):
     return all(v[0] in SB and SB[v[0]][1] in (BF, HF, U2) for v in vs)
 
 
-def regions():
-    out = []
-    for ci, n in enumerate(CHUNKS):
-        if NCH == 2:
-            b = [2 + 3 * ci, 3 + 3 * ci, 4 + 3 * ci]
-            t = {"Pp": (0, 0), "Bp": (0, 1), "Sp": (0, 2), "oT": (0, 3), "R": (1, 0), "D": (1, 0), "val": (1, 0), "mk": (1, 1),
-                 "Wp": (1, 1), "ma": (1, 2), "Tab": (2, 1), "ms": (1, 3), "u": (1, 3), "Zsum": (2, 0), "L1": (2, 0),
-                 "ZT": (2, 1), "U": (2, 2), "new": (2, 2), "nU": (2, 3), "nW": (1, 2)}
-            t.update({"Sp": (1, 2), "Bp": (2, 3), "oT": (1, 1)})
-            out.append({k: V("ps%d" % b[i], 128 * s, 128 * s + n) for k, (i, s) in t.items()})
-            out[-1].update({"P2": V("ps%d" % b[0], 0, 2 * n, 2 - PAIR[0]), "B2": V("ps%d" % b[0], 256, 256 + 2 * n, 2 - PAIR[1])})
-            if not PAIR[1]:
-                out[-1]["B2"] = V("ps%d" % b[0], 256, 256 + n, 2)
-                out[-1]["Bp"] = V("ps%d" % b[0], 256, 256 + n)
-        elif NCH == 3:
-            ob, mb = 2 + 2 * ci, 3 + 2 * ci
-            t = {"Pp": (ob, 0), "Bp": (ob, 1), "Sp": (ob, 2), "oT": (ob, 4), "R": (mb, 0), "D": (mb, 0), "val": (mb, 0),
-                 "mk": (ob, 3), "Wp": (ob, 3), "ma": (ob, 3), "Tab": (mb, 3), "ms": (mb, 1), "u": (mb, 1), "Zsum": (mb, 2),
-                 "L1": (mb, 2), "ZT": (mb, 3), "U": (mb, 4), "new": (mb, 4), "nU": (ob, 2)}
-            out.append({k: V("ps%d" % b, 96 * s, 96 * s + n) for k, (b, s) in t.items()})
-        else:
-            ob, mb, h = 2 + ci % 2, 4 + ci, 4 * (ci // 2)
-            t = {"Pp": (ob, h), "Bp": (ob, h + 1), "Sp": (ob, h + 2), "oT": (ob, h + 3), "R": (mb, 0), "D": (mb, 0), "val": (mb, 0),
-                 "mk": (mb, 1), "Wp": (mb, 1), "ma": (mb, 2), "Tab": (mb, 5), "ms": (mb, 3), "u": (mb, 3), "Zsum": (mb, 4),
-                 "L1": (mb, 4), "ZT": (mb, 5), "U": (mb, 6), "new": (mb, 6), "nU": (mb, 7), "nW": (mb, 2)}
-            out.append({k: V("ps%d" % b, 64 * s, 64 * s + n) for k, (b, s) in t.items()})
-            out[-1].update({"P2": out[-1]["Pp"], "B2": out[-1]["Bp"]})
+def regions(ci):
+    slot = {"R": 0, "val": 0, "zt": 1, "oa": 1, "mk": 2, "new": 2, "th": 3, "L1": 7, "P": 4, "F": 4, "A": 0, "Tn": 5, "pr": 6}
+    out = {k: V("ps%d" % (4 + ci), BN * s, BN * s + BN) for k, s in slot.items()}
+    out["Pa"] = V("ps%d" % OPB["c"][ci], BN * ci, BN * ci + BN)
+    out["B"] = V("ps%d" % OPB["e"][ci], BN * (NB + ci), BN * (NB + ci) + BN)
     return out
 
 
 def build():
     ops = []
     tag = [None]
-    moved = []
+    kept = []
 
     def add(eng, cost, reads, writes, fn, kind="c", sem=None, after=None, ck=None):
-        ops.append({"e": eng, "cost": cost + (FV if eng == "v" else FA if eng == "a" else 0.0), "r": [r for r in reads if isv(r)], "w": writes, "fn": fn, "kind": kind, "sem": sem,
-                    "after": after, "ck": ck or (kind if kind != "c" else eng), "tag": tag[0], "cont": False})
+        ops.append({"e": eng, "cost": cost, "r": [r for r in reads if isv(r)], "w": writes, "fn": fn, "kind": kind, "sem": sem,
+                    "after": after, "ck": ck or (kind if kind != "c" else eng), "tag": tag[0], "cont": False, "n": 1})
         return len(ops) - 1
 
     def a_(T, x):
         return ap(T, x) if isv(x) else x
 
     def ts(out, in0, s1, op0, s2=None, op1=None):
-        if (tag[0] is None and len(moved) < NACT and op0 == AL.mult and (op1 is None or op1 == AL.add)
-                and SB[out[0]][1] in (BF, F4) and in0[0] in SB and SB[in0[0]][1] in (BF, F4)):
-            moved.append(out)
-            return act(out, in0, AF.Identity, 0.0 if s2 is None else s2, s1)
         n = nel(in0) * (0.5 if two(out, in0) else 1.0)
         if op1 is None:
             f = lambda g, T: g.vector.tensor_scalar(ap(T, out), ap(T, in0), a_(T, s1), None, op0)
         else:
             f = lambda g, T: g.vector.tensor_scalar(ap(T, out), ap(T, in0), a_(T, s1), a_(T, s2), op0, op1)
         add("v", max(64, n), [in0, s1, s2], [out], f)
+
+    def lin(out, in0, a, b=0.0):
+        if len(kept) < NVEC:
+            kept.append(out)
+            return ts(out, in0, a, AL.mult, b, AL.add)
+        act(out, in0, AF.Identity, b, a)
 
     def cp(out, in0):
         n = nel(in0) * (0.5 if two(out, in0) else 1.0)
@@ -181,6 +117,11 @@ def build():
     def tt(out, in0, in1, op):
         n = nel(in0) * (2.0 if in0[0] in SB and in1[0] in SB else 1.0)
         add("v", max(64, n), [in0, in1], [out], lambda g, T: g.vector.tensor_tensor(ap(T, out), ap(T, in0), ap(T, in1), op))
+
+    def compare(rows, opnd, op):
+        f = lambda g, T: [g.vector.tensor_tensor(ap(T, o), ap(T, x), ap(T, opnd), op) for o, x in rows]
+        i = add("v", BN * len(rows), [x for o, x in rows] + [opnd], [o for o, x in rows], f)
+        ops[i]["n"] = len(rows)
 
     def ms(out, c):
         add("v", max(64, nel(out) * (0.5 if two(out) else 1.0)), [], [out], lambda g, T: g.vector.memset(ap(T, out), c))
@@ -197,7 +138,7 @@ def build():
             lambda g, T: g.scalar.activation(ap(T, out), ap(T, win).indirect(ap(T, off)), AF.Identity), ck="ga")
 
     def mm(out, terms, first=True, last=True, whole=None):
-        cost = sum(max(64, nel(r)) * (4 if SB[r[0]][1] == F4 else 1) for l, r in terms) * PEC + 20
+        cost = sum(max(64, nel(r)) for l, r in terms) * PEC + 20
 
         def f(g, T):
             ins = None
@@ -217,6 +158,9 @@ def build():
     def asel(out, in0, pat, op, fill, base, cm):
         add("g", 210 + 2 * nel(out), [in0], [out], lambda g, T: g.affine_select(ap(T, out), ap(T, in0), pat, op, fill, base, cm))
 
+    def diag(out, in0, fill):
+        asel(out, in0, [[1, 128]], AL.not_equal, fill, 0, -1)
+
     def load(name, out, src, eng="s"):
         if eng == "g":
             f = lambda g, T: g.dma_start(ap(T, out), src(T), allow_slow_non_contiguous=True)
@@ -227,7 +171,8 @@ def build():
     def store(dst, src):
         add("s", 100, [src], [], lambda g, T: g.sync.dma_start(dst(T), ap(T, src)), "dma", "stored")
 
-    M = lambda k: V(k, 0, 128)
+    M = lambda k: V(MAT[k][0], MAT[k][1], MAT[k][1] + 128)
+    Ms = lambda k, r: V(MAT[k][0], MAT[k][1] + r, MAT[k][1] + 128, 16)
     sel = lambda k, r: V(k, 15 - r, 143 - r)
     sel2 = lambda k, b: V(k, 14 - 2 * b, 142 - 2 * b)
     names = {}
@@ -238,345 +183,299 @@ def build():
         return V("col", names[k], names[k] + 1)
     MK = lambda j: V("MK", j, j + 1)
     OH = lambda j: V("OH", j, j + 1)
+    top8 = (0, 8)
 
-    load("nam", V("nami", 0, C), lambda T: T.nam[:])
+    def state(buf, v, ci, part):
+        grp = [x for x in BGROUPS if ci in x][0]
+        lo = 2 * (v * C + grp[0] * BN) + (part * len(grp) + ci - grp[0]) * BN
+        return V(buf, lo, lo + BN)
+
     load("dep0", V("x0", 0, W // 2), lambda T: T.dep[:, 0:W // 2])
     load("dep1", V("x0", W // 2, W), lambda T: T.dep[:, W // 2:W])
+    load("nam", V("nami", 0, C), lambda T: T.nam[:])
     load("mrk", V("mrki", 0, C), lambda T: T.mrk[:])
-    load("thr", V("thri", 0, NV, 1, (0, 8)), lambda T: T.thr[:])
-    load("pic", V("picb", 0, C), lambda T: T.pic[:])
+    load("thr", V("thri", 0, NV, 1, top8), lambda T: T.thr[:])
+    for j, grp in enumerate(BGROUPS):
+        lo, n = grp[0] * BN, len(grp) * BN
+        load("pic%d" % j, V("Ti", 2 * lo, 2 * lo + n), lambda T, lo=lo, n=n: T.pic[:, lo:lo + n])
     load("own", V("owni", 0, C // 2), lambda T: T.own[:])
     E0 = V("u0", 15, 143)
     iota(V("u0", 0, 144), [[1, 144]], -15, -1)
     iota(V("pi", 0, 1), [[0, 1]], 0, 1)
     asel(M("E1"), E0, [[16, 8], [0, 16]], AL.is_ge, 200.0, 15, -1)
     asel(M("E"), M("E1"), [[-16, 8], [0, 16]], AL.is_ge, 200.0, 0, 1)
+    iota(V("ug", 0, 128, 1, top8), [[1, 8], [0, 16]], 0, -1)
+    ts(V("Eg", 0, 128, 1, top8), V("ug", 0, 128, 1, top8), 0.0, AL.is_equal)
+    for k, c in (("I", 1.0), ("nOm", -OM), ("p2Om", 2 * OM), ("Ie", 1 - ETA), ("Iem", (ETA - 1) * OM),
+                 ("It", -256.0 / OM), ("pK", KILL), ("nK", -KILL)):
+        ts(M(k), E0, 0.0, AL.is_equal, c, AL.mult)
     cp(col("p"), V("pi", 0, 1))
-    ts(V("jj", 0, 16), V("u0", 15, 31), col("p"), AL.add)
-    ms(M("one"), 1.0)
-    asel(V("Eg0", 0, 128, 1, (0, 8)), V("one", 0, 128, 1, (0, 8)), [[1, 128]], AL.is_ge, 0.0, 0, -16)
-    asel(V("Eg", 0, 128, 1, (0, 8)), V("Eg0", 0, 128, 1, (0, 8)), [[-1, 128]], AL.is_ge, 0.0, 15, 16)
-    ts(V("a8", 0, 32), V("u0", 15, 47), col("p"), AL.add, 8.0, AL.mult)
-    ts(V("cix", 0, 128), E0, col("p"), AL.add, 1.0, AL.add)
-    ts(V("cix", 128, 256), E0, col("p"), AL.add, 129.0, AL.add)
-    load("wt", V("wti", 0, 1), lambda T: T.wt[:], "g")
-    ts(M("nI"), E0, 0.0, AL.is_equal, -1.0, AL.mult)
-    ts(M("Is"), E0, 0.0, AL.is_equal, 1.0 / 256, AL.mult)
-    ts(M("I"), E0, 0.0, AL.is_equal)
-    ts(M("Ih"), E0, 0.0, AL.is_equal)
     ts(V("si", 0, 1), V("pi", 0, 1), 15, AL.bitwise_and)
     s = col("s")
     cp(s, V("si", 0, 1))
-    ts(col("ns"), s, -1.0, AL.mult)
-    ts(V("Wd", 0, 144), V("u0", 0, 144), col("ns"), AL.is_equal)
-    ts(V("Wh", 0, 144), V("u0", 0, 144), col("ns"), AL.is_equal)
-    NB = 16 // DUP
-    tt(V("W2", 0, 143), V("Wd", 0, 143), V("Wd", 1, 144), AL.add)
-    if DUP == 4:
-        tt(V("W4", 0, 141), V("W2", 0, 141), V("W2", 2, 143), AL.add)
-    ts(V("WS", 0, 145 - DUP), V("W4" if DUP == 4 else "W2", 0, 145 - DUP), s, AL.mult)
-    ts(V("si", 1, 2), V("si", 0, 1), 1, AL.arith_shift_right)
-    cp(col("s2"), V("si", 1, 2))
-    ts(V("si", 2, 3), V("si", 0, 1), DUP // 2, AL.arith_shift_right)
-    ts(col("s16"), V("si", 2, 3), 16.0, AL.mult)
-    ts(V("a128", 0, 16), V("jj", 0, 16), 16.0 * NB, AL.mult)
+    ts(V("si", 1, 2), V("pi", 0, 1), 1, AL.bitwise_and)
+    cp(col("odd"), V("si", 1, 2))
+    lin(col("ns"), s, -1.0)
+    lin(V("jj", 0, 16), V("u0", 15, 31), 1.0, col("p"))
     ts(V("MK", 0, 16), V("jj", 0, 16), s, AL.is_le)
     ts(V("OH", 0, 16), V("jj", 0, 16), s, AL.is_equal)
-    ts(M("ON"), M("E"), 100.0, AL.is_lt)
-    ts(M("ONh"), M("E"), 100.0, AL.is_lt)
-    ts(M("GT"), M("E"), 0.0, AL.is_lt)
-    ts(M("B2"), M("E"), 100.0, AL.is_lt, 2.0, AL.mult)
-    ts(M("nB2"), M("E"), 100.0, AL.is_lt, -2.0, AL.mult)
-    ts(M("m1"), M("E"), 0.5, AL.is_lt)
-    tt(M("LT"), M("ON"), M("m1"), AL.subtract)
-    tt(M("m2"), M("I"), M("LT"), AL.subtract)
-    ts(M("Mr"), M("m2"), 0.5, AL.mult)
-    tt(M("Mv"), M("Mr"), M("LT"), AL.max)
-    ts(col("np"), OH(0), -1.0, AL.mult)
-    ts(M("Mpar"), M("ON"), col("np"), AL.mult)
-    ts(col("isk"), s, -0.5, AL.mult, 0.5, AL.add)
-    ts(col("x"), s, -1.0, AL.mult, 1.5, AL.add)
-    ts(col("sg"), OH(0), OH(1), AL.subtract, 0.5, AL.mult)
-    ts(col("nsg"), col("sg"), -1.0, AL.mult)
-    ts(M("Msg"), M("I"), col("sg"), AL.mult)
-    ts(col("ncb"), OH(15), 8192.0, AL.mult, 0.5, AL.add)
-    ts(M("N2"), M("B2"), OH(0), AL.mult)
-    ts(col("cn"), OH(15), -1.0 / 32, AL.mult, 1.0 / 32, AL.add)
-    ts(col("bq"), OH(15), -0.5 - 2.0 ** -12, AL.mult)
-    ts(M("Msm"), sel("Wd", 15), 1.5 * 2 ** 25, AL.mult)
-    ts(M("Rr"), M("E"), s, AL.add)
-    ts(M("m4"), M("Rr"), 8.0, AL.is_lt, 32.0, AL.mult)
-    ts(M("m5"), M("Rr"), 12.0, AL.is_lt, 64.0, AL.mult)
-    tt(M("Mx"), M("m5"), M("m4"), AL.subtract)
-    tt(M("m1"), M("Mx"), M("Rr"), AL.mult)
-    ts(M("m2"), M("ON"), 8.0, AL.mult)
-    ts(V("m2", 15, 128, 16), V("ON", 15, 128, 16), 0.125, AL.mult)
-    tt(M("m3"), M("m2"), M("m1"), AL.subtract)
-    ts(M("m1"), M("m3"), OH(15), AL.mult, 1.0 / 256, AL.mult)
-    ts(M("m2"), M("I"), col("cn"), AL.mult)
-    tt(M("Mnc"), M("m1"), M("m2"), AL.add)
-    ts(col("lo8"), MK(8), -1.0, AL.mult, 1.0, AL.add)
-    ts(M("Sm"), M("E"), -1.0, AL.is_equal)
-    tt(M("h2"), M("Ih"), M("Sm"), AL.subtract)
-    ts(M("ISm"), M("h2"), 0.5, AL.mult)
-    ts(M("h1"), M("E"), 1.0, AL.is_equal)
-    tt(M("SI"), M("h1"), M("Ih"), AL.subtract)
-    cp(M("SI4"), M("SI"))
-    ts(M("h2"), sel("Wh", 0), -1.0, AL.mult)
-    tt(M("IR"), M("h2"), M("Ih"), AL.subtract)
-    ts(col("a"), col("lo8"), OH(13), AL.add)
-    ts(M("Pm"), sel("Wh", 0), col("a"), AL.mult)
-    ts(col("n1"), MK(8), 2.0, AL.mult, -1.0, AL.add)
-    ts(col("lo13"), MK(13), -1.0, AL.mult, 1.0, AL.add)
-    ts(col("nb"), col("n1"), col("lo13"), AL.mult)
-    ts(M("NBm"), M("ONh"), col("nb"), AL.mult)
-    tt(M("Pm2"), M("Pm"), M("NBm"), AL.subtract)
-    ts(col("wa"), col("lo8"), OH(12), AL.subtract, OH(14), AL.subtract)
-    ts(col("w9"), OH(12), -1.125, AL.mult, col("nb"), AL.add)
-    ts(col("wb"), col("w9"), OH(14), AL.subtract)
-    ts(V("WB", 0, 142), V("Wh", 1, 143), col("wa"), AL.mult)
-    ts(V("WC", 0, 142), V("Wh", 0, 142), col("wb"), AL.mult)
-    tt(V("WA", 0, 142), V("WB", 0, 142), V("WC", 0, 142), AL.add)
-    ts(M("M15"), M("Ih"), OH(15), AL.mult, 2048.0, AL.mult)
-    ts(M("D14"), M("I"), OH(14), AL.mult)
-    ts(col("c1"), col("s2"), -511.0, AL.mult, 2048.0, AL.add)
-    ts(col("oc"), s, 256.0, AL.mult, col("c1"), AL.add)
+    ts(V("Wd", 0, 144), V("u0", 0, 144), col("ns"), AL.is_equal)
+    ms(V("one", 0, BN), 1.0)
+    for ci in range(NB):
+        ms(V("G", ci * GW, ci * GW + 16), -OM)
+    for k, x, op, c in (("ON", 100.0, AL.is_lt, 1.0), ("Sd", 1.0, AL.is_equal, 1.0), ("Sm", -1.0, AL.is_equal, 1.0),
+                        ("pKGE", 0.5, AL.is_lt, KILL)):
+        ts(M(k), M("E"), x, op, c, AL.mult)
+    lin(col("isk"), s, -0.5, 0.5)
+    lin(col("x"), s, 1.0, -0.5)
+    asel(M("LT"), M("ON"), [[1, 128]], AL.is_gt, 0.0, 0, -1)
+    lin(M("nh"), M("LT"), -0.5)
+    diag(M("Mr"), M("nh"), 0.5)
+    load("wt", V("wti", 0, 1), lambda T: T.wt[:], "g")
+    diag(M("Mv"), M("LT"), 0.5)
+    for k, x, c in (("nSd", "Sd", -1.0), ("pKS", "Sd", KILL), ("nKS", "Sd", -KILL), ("pKON", "ON", KILL), ("nKON", "ON", -KILL),
+                    ("nKGE", "pKGE", -1.0), ("nON", "ON", -1.0)):
+        lin(M(k), M(x), c)
+    diag(M("SmI"), M("Sm"), -1.0)
+    diag(M("ISd"), M("nSd"), 1.0)
+    lin(V("W18", 0, 144), V("Wd", 0, 144), 1.0 / OM)
+    lin(V("WS", 0, 143), V("Wd", 1, 144), s)
+    lin(V("WS", 15, 143, 16), V("Wd", 15, 143, 16), -2048.0)
+    lin(col("s8"), col("odd"), -8.0, 16.0)
+    lin(col("s16"), s, 8.0, col("s8"))
+    lin(V("a128", 0, 16), V("jj", 0, 16), 128.0)
+    lin(col("in6"), MK(7), -1.0, MK(1))
+    lin(col("sg"), col("odd"), -1.0, 0.5)
+    lin(col("par"), col("in6"), col("sg"))
+    lin(M("Mpar"), M("ON"), col("par"))
+    lin(col("h6"), col("in6"), 0.5)
+    lin(V("Mc", 0, 8), Ms("ON", 0), col("h6"))
+    lin(col("t0"), col("in6"), CU)
+    lin(col("t1"), MK(6), -CU / 2, CU / 2)
+    lin(M("Mt0"), M("I"), col("t0"))
+    lin(M("Mt1"), M("Sd"), col("t1"))
+    tt(M("Mth"), M("Mt0"), M("Mt1"), AL.add)
+    lin(col("t2"), col("in6"), CU / 2, -0.5)
+    lin(col("t3"), OH(0), BIG, OH(8))
+    lin(col("thb"), col("t2"), 1.0, col("t3"))
+    lin(col("tc"), OH(0), -256.0)
+    lin(M("Tc"), M("ON"), col("tc"))
+    lin(col("gc"), OH(7), 16.0)
+    lin(M("Gc"), M("ON"), col("gc"))
+    lin(col("f0"), OH(0), 2.0, -1.0)
+    lin(M("Rr"), M("E"), 1.0, s)
+    ts(M("pA"), M("Rr"), 12.0, AL.is_lt, CU, AL.mult)
+    lin(M("nA"), M("pA"), -1.0)
+    lin(col("lo8"), MK(8), -1.0, 1.0)
+    lin(col("lo12"), MK(12), -1.0, 1.0)
+    ts(col("un"), col("lo8"), col("lo12"), AL.add, 4 * CU, AL.mult)
+    lin(col("u15"), OH(15), 2048.0, col("un"))
+    lin(col("mg"), col("u15"), 1.5 * 2 ** 23)
+    lin(M("pR"), M("I"), col("mg"))
+    lin(M("nR"), M("pR"), -1.0)
+    lin(col("r8"), MK(8), -8.0, s)
+    ts(col("cr"), col("r8"), col("lo12"), AL.mult, -CU, AL.mult)
+    lin(col("o1"), col("un"), -0.5, col("cr"))
+    lin(col("o2"), col("lo12"), CU / 2, col("o1"))
+    lin(M("Doff"), M("I"), col("o2"))
+    lin(col("o3"), OH(14), -0.5)
+    lin(col("o4"), OH(15), 1024.0, col("o3"))
+    lin(Ms("Doff", 15), Ms("ON", 15), col("o4"))
+    ts(col("pa"), MK(8), MK(12), AL.subtract, OH(14), AL.add)
+    ts(col("g1"), col("lo12"), OH(14), AL.add, BIG / 2, AL.mult)
+    lin(col("g2"), col("pa"), -2048.0, col("g1"))
+    lin(col("g6"), OH(15), BIG - 1, col("cr"))
+    lin(col("g3"), col("g2"), 1.0, col("g6"))
+    ts(col("g4"), OH(12), col("pa"), AL.subtract, 2048.0, AL.mult)
+    lin(col("g5"), col("g3"), -1.0, col("g4"))
+    lin(M("Gm"), M("pA"), OH(7))
+    lin(col("g7"), OH(7), -BIG / 2)
+    lin(col("g8"), OH(8), BIG / 2, col("g7"))
+    lin(Ms("Gm", 14), Ms("ON", 14), col("g7"))
+    lin(Ms("Gm", 15), Ms("ON", 15), col("g8"))
     ts(V("wm", 0, 1), V("wti", 0, 1), W - 1, AL.bitwise_and)
-    ts(V("wc", 0, 1), V("wm", 0, 1), 0.125, AL.mult)
-    ts(M("Mw"), sel("Wh", 15), V("wc", 0, 1), AL.mult)
+    cp(V("wc", 0, 1), V("wm", 0, 1))
+    ts(M("pMw"), sel("Wd", 15), V("wc", 0, 1), AL.mult)
+    ts(M("nMw"), M("pMw"), -1.0, AL.mult)
+    ts(col("n1"), col("lo12"), col("lo8"), AL.subtract, col("lo8"), AL.subtract)
+    lin(col("nb"), OH(12), 4.0, col("n1"))
+    ts(col("nb0"), col("nb"), col("lo8"), AL.add, OH(13), AL.subtract)
+    lin(col("nb15"), OH(15), 1.0, col("nb"))
+    lin(M("pNB"), M("ON"), col("nb"))
+    lin(M("nNB"), M("nON"), col("nb"))
+    lin(Ms("pNB", 0), Ms("ON", 0), col("nb0"))
+    lin(Ms("pNB", 15), Ms("ON", 15), col("nb15"))
+    lin(col("wa"), OH(14), 1.0, col("lo8"))
+    lin(col("wb"), OH(14), 2.0, col("n1"))
+    lin(V("WA", 0, 143), V("Wd", 1, 144), col("wa"))
+    lin(V("WA", 15, 143, 16), V("Wd", 15, 143, 16), col("wb"))
+    lin(col("oc"), col("odd"), 10240.0, 2047.0)
+    lin(col("p1"), col("p"), 1.0, 1.0)
+    lin(col("p2"), col("p"), 1.0, 129.0)
+    lin(V("cix", 0, 128), E0, 1.0, col("p1"))
+    lin(V("cix", 128, 256), E0, 1.0, col("p2"))
+    lin(M("D14"), M("I"), OH(14))
     ts(col("d1"), MK(4), MK(8), AL.add, MK(12), AL.add)
-    ts(col("d2"), col("d1"), -4.0, AL.mult, 8.0, AL.add)
+    lin(col("d2"), col("d1"), -4.0, 8.0)
     ts(M("Mpr"), M("E"), col("d2"), AL.is_equal)
-    ts(col("d3"), MK(8), -8.0, AL.mult)
+    lin(col("d3"), MK(8), -8.0)
     ts(M("Mdi"), M("E"), col("d3"), AL.is_equal)
     ts(V("owe", 0, 128), V("owni", 0, 128), 1.0, AL.add, col("lo8"), AL.mult)
     ts(V("owo", 0, 128), V("owni", 0, 128), 1.0, AL.add, MK(8), AL.mult)
-    ts(col("o1"), MK(12), MK(8), AL.subtract, OH(12), AL.add)
-    ts(col("o2"), col("o1"), 2048.0, AL.mult)
+    ts(col("o5"), MK(12), MK(8), AL.subtract, 2048.0, AL.mult)
     mm(V("ps1", 128, 256), [(M("Mpr"), V("owe", 0, 128)), (M("Mdi"), V("owe", 0, 128)), (M("D14"), V("cix", 0, C, 2))])
     mm(V("ps1", 256, 384), [(M("Mpr"), V("owo", 0, 128)), (M("Mdi"), V("owo", 0, 128)), (M("D14"), V("cix", 1, C, 2))])
-    ts(V("OwnT", 0, C, 2), V("ps1", 128, 256), col("o2"), AL.add)
-    ts(V("OwnT", 1, C, 2), V("ps1", 256, 384), col("o2"), AL.add)
-    cp(V("thb", 0, NV, 1, (0, 8)), V("thri", 0, NV, 1, (0, 8)))
-    mm(V("ps1", 0, NV), [(V("Eg", 0, 128, 1, (0, 8)), V("thb", 0, NV, 1, (0, 8)))])
-    ts(V("thc", 0, NV), V("ps1", 0, NV), -1.0, AL.mult, 0.5, AL.add)
+    ts(V("OwnT", 0, C, 2), V("ps1", 128, 256), col("o5"), AL.add)
+    ts(V("OwnT", 1, C, 2), V("ps1", 256, 384), col("o5"), AL.add)
+    cp(V("thb", 0, NV, 1, top8), V("thri", 0, NV, 1, top8))
+    mm(V("ps1", 0, NV), [(V("Eg", 0, 128, 1, top8), V("thb", 0, NV, 1, top8))])
+    lin(V("thc", 0, NV), V("ps1", 0, NV), -1.0, 0.5)
     cp(V("nm", 0, C), V("nami", 0, C))
     ts(V("ta", 0, C), V("mrki", 0, C), -2.0, AL.mult, 1.0, AL.add)
     ts(V("tb", 0, C), V("nami", 0, C), 1.0, AL.add)
-    tt(V("Z", 0, C), V("ta", 0, C), V("tb", 0, C), AL.mult)
-    ts(V("Tp", 0, C), V("picb", 0, C), 1.0 / 256, AL.mult)
-    ms(V("S", 0, C), 0.0)
-    ms(V("y", W, WIN), 0.0)
+    tt(V("Zi", 0, C), V("ta", 0, C), V("tb", 0, C), AL.mult)
+    for ci in range(NB):
+        lin(state("Ti", 0, ci, 1), V("one", 0, BN), col("f0"))
     for b in range(4):
         lo, hi, pb = 512 * b, 512 * b + 512, V("ps%d" % (4 + b), 0, 512)
         ts(V("z0", lo, hi), V("x0", lo, hi), 0.0, AL.is_equal)
-        mm(pb, [(M("Is"), V("x0", lo, hi)), (M("nI"), V("z0", lo, hi))])
-        if b == 3:
+        mm(pb, [(M("I"), V("x0", lo, hi)), (M("nOm"), V("z0", lo, hi))])
+        if b % 2:
             cp(V("y", lo, hi), pb)
         else:
             act(V("y", lo, hi), pb, AF.Identity)
 
-    reg = regions()
-    c0s = [sum(CHUNKS[:i]) for i in range(NCH)]
-
-    def span(ci):
-        grp = [x for x in SGROUPS if ci in x][0]
-        return c0s[grp[0]], c0s[grp[-1]] + CHUNKS[grp[-1]]
-
-    def send(kind, v, ci, pairs):
+    def send(kind, v, ci, a, b):
         sem = "r%s%d_%d" % (kind, v + 1, ci)
-        i = add("g", SENDC, [a for a, b in pairs], [], pairs, "send", sem)
-        add("n", 0, [], [b for a, b in pairs], None, "recv", sem, i)
+        i = add("g", SENDC, [a], [], (a, b), "send", sem)
+        add("n", 0, [], [b], None, "recv", sem, i)
 
-    def passes(ci, src, dst, opnd, op, bank, extra):
-        n, c0 = CHUNKS[ci], c0s[ci]
-        cnt, whole = V(bank, 0, n), V(bank, 0, 512)
-        if nel(opnd) < n or NCH > 2:
-            return passes1(ci, src, dst, V(opnd[0], opnd[1], opnd[2]), op, cnt, whole, extra)
-        ks = list(range(1, 9))
-        for i, w in ((0, 3), (3, 2), (5, 2), (7, 1)):
-            terms = list(extra) if i == 3 else []
-            for k in ks[i:i + w]:
-                lo = 16 * c0 + 2 * (k - 1) * n
-                if k < 8 and opnd[3] == 2:
-                    for j in range(2):
-                        o = V(dst, lo + j * n, lo + (j + 1) * n)
-                        tt(o, V(src, 16 * c0 + k + 8 * j, 16 * (c0 + n), 16), opnd, op)
-                        terms.append((sel("Wd", k + 8 * j), o))
-                elif k < 8:
-                    tt(V(dst, lo, lo + 2 * n), V(src, 16 * c0 + k, 16 * (c0 + n), 8), opnd, op)
-                    terms += [(sel("Wd", k), V(dst, lo, lo + 2 * n, 2)), (sel("Wd", k + 8), V(dst, lo + 1, lo + 2 * n, 2))]
-                else:
-                    tt(V(dst, lo, lo + n), V(src, 16 * c0 + k, 16 * (c0 + n), 16), V(opnd[0], opnd[1], opnd[2], 2), op)
-                    terms.append((sel("Wd", k), V(dst, lo, lo + n)))
-            mm(cnt, terms, i == 0, i == 7, whole)
+    def passes(ci, src, dst, opnd, op, bank, head, late):
+        c0, g0 = ci * BN, ci * GW + 16
+        cnt, whole = V(bank, 0, BN), V(bank, 0, 512)
+        for i in range(0, len(head), HSUB):
+            mm(cnt, head[i:i + HSUB], i == 0, False, whole if i == 0 else None)
+        i = 1
+        for x, w in enumerate(BATCH):
+            rows = [(V(dst, 16 * c0 + k * BN, 16 * c0 + (k + 1) * BN), V(src, g0 + k, g0 + 16 * BN, 16)) for k in range(i, i + w)]
+            compare(rows, opnd, op)
+            opens = i == 1 and not head
+            mm(cnt, (list(late) if x == 1 else []) + [(sel("Wd", i + k), rows[k][0]) for k in range(w)], opens, i + w == 16,
+               whole if opens else None)
+            i += w
         return cnt
 
-    def passes1(ci, src, dst, opnd, op, cnt, whole, extra):
-        n, c0 = CHUNKS[ci], c0s[ci]
-        for i, w in ((1, 7), (8, 6), (14, 2)):
-            terms = list(extra) if i == 8 else []
-            for k in range(i, i + w):
-                o = V(dst, 16 * c0 + k * n, 16 * c0 + (k + 1) * n)
-                tt(o, V(src, 16 * c0 + k, 16 * (c0 + n), 16), opnd, op)
-                terms.append((sel("Wd", k), o))
-            mm(cnt, terms, i == 1, i == 14, whole)
-        return cnt
-
-    def twice(out, src, func):
-        if NCH > 2:
-            return act(out, src, func)
-        for j in range(2 if out[3] == 1 else 1):
-            act(V(out[0], out[1] + j, out[2], 2), src, func)
-
+    one = V("one", 0, BN)
     for v in range(NV):
         last = v == NV - 1
-        for ci in range(NCH):
-            n, c0, R = CHUNKS[ci], c0s[ci], reg[ci]
-            t = lambda k: V(k, c0, c0 + n)
-            st = lambda k: V(k, v * C + c0, v * C + c0 + n)
-            tag[0] = (v, "g%d" % ci)
-            for a in range(c0, c0 + n, GSUB):
-                b = min(a + GSUB, c0 + n)
-                gather(V("G", 16 * a, 16 * b), V("nm", v * C + a, v * C + b), vec=a in (VG if v else VG0))
-            P = V("G", 16 * c0, 16 * (c0 + n), 16)
-            tag[0] = (v, "c%d" % ci)
-            twice(R["P2"], P, AF.Abs)
-            cnt = passes(ci, "G", "c1", R["P2"], AL.is_gt, "ps0", [(M("Mpar"), st("S"))] if v else [])
-            tag[0] = (v, "h%d" % ci)
+        floor = 0.0 if last else -OM
+        for ci in range(NB):
+            c0, g0, R = ci * BN, ci * GW + 16, regions(ci)
+            t = lambda k: V(k, c0, c0 + BN)
+            Z = V("Zi", v * C + c0, v * C + c0 + BN)
+            Tp, th, Tn, thn = [state(b, v, ci, j) for b in ("Ti", "To") for j in range(2)]
+            tag[0] = (v, "g", ci)
+            for a in range(0, BN, GSUB):
+                gather(V("G", g0 + 16 * a, g0 + 16 * (a + GSUB)), V("nm", v * C + c0 + a, v * C + c0 + a + GSUB),
+                       vec=c0 + a in (VG if v else VG0))
+            P = V("G", g0, g0 + 16 * BN, 16)
+            tag[0] = (v, "c", ci)
+            act(R["Pa"], P, AF.Abs)
+            cnt = passes(ci, "G", "c1", R["Pa"], AL.is_gt, "ps%d" % CNT["c"][ci], [], [(M("Mpar"), th)] if v else [])
+            if not PV:
+                mm(R["P"], [(M("I"), P)])
+            tag[0] = (v, "h", ci)
             act(t("cl"), cnt, AF.Sign, V("thc", v, v + 1))
             mm(R["R"], [(M("Mr"), t("cl"))])
             act(t("isk"), R["R"], AF.Relu, col("isk"))
-            zt = V(R["ZT"][0], R["ZT"][1], R["ZT"][1] + n // NB)
-            mm(zt, [(M("I"), V("a128", 0, n // NB))]
-               + [(V("WS", 16 - DUP * (b + 1), 144 - DUP * (b + 1)), V("isk", c0 + b, c0 + n, NB)) for b in range(NB)])
-            ok = V("offk", 32 * ci, 32 * ci + n // NB)
+            zt = V(R["zt"][0], R["zt"][1], R["zt"][1] + 8)
+            mm(zt, [(M("I"), V("a128", 0, 8))] + [(sel2("WS", b), V("isk", c0 + b, c0 + BN, 8)) for b in range(8)])
+            ok = V("offk", 8 * ci, 8 * ci + 8)
             ts(ok, zt, col("s16"), AL.add)
-            gather(V("xk", DUP * c0, DUP * (c0 + n)), ok, V("G", 16 * c0, 16 * (c0 + n)))
-            xk = V("xk", DUP * c0, DUP * (c0 + n), DUP)
-            if MKP:
+            gather(V("xx", 2 * c0, 2 * (c0 + BN)), ok, V("G", g0 - 16, g0 + 16 * BN))
+            xk, Pe = V("xx", 2 * c0, 2 * (c0 + BN), 2), V("xx", 2 * c0 + 1, 2 * (c0 + BN), 2)
+            tt(t("m"), xk, P if PV else R["P"], AL.is_gt)
+            mm(R["B"], [(M("Ie"), xk), (M("Iem"), t("m"))])
+            tag[0] = (v, "o", ci)
+            if not MKV:
                 mm(R["mk"], [(M("I"), t("isk"))])
-                tt(t("Zk"), st("Z"), R["mk"], AL.mult)
-            else:
-                tt(t("Zk"), st("Z"), t("isk"), AL.mult)
-            mm(R["Zsum"], [(M("ONh"), t("Zk"))])
-            act(t("nc"), R["Zsum"], AF.Sign, col("ncb"))
-            mm(R["Tab"], [(M("Ih"), t("OwnT")), (sel("Wh", 13), t("Zk"))])
-            tag[0] = (v, "o%d" % ci)
-            mm(R["ma"], [(M("GT"), t("isk"))])
-            mm(R["ms"], [(M("B2"), t("isk"))])
-            tt(t("Za"), st("Z"), R["ma"], AL.mult)
-            tt(t("Zs"), st("Z"), R["ms"], AL.mult)
-            if UV >= 1:
-                tt(R["nU"], R["ms"], P, AL.subtract)
-            else:
-                mm(R["nU"], [(M("nI"), P), (M("B2"), t("isk"))])
-            if UV >= 2:
-                tt(R["U"], P, R["ms"], AL.subtract)
-            else:
-                mm(R["U"], [(M("I"), P), (M("nB2"), t("isk"))])
-            tt(t("t1"), st("Tp"), R["nU"], AL.min)
-            tt(st("Tpo"), t("t1"), R["U"], AL.max)
-            mm(R["Sp"], [(M("I"), st("S")), (M("Msg"), t("nc"))])
-            act(t("oct") if last else st("So"), R["Sp"], AF.Abs, col("nsg"))
-            if not last:
-                for grp in BGROUPS:
-                    if grp[-1] == ci:
-                        bv = lambda k, u: V(k, u * C + c0s[grp[0]], u * C + c0 + n)
-                        send("b", v, ci, [(bv("Tpo", v), bv("Tp", v + 1)), (bv("So", v), bv("S", v + 1))])
-            else:
-                ts(t("opc"), st("Tpo"), 256.0, AL.mult)
-            tag[0] = (v, "f%d" % ci)
-            mm(R["D"], [(M("nI"), P), (M("N2"), t("nc")), (M("I"), xk)])
-            act(R["Wp"], R["D"], AF.Sign, 2.0 - 1.0 / 512)
-            Fv, Bv = V("FB", 2 * c0, 2 * (c0 + n), 2), V("FB", 2 * c0 + 1, 2 * (c0 + n), 2)
-            if BV:
-                act(R["nW"], R["D"], AF.Sign, 1.0 / 512 - 2.0, -1.0)
-                tt(R["Bp"], xk, R["nW"], AL.min)
-            tt(Fv, xk, R["Wp"], AL.min)
-            if not BV:
-                mm(R["Bp"], [(M("I"), xk), (M("nI"), V("one", 0, n)), (M("nI"), Fv)])
-            if PAIR[1]:
-                twice(R["B2"], R["Bp"], AF.Identity)
-            act(Bv, R["Bp"], AF.Identity)
-            tag[0] = (v, "m%d" % ci)
-            mm(R["u"], [(M("Mw"), st("Tpo")), (M("Msm"), t("isk")), (M("Mnc"), t("nc")), (M("Mx"), xk)])
-            ts(t("q"), R["u"], col("bq"), AL.add)
-            tt(t("A1"), t("q"), R["u"], AL.is_equal)
-            tt(t("pr"), t("A1"), R["Tab"], AL.mult)
-            tag[0] = (v, "l%d" % ci)
-            tt(t("J"), R["u"], t("q"), AL.subtract)
-            tag[0] = (v, "b%d" % ci)
-            for a in range(c0, c0 + n, ASUB):
-                b = min(a + ASUB, c0 + n)
-                act(V("Gp", 16 * a, 16 * b), V("G", 16 * a, 16 * b), AF.Abs)
+            tt(t("Zk"), Z, t("isk") if MKV else R["mk"], AL.mult)
+            mm(R["th"], [(M("Mth"), th), (M("nON"), t("Zk"))])
+            act(thn, R["th"], AF.Sign, col("thb"))
+            tag[0] = (v, "m", ci)
+            mm(R["Tn"], [(M("I"), Tp), (M("Tc"), th), (M("It"), Pe)])
+            tt(Tn, Pe, R["Tn"], AL.max)
+            mm(R["pr"], [(M("Doff"), one), (M("pA"), xk), (M("nMw"), Tn), (M("pR"), one), (M("nR"), one),
+                         (M("nA"), xk), (M("pMw"), Tn), (M("I"), t("OwnT")), (sel("Wd", 13), t("Zk")), (M("Gm"), thn)])
+            ts(t("pr"), R["pr"], col("g3"), AL.max, col("g5"), AL.add)
+            tag[0] = (v, "f", ci)
+            mm(R["F"], [(M("I"), xk), (M("p2Om"), t("m"))])
+            ts(V("FB", 2 * c0, 2 * (c0 + BN), 2), R["F"], -2 * OM, AL.add, floor, AL.max)
+            act(V("FB", 2 * c0 + 1, 2 * (c0 + BN), 2), R["B"], AF.Relu if last else AF.Identity, 0.0, 1.0 / (1 - ETA))
+            tag[0] = (v, "b", ci)
+            for a in range(g0, g0 + 16 * BN, ASUB) if ci in ABSB else []:
+                act(V("Gp", a, a + ASUB), V("G", a, a + ASUB), AF.Abs)
+            tag[0] = (v, "m", ci)
+            for grp in BGROUPS:
+                if grp[-1] == ci:
+                    lo, n = 2 * (v * C + grp[0] * BN), BN * len(grp)
+                    if last:
+                        store(lambda T, a=grp[0] * BN, n=n: T.ypic[:, a:a + n], V("To", lo, lo + n))
+                    else:
+                        send("b", v, ci, V("To", lo, lo + 2 * n), V("Ti", lo + 2 * C, lo + 2 * C + 2 * n))
+            if last:
+                tag[0] = (v, "l", ci)
+                A = V(R["A"][0], R["A"][1], R["A"][2], 1, top8)
+                mm(A, [(V("Mc", 0, 8), thn)])
+                act(V("oct", c0, c0 + BN, 1, top8), A, AF.Identity, 3.0)
+                ts(V("yo", 512 * ci, 512 * ci + 512), V("y", 512 * ci, 512 * ci + 512), 0.0, AL.max)
         for grp in SGROUPS:
-            tag[0] = (v, "s%d" % grp[-1])
-            g0, g1 = span(grp[0])
-            oT = reg[grp[-1]]["oT"]
-            oa = V(oT[0], oT[1], oT[1] + (g1 - g0) // 8)
-            mm(oa, [(M("I"), V("a8", g0 // 8, g1 // 8))] + [(sel2("WA", b), V("pr", g0 + b, g1, 8)) for b in range(8)])
-            off = V("offs", g0 // 8, g1 // 8)
+            tag[0] = (v, "s", grp[-1])
+            lo, hi = grp[0] * BN, grp[-1] * BN + BN
+            oT = regions(grp[-1])["oa"]
+            oa = V(oT[0], oT[1], oT[1] + (hi - lo) // 8)
+            mm(oa, [(sel2("WA", b), V("pr", lo + b, hi, 8)) for b in range(8)])
+            off = V("offs", lo // 8, hi // 8)
             ts(off, oa, col("oc"), AL.add)
-            win, fb = V("y", 0, WIN), V("FB", 2 * g0, 2 * g1)
+            win, fb = V("yo" if last else "y", 0, WIN), V("FB", 2 * lo, 2 * hi)
             add("v", 60 + SCAT * nel(fb), [off, fb], [win],
                 lambda g, T, win=win, off=off, fb=fb: g.vector.tensor_copy(ap(T, win).indirect(ap(T, off)), ap(T, fb)), ck="sc")
         if last:
-            for b in range(4):
-                lo, hi = 512 * b, 512 * b + 512
-                if b % 2:
-                    ts(V("yo", lo, hi), V("y", lo, hi), 0.0, AL.max, 256.0, AL.mult)
-                else:
-                    act(V("yo", lo, hi), V("y", lo, hi), AF.Relu, 0.0, 256.0)
             store(lambda T: T.ydep[:], V("yo", 0, W))
-            store(lambda T: T.ypic[:], V("opc", 0, C))
-            for gi in range(8):
-                store(lambda T, gi=gi: T.ycut[gi:gi + 1, :], V("oct", 0, C, 1, (16 * gi + 1, 16 * gi + 2)))
-        for ci in range(NCH):
-            n, c0, R = CHUNKS[ci], c0s[ci], reg[ci]
-            t = lambda k: V(k, c0, c0 + n)
-            st = lambda k: V(k, v * C + c0, v * C + c0 + n)
-            base = [(M("Sm"), st("Z")), (M("ISm"), t("Zs")), (M("SI"), t("Za")), (M("IR"), t("Zk"))]
-            tag[0] = (v, "l%d" % ci)
-            mm(R["L1"], base + [(M("Pm2"), t("pr"))])
-            if LV:
-                act(t("L1s"), R["L1"], AF.Identity)
-            tag[0] = (v, "e%d" % ci)
-            cnt = passes(ci, "Gp", "c2", R["B2"], AL.is_lt, "ps1", [])
-            tag[0] = (v, "t%d" % ci)
-            act(t("e"), cnt, AF.Sign, -1.5)
+            store(lambda T: T.ycut[:], V("oct", 0, C, 1, top8))
+        for ci in range(NB):
+            c0, g0, R = ci * BN, ci * GW + 16, regions(ci)
+            t = lambda k: V(k, c0, c0 + BN)
+            Z, thn = V("Zi", v * C + c0, v * C + c0 + BN), state("To", v, ci, 1)
+            tag[0] = (v, "l", ci)
+            mm(R["L1"], [(M("SmI"), Z), (M("pKON"), t("isk")), (M("nKON"), t("isk")), (M("ISd"), Z), (M("pKGE"), t("isk")),
+                         (M("nKGE"), t("isk")), (M("Sd"), Z)])
+            cp(t("L1"), R["L1"])
+            tag[0] = (v, "e", ci)
+            head = [] if ci in ABSB else [(sel("W18", k), V("G", g0 + k, g0 + 16 * BN, 16)) for k in range(1, 16)]
+            cnt = passes(ci, "Gp" if ci in ABSB else "G", "c2", R["B"], AL.is_lt, "ps%d" % CNT["e"][ci], head, [(M("Gc"), thn)])
+            tag[0] = (v, "t", ci)
+            act(t("e"), cnt, AF.Sign, -17.5)
             mm(R["val"], [(M("LT"), t("isk")), (M("Mv"), t("e"))])
-            ts(t("X"), R["val"], col("x"), AL.is_ge)
-            tt(t("Q"), t("X"), R["L1"], AL.mult)
-            nx = lambda k: V(k, (v + 1) * C + c0, (v + 1) * C + c0 + n)
-            one = ONE and not last
-            if LV:
-                nz = st("nz")
-                mm(R["new"], [(M("NBm"), t("pr")), (M("M15"), t("J")), (M("SI4"), t("Q"))])
-                tt(nz, t("L1s"), R["new"], AL.add)
-            else:
-                nz = R["new"]
-                mm(nz, base + [(M("Pm"), t("pr")), (M("M15"), t("J")), (M("SI4"), t("Q"))])
-                if one:
-                    act(st("nz"), nz, AF.Identity)
-            if one:
-                send("a", v, ci, [(st("nz"), nx("Zf"))])
-                tag[0] = (v + 1, "r%d" % ci)
-                act(t("aZ"), nx("Zf"), AF.Abs)
-                ts(nx("nm"), t("aZ"), -1.0, AL.add)
-                cp(nx("Z"), nx("Zf"))
-                continue
+            act(t("X"), R["val"], AF.Relu, col("x"))
+            nz = R["new"]
+            mm(nz, [(M("I"), t("L1")), (M("nNB"), t("pr")), (M("pK"), t("X")), (M("nK"), t("X")), (M("pNB"), t("pr")),
+                    (M("nSd"), t("L1")), (M("pKS"), t("X")), (M("nKS"), t("X")), (M("Sd"), t("L1"))])
             act(t("aZ"), nz, AF.Abs)
             if not last:
-                ts(st("nmo"), t("aZ"), -1.0, AL.add)
-                send("a", v, ci, [(st("nmo"), nx("nm"))])
-                cp(st("Zo"), nz)
-                send("z", v, ci, [(st("Zo"), nx("Z"))])
+                lo = v * C + c0
+                ts(V("nmo", lo, lo + BN), t("aZ"), -1.0, AL.add)
+                send("a", v, ci, V("nmo", lo, lo + BN), V("nm", lo + C, lo + C + BN))
+                cp(V("Zo", lo, lo + BN), nz)
+                for grp in ZGROUPS:
+                    if grp[-1] == ci:
+                        lo, hi = v * C + grp[0] * BN, v * C + c0 + BN
+                        send("z", v, ci, V("Zo", lo, hi), V("Zi", lo + C, hi + C))
             else:
-                ts(t("onm"), t("aZ"), -1.0, AL.add)
+                act(t("onm"), t("aZ"), AF.Identity, -1.0)
                 ts(t("omk"), nz, 0.0, AL.is_lt)
-                store(lambda T, c0=c0, n=n: T.ynam[:, c0:c0 + n], t("onm"))
-                store(lambda T, c0=c0, n=n: T.ymrk[:, c0:c0 + n], t("omk"))
+                store(lambda T, c0=c0: T.ynam[:, c0:c0 + BN], t("onm"))
+                store(lambda T, c0=c0: T.ymrk[:, c0:c0 + BN], t("omk"))
     return ops
 
 
@@ -589,13 +488,13 @@ def plan():
         if o["after"] is not None:
             deps[i].add(o["after"])
         for x, wr in [(x, False) for x in o["r"]] + [(x, True) for x in o["w"]]:
-            for (lo, hi, j, w2) in hist.get(x[0], []):
-                if j != i and (wr or w2) and lo < x[2] and x[1] < hi:
+            for (lo, hi, j, w2, st) in hist.get(x[0], []):
+                if j != i and (wr or w2) and lo < x[2] and x[1] < hi and not (st == x[3] > 1 and (lo - x[1]) % st):
                     deps[i].add(j)
         for x in o["w"]:
             hist[x[0]] = [h for h in hist.get(x[0], []) if not (x[1] <= h[0] and h[1] <= x[2] and x[3] == 1 and x[4] is None)]
         for x, wr in [(x, False) for x in o["r"]] + [(x, True) for x in o["w"]]:
-            hist.setdefault(x[0], []).append((x[1], x[2], i, wr))
+            hist.setdefault(x[0], []).append((x[1], x[2], i, wr, x[3]))
     extra = [DMAL if o["kind"] == "dma" else COMM if o["kind"] == "send" else LAT for o in ops]
     succ = [[] for _ in range(n)]
     for i in range(n):
@@ -605,115 +504,172 @@ def plan():
     eng = [o["e"] for o in ops]
     banks = [sorted(set(x[0] for x in o["r"] + o["w"] if x[0] not in SB)) for o in ops]
     pred = [sorted(d) for d in deps]
+    hard = [[j for j in pred[i] if not (ops[i]["cont"] and eng[j] == "p")] for i in range(n)]
+    table = [([cost[i] * m.get(ops[i]["ck"], 1.0) for i in range(n)], [extra[i] * m.get("x" + ops[i]["kind"], 1.0) for i in range(n)])
+             for m in MODELS + CHECK]
+    nm = len(MODELS)
 
-    def place(key, back):
-        before = succ if back else pred
-        start = [0.0] * n
-        lines = {}
-        for i in sorted(range(n), key=lambda i: (key[i], -i if back else i)):
-            t0 = 0.0
-            for j in before[i]:
-                a, b = (i, j) if back else (j, i)
-                t0 = max(t0, start[j] + cost[j] + (0.0 if ops[b]["cont"] and eng[a] == "p" else extra[a]))
-            if back and not before[i]:
-                t0 = extra[i]
-            e, c = eng[i], cost[i]
-            if e != "n":
-                res = [(lines.setdefault(e, ([], [])), 0.0)] + [(lines.setdefault(b, ([], [])), LAT) for b in banks[i]]
-                moved = True
-                while moved:
-                    moved = False
-                    for (ss, jj), gap in res:
-                        x = max(0, find(ss, t0) - (1 if gap == 0.0 else 4))
-                        while x < len(ss) and ss[x] < t0 + c + gap:
-                            j = jj[x]
-                            if (gap == 0.0 or eng[j] != e) and ss[x] + cost[j] + gap > t0:
-                                t0 = ss[x] + cost[j] + gap
-                                moved = True
-                            x += 1
-                for (ss, jj), gap in res:
-                    x = find(ss, t0)
-                    ss.insert(x, t0)
-                    jj.insert(x, i)
-            start[i] = t0
-        end = max(start[i] + cost[i] + (0.0 if back else extra[i]) for i in range(n))
-        return start, end
-
-    def find(ss, t0):
-        lo, hi = 0, len(ss)
-        while lo < hi:
-            m = (lo + hi) // 2
-            if ss[m] <= t0:
-                lo = m + 1
-            else:
-                hi = m
-        return lo
-
-    def finish(start):
-        order = sorted(range(n), key=lambda i: (start[i], i))
-        dp = [set(d) for d in deps]
-        lastuse = {}
+    def walk(order, mi):
+        cs, ex = table[mi]
+        end, fin, par = [0.0] * n, [0.0] * n, [None] * n
+        last, use = {}, {}
         for i in order:
+            e = eng[i]
+            j = last.get(e)
+            t0, pj = (end[j], (j, True)) if j is not None else (0.0, None)
+            for j in hard[i]:
+                if fin[j] > t0:
+                    t0, pj = fin[j], (j, False)
             for b in banks[i]:
-                for e2, j in lastuse.get(b, {}).items():
-                    if e2 != eng[i]:
-                        dp[i].add(j)
-                lastuse.setdefault(b, {})[eng[i]] = i
-        return order, dp
+                u = use.setdefault(b, {})
+                for e2, j in u.items():
+                    if e2 != e and fin[j] > t0:
+                        t0, pj = fin[j], (j, True)
+                u[e] = i
+            if e != "n":
+                last[e] = i
+            end[i] = t0 + cs[i]
+            fin[i] = end[i] + ex[i]
+            par[i] = pj
+        return end, fin, par
 
-    def replay(order, dp, m):
-        fin = [0.0] * n
-        free = {}
-        for i in order:
-            o = ops[i]
-            t0 = max([free.get(eng[i], 0.0)] + [fin[j] for j in dp[i] if not (o["cont"] and eng[j] == "p")])
-            t1 = t0 + cost[i] * m.get(o["ck"], 1.0)
-            if eng[i] != "n":
-                free[eng[i]] = t1
-            fin[i] = t1 + extra[i] * m.get("x" + o["kind"], 1.0)
-        return max(fin)
+    def chain(w):
+        fin, par = w[1:]
+        i = max(range(n), key=lambda i: fin[i])
+        arcs = []
+        while par[i] is not None:
+            if par[i][1]:
+                arcs.append((par[i][0], i))
+            i = par[i][0]
+        return arcs
 
-    rng = np.random.default_rng(SEED)
-    tail = [0.0] * n
-    for i in range(n - 1, -1, -1):
-        tail[i] = cost[i] + extra[i] + max([tail[j] for j in succ[i]] + [0.0])
-    top = max(tail)
-    rel, run = [], {}
+    twin, seen = {}, {}
     for i in range(n):
         tg = ops[i]["tag"]
-        rel.append(run.get(tg, 0.0))
-        run[tg] = rel[i] + 0.6 * cost[i]
+        if tg is not None:
+            seen[tg] = seen.get(tg, 0) + 1
+            twin[tg + (seen[tg],)] = i
+            ops[i]["id"] = tg + (seen[tg],)
 
-    def keys(off):
-        key = [0.0] * n
+    def greedy(prio):
+        cs, ex = table[0]
+        left = [len(d) for d in pred]
+        at = [0.0] * n
+        ready = {e: [] for e in "vapgsn"}
+        free = {e: 0.0 for e in ready}
+        use = {"ps%d" % b: {} for b in range(8)}
+        order = []
+        for i in range(n):
+            if not left[i]:
+                ready[eng[i]].append(i)
+
+        def est(i, e):
+            t0 = max(at[i], free[e])
+            for b in banks[i]:
+                for e2, t in use[b].items():
+                    if e2 != e and t > t0:
+                        t0 = t
+            return t0
+        known, stale = {}, set(ready)
+        while len(order) < n:
+            for e in stale:
+                c = [(est(i, e), i) for i in ready[e]]
+                known[e] = (min([t + cs[i] for t, i in c], default=1e18), e, c)
+            low, e, pick = min(known.values())
+            t, i = max([x for x in pick if x[0] <= low], key=lambda x: prio[x[1]])
+            stale = {e, "v", "a", "p"} if banks[i] else {e}
+            ready[e].remove(i)
+            order.append(i)
+            if e != "n":
+                free[e] = t + cs[i]
+            fin = t + cs[i] + ex[i]
+            for b in banks[i]:
+                use[b][e] = fin
+            for j in succ[i]:
+                at[j] = max(at[j], t + cs[i] if ops[j]["cont"] and e == "p" else fin)
+                left[j] -= 1
+                if not left[j]:
+                    ready[eng[j]].append(j)
+                    stale.add(eng[j])
+        return order
+
+    def squeak(tries, rng):
+        tail = [0.0] * n
         for i in range(n - 1, -1, -1):
-            tg = ops[i]["tag"]
-            if tg is None:
-                key[i] = min([key[j] - cost[i] - extra[i] for j in succ[i]] + [1e9])
-            else:
-                key[i] = tg[0] * off["T"] + off.get(tg[1], -9000) + rel[i] + off.get(tg[1] + ("a" if tg[0] == 0 else "z" if tg[0] == NV - 1 else "m"), 0)
-        for i in range(n):
-            key[i] = max([key[i]] + [key[j] + 1e-3 for j in pred[i]])
-        return key
-    if SEARCH:
-        DB[:] = [[cost[i] + extra[i] for i in range(n)], cost, sorted(set(o["tag"][1] + x for o in ops if o["tag"] for x in "az"))]
-        return SEARCH[0](keys, place, finish, replay)
-    best = None
-    key = keys(OFFS)
-    for it in range(ROUNDS):
-        start, end = place(key, False)
-        order, dp = finish(start)
-        score = [replay(order, dp, m) for m in MODELS]
-        if best is None or sum(score) < best[0]:
-            best = (sum(score), start, order, dp, score)
-        src = best[1] if it % 4 == 3 else start
-        rs, end = place([-(src[i] + cost[i] + extra[i]) for i in range(n)], True)
-        key = [-(rs[i] + cost[i]) for i in range(n)]
-        noise = NOISE * rng.random(n)
-        for i in range(n):
-            key[i] = max([key[i] + float(noise[i])] + [key[j] + 1e-3 for j in pred[i]])
-    start, order, deps = best[1], best[2], best[3]
-    done = [start[i] + cost[i] + extra[i] for i in range(n)]
+            tail[i] = cost[i] + extra[i] + max([tail[j] for j in succ[i]] + [0.0])
+        name = [ops[i]["id"][1:] if "id" in ops[i] else i for i in range(n)]
+        cur, best, adj, prio = None, None, {}, tail
+        for it in range(tries):
+            new = dict(adj)
+            if cur is not None:
+                arcs = chain(cur[1][it % nm])
+                for x in range(int(rng.integers(1, 4))):
+                    a, b = arcs[int(rng.integers(len(arcs)))]
+                    d = max(0.0, prio[a] - prio[b]) + BUMP * rng.random()
+                    if rng.random() < 0.5:
+                        new[name[a]] = new.get(name[a], 0.0) - d
+                    else:
+                        new[name[b]] = new.get(name[b], 0.0) + d
+            p2 = [tail[i] + new.get(name[i], 0.0) for i in range(n)]
+            order = greedy(p2)
+            w = [walk(order, mi) for mi in range(nm)]
+            val = sum(max(x[1]) for x in w) / nm
+            if cur is None or val < cur[0] - HEAT * (1.0 - it / tries) * float(np.log(rng.random())):
+                cur, adj, prio = (val, w), new, p2
+                if best is None or val < best[0]:
+                    best = (val, order)
+        return best[1]
+
+    def shift(order, a, b, up):
+        lo, hi = order.index(a), order.index(b)
+        if lo >= hi:
+            return None
+        seg = order[lo:hi + 1]
+        take = {b if up else a}
+        for i in (reversed(seg) if up else seg):
+            if i in take or any(j in take for j in (succ[i] if up else pred[i])):
+                take.add(i)
+        if (a if up else b) in take:
+            return None
+        x, y = [i for i in seg if i in take], [i for i in seg if i not in take]
+        return order[:lo] + (x + y if up else y + x) + order[hi + 1:]
+
+    def polish(order, moves, rng):
+        cur = [walk(order, mi) for mi in range(nm)]
+        val = sum(max(w[1]) for w in cur) / nm
+        best = (val, order)
+        for it in range(moves):
+            arcs = chain(cur[it % nm])
+            a, b = arcs[int(rng.integers(len(arcs)))]
+            up, alone = rng.random() < 0.5, rng.random() < 0.15
+            pairs = [(a, b)]
+            if not alone and "id" in ops[a] and "id" in ops[b]:
+                ia, ib = ops[a]["id"], ops[b]["id"]
+                pairs = [(twin.get((ia[0] + d,) + ia[1:]), twin.get((ib[0] + d,) + ib[1:])) for d in range(-NV, NV)]
+            new = order
+            for x, y in pairs:
+                if x is not None and y is not None and eng[x] == eng[a] and eng[y] == eng[b]:
+                    new = shift(new, x, y, up) or new
+            if new is order:
+                continue
+            w = [walk(new, mi) for mi in range(nm)]
+            v2 = sum(max(x[1]) for x in w) / nm
+            if v2 < val - COOL * (1.0 - it / moves) * float(np.log(rng.random())):
+                order, cur, val = new, w, v2
+                if val < best[0]:
+                    best = (val, order)
+        return best[1]
+
+    rng = np.random.default_rng(SEED)
+    order = polish(squeak(TRIES, rng), MOVES, rng)
+    end, done = walk(order, 0)[:2]
+    lastuse = {}
+    for i in order:
+        for b in banks[i]:
+            for e2, j in lastuse.get(b, {}).items():
+                if e2 != eng[i]:
+                    deps[i].add(j)
+            lastuse.setdefault(b, {})[eng[i]] = i
     count = {}
     token = [None] * n
     clock = [None] * n
@@ -737,12 +693,13 @@ def plan():
                     if k.get(s2, 0) < c2:
                         k[s2] = c2
         s = o["sem"] if o["kind"] == "dma" else "sent" if o["kind"] == "send" else "q" + e
-        count[s] = count.get(s, 0) + 1
+        count[s] = count.get(s, 0) + o["n"]
         token[i] = (s, count[s])
         clock[i] = dict(k)
         clock[i][s] = count[s]
         steps.append((i, sorted(waits.items())))
-    return {"ops": ops, "steps": steps, "count": count, "span": max(done), "done": done, "order": order, "score": best[4]}
+    return {"ops": ops, "steps": steps, "count": count, "start": [end[i] - cost[i] for i in range(n)],
+            "score": [max(walk(order, mi)[1]) for mi in range(len(table))], "order": order, "deps": deps, "pure": pred, "extra": extra}
 
 
 PLAN = {}
@@ -758,13 +715,10 @@ def rank_program(g, core, T, topo):
     nr = len(T.cores)
     nxt, prv = T.cores[(rank + 1) % nr], T.cores[(rank - 1) % nr]
 
-    def masks(a, b):
+    def lanes(a, b):
         eng = topo.engines(a, b)
-        eng = eng[::max(1, len(eng) // 8)]
-        h = len(eng) // 2
-        return [sum(1 << x for x in eng[:h]), sum(1 << x for x in eng[h:2 * h])], 2 * h
-    mk, nout = masks(core, nxt)
-    nin = masks(prv, core)[1]
+        return eng[::max(1, len(eng) // 8)]
+    mask, nout, nin = sum(1 << x for x in lanes(core, nxt)), len(lanes(core, nxt)), len(lanes(prv, core))
     rid, pid = topo.addr(nxt, core)
     queue = {"v": g.vector, "a": g.scalar, "p": g.tensor, "g": g, "s": g.sync}
 
@@ -776,13 +730,13 @@ def rank_program(g, core, T, topo):
         for s, c in waits:
             q.wait_ge(T.sem[s], c * unit(s))
         if o["kind"] == "send":
-            g.remote_dma_fused([RemoteDMATransfer(dst_ids=[DstId(rid=rid, pnc=pid)], dma_engine_mask=mk[j] if len(o["fn"]) > 1 else mk[0] | mk[1], remote_sem=T.sem[o["sem"]],
-                                                  src=ap(T, a), dst=ap(T, b)) for j, (a, b) in enumerate(o["fn"])],
-                               local_sem=T.sem["sent"])
+            g.remote_dma(ap(T, o["fn"][1]), ap(T, o["fn"][0]), T.sem[o["sem"]], T.sem["sent"], pid, rid, mask)
         elif o["kind"] == "dma":
             o["fn"](g, T).then_inc(T.sem[o["sem"]], 16)
         else:
-            o["fn"](g, T).then_inc(T.sem["q" + o["e"]], 1)
+            r = o["fn"](g, T)
+            for ins in r if isinstance(r, list) else [r]:
+                ins.then_inc(T.sem["q" + o["e"]], 1)
     for s, c in sorted(p["count"].items()):
         if not s.startswith("ld_"):
             g.wait_ge(T.sem[s], c * unit(s))

@@ -6,22 +6,27 @@ NB, BN = 4, 64
 GW = 16 * BN + 16
 SGROUPS = [[0, 1], [2, 3]]
 ZGROUPS = [[0], [1], [2], [3]]
-BGROUPS = [[0, 1, 2, 3]]
+BGROUPS = [[0, 1], [2, 3]]
+BGROUP0 = [[0], [1, 2, 3]]
 ABSB, ASUB = [1, 2, 3], 256
-BATCH = [6, 6, 3]
+BATCH = [4, 4, 4, 3]
 GSUB, HSUB = 32, 5
-VG, VG0 = [32, 160], [32, 96]
+VG, VG0, VG5 = [32, 96, 160], [32, 96], [32, 160]
 OPB = {"c": [2, 3, 2, 2], "e": [3, 3, 2, 3]}
 CNT = {"c": [0, 0, 0, 0], "e": [1, 1, 0, 1]}
 MKV, PV, NVEC = False, True, 12
+SPLIT, PAIR, PT = 1, [0, 1, 2, 3], []
 OM, ETA, KILL, CU, BIG = 2.0 ** 18, 2.0 ** -8, 2.0 ** 40, 4096.0, 8192.0
 WIN = 2 * W + 2 * C + 16
-GATH, SCAT, PEC, LAT, DMAL, COMM, SENDC = 1.56, 3.8, 0.5, 260.0, 2400.0, 3000.0, 1000.0
+GATH, SCAT, PEC, LAT, DMAL, DMAB, COMM, SENDC = 1.56, 3.8, 0.5, 260.0, 2000.0, 0.7, 3000.0, 1000.0
+SENDB, FIRST = 2.5, 2500.0
 MODELS = [{}, {"ga": 1.2, "sc": 1.2, "xc": 1.3, "xsend": 1.5}]
 CHECK = [{}, {"ga": 0.7, "sc": 0.5, "xsend": 1.4}, {"ga": 1.33, "sc": 1.5, "xsend": .8},
          {"xc": 1.5, "xsend": 1.6}, {"ga": 1.33, "sc": 0.6, "xc": .7, "xsend": 1.2, "p": 1.2},
          {"ga": 0.75, "sc": 1.4, "xc": 1.2, "send": 1.5}]
-TRIES, MOVES, BUMP, HEAT, COOL, SEED = 800, 5000, 500.0, 500.0, 100.0, 0
+ALONE, FAR = 0.15, 0.6
+FLAT, QUEUE, WIDE, RAISE = 100.0, {}, 0.3, {}
+TRIES, MOVES, BUMP, HEAT, COOL, EDGE, SEED = 250, 21000, 500.0, 200.0, 150.0, 0.4, 3
 
 BF, HF, F4, I4, U2 = "bfloat16", "float16", "float32", "int32", "uint16"
 SB = {
@@ -38,16 +43,16 @@ SB = {
     "u0": (144, BF), "Wd": (144, BF), "W18": (144, BF), "WS": (144, BF), "WA": (144, BF), "ug": (128, BF), "Eg": (128, BF),
     "one": (BN, BF), "Mc": (8, BF),
 }
-MB = ["E1", "E", "Rr", "ON", "I", "nOm", "p2Om", "Ie", "Iem", "It", "pK", "nK", "pKS", "nKS", "pKON", "nKON", "pKGE", "nKGE",
+MB = ["E1", "E", "Rr", "ON", "I", "nOm", "p2Om", "Ie", "Iem", "It", "pK", "KSI", "nKS", "pKON", "nKLT", "nKGE",
       "LT", "Mv", "nh", "Mr", "pA", "nA", "pR", "nR", "D14", "Sd", "nSd", "Sm", "SmI", "ISd", "Mpar", "nON", "Mt0", "Mt1", "Mth",
-      "Tc", "Doff", "Gm", "pNB", "nNB", "Gc", "Mpr", "Mdi"]
+      "Tc", "Doff", "Gm", "pNB", "nNB", "Gc", "Mpr", "Mdi", "n2", "pH", "nH"]
 MH = ["pMw", "nMw"]
 SB["MB"], SB["MH"] = (128 * len(MB), BF), (128 * len(MH), HF)
 MAT = {k: (b, 128 * i) for b, ks in (("MB", MB), ("MH", MH)) for i, k in enumerate(ks)}
 SCRATCH = {k: ("sbuf", [128, n], d) for k, (n, d) in SB.items()}
 for _b in range(8):
     SCRATCH["ps%d" % _b] = ("psum", [128, 512], F4)
-LOADS = ["nam", "dep0", "dep1", "mrk", "thr", "pic0", "pic1", "pic2", "pic3", "own", "wt"]
+LOADS = ["nam", "dep0", "dep1", "dep2", "dep3", "mrk", "thr", "pic0", "pic1", "pic2", "pic3", "own", "wt"]
 SEMAPHORES = (["qv", "qa", "qp", "qg", "sent", "stored"] + ["ld_" + k for k in LOADS]
               + ["r%s%d_%d" % (k, v, c) for k in "azb" for v in range(1, NV) for c in range(NB)])
 AL, AF = AluOpType, ActivationFunctionType
@@ -78,6 +83,12 @@ def two(*vs):
 def regions(ci):
     slot = {"R": 0, "val": 0, "zt": 1, "oa": 1, "mk": 2, "new": 2, "th": 3, "L1": 7, "P": 4, "F": 4, "A": 0, "Tn": 5, "pr": 6}
     out = {k: V("ps%d" % (4 + ci), BN * s, BN * s + BN) for k, s in slot.items()}
+    if SPLIT:
+        h, q = PAIR[ci] // 2, PAIR[ci] % 2
+        out = {k: V("ps%d" % (4 + q), BN * (s + 3 * h), BN * (s + 3 * h) + BN) for k, s in {"Tn": 1, "pr": 2, "F": 3, "P": 3, "A": 3}.items()}
+        out.update({k: V("ps%d" % (4 + q), 32 * h + s, 32 * h + s + 24) for k, s in {"zt": 0, "oa": 8}.items()})
+        out.update({k: V("ps%d" % (6 + (q if SPLIT == 1 else h)), BN * (s + 4 * (h if SPLIT == 1 else q)), BN * (s + 4 * (h if SPLIT == 1 else q)) + BN)
+                    for k, s in {"R": 0, "val": 0, "mk": 1, "new": 1, "L1": 2, "th": 3}.items()})
     out["Pa"] = V("ps%d" % OPB["c"][ci], BN * ci, BN * ci + BN)
     out["B"] = V("ps%d" % OPB["e"][ci], BN * (NB + ci), BN * (NB + ci) + BN)
     return out
@@ -86,11 +97,11 @@ def regions(ci):
 def build():
     ops = []
     tag = [None]
-    kept = []
+    kept, sends = [], []
 
     def add(eng, cost, reads, writes, fn, kind="c", sem=None, after=None, ck=None):
         ops.append({"e": eng, "cost": cost, "r": [r for r in reads if isv(r)], "w": writes, "fn": fn, "kind": kind, "sem": sem,
-                    "after": after, "ck": ck or (kind if kind != "c" else eng), "tag": tag[0], "cont": False, "n": 1})
+                    "after": after, "ck": ck or (kind if kind != "c" else eng), "tag": tag[0], "cont": False, "n": 1, "behind": []})
         return len(ops) - 1
 
     def a_(T, x):
@@ -166,10 +177,10 @@ def build():
             f = lambda g, T: g.dma_start(ap(T, out), src(T), allow_slow_non_contiguous=True)
         else:
             f = lambda g, T: g.sync.dma_start(ap(T, out), src(T))
-        add(eng, 100, [], [out], f, "dma", "ld_" + name)
+        add(eng, 100 + DMAB * nel(out), [], [out], f, "dma", "ld_" + name)
 
     def store(dst, src):
-        add("s", 100, [src], [], lambda g, T: g.sync.dma_start(dst(T), ap(T, src)), "dma", "stored")
+        add("s", 100 + DMAB * nel(src), [src], [], lambda g, T: g.sync.dma_start(dst(T), ap(T, src)), "dma", "stored")
 
     M = lambda k: V(MAT[k][0], MAT[k][1], MAT[k][1] + 128)
     Ms = lambda k, r: V(MAT[k][0], MAT[k][1] + r, MAT[k][1] + 128, 16)
@@ -186,12 +197,12 @@ def build():
     top8 = (0, 8)
 
     def state(buf, v, ci, part):
-        grp = [x for x in BGROUPS if ci in x][0]
+        grp = [x for x in (BGROUP0 if v == (buf == "Ti") else BGROUPS) if ci in x][0]
         lo = 2 * (v * C + grp[0] * BN) + (part * len(grp) + ci - grp[0]) * BN
         return V(buf, lo, lo + BN)
 
-    load("dep0", V("x0", 0, W // 2), lambda T: T.dep[:, 0:W // 2])
-    load("dep1", V("x0", W // 2, W), lambda T: T.dep[:, W // 2:W])
+    for b in range(4):
+        load("dep%d" % b, V("x0", 512 * b, 512 * b + 512), lambda T, b=b: T.dep[:, 512 * b:512 * b + 512])
     load("nam", V("nami", 0, C), lambda T: T.nam[:])
     load("mrk", V("mrki", 0, C), lambda T: T.mrk[:])
     load("thr", V("thri", 0, NV, 1, top8), lambda T: T.thr[:])
@@ -207,7 +218,7 @@ def build():
     iota(V("ug", 0, 128, 1, top8), [[1, 8], [0, 16]], 0, -1)
     ts(V("Eg", 0, 128, 1, top8), V("ug", 0, 128, 1, top8), 0.0, AL.is_equal)
     for k, c in (("I", 1.0), ("nOm", -OM), ("p2Om", 2 * OM), ("Ie", 1 - ETA), ("Iem", (ETA - 1) * OM),
-                 ("It", -256.0 / OM), ("pK", KILL), ("nK", -KILL)):
+                 ("It", -256.0 / OM), ("pK", KILL)) + ((("n2", -2.0), ("pH", 3 * OM * 2 ** 23), ("nH", -3 * OM * 2 ** 23)) if PT else ()):
         ts(M(k), E0, 0.0, AL.is_equal, c, AL.mult)
     cp(col("p"), V("pi", 0, 1))
     ts(V("si", 0, 1), V("pi", 0, 1), 15, AL.bitwise_and)
@@ -224,7 +235,7 @@ def build():
     for ci in range(NB):
         ms(V("G", ci * GW, ci * GW + 16), -OM)
     for k, x, op, c in (("ON", 100.0, AL.is_lt, 1.0), ("Sd", 1.0, AL.is_equal, 1.0), ("Sm", -1.0, AL.is_equal, 1.0),
-                        ("pKGE", 0.5, AL.is_lt, KILL)):
+                        ("nSd", 1.0, AL.is_equal, -1.0), ("nKGE", 0.5, AL.is_lt, -KILL)):
         ts(M(k), M("E"), x, op, c, AL.mult)
     lin(col("isk"), s, -0.5, 0.5)
     lin(col("x"), s, 1.0, -0.5)
@@ -233,11 +244,10 @@ def build():
     diag(M("Mr"), M("nh"), 0.5)
     load("wt", V("wti", 0, 1), lambda T: T.wt[:], "g")
     diag(M("Mv"), M("LT"), 0.5)
-    for k, x, c in (("nSd", "Sd", -1.0), ("pKS", "Sd", KILL), ("nKS", "Sd", -KILL), ("pKON", "ON", KILL), ("nKON", "ON", -KILL),
-                    ("nKGE", "pKGE", -1.0), ("nON", "ON", -1.0)):
-        lin(M(k), M(x), c)
     diag(M("SmI"), M("Sm"), -1.0)
     diag(M("ISd"), M("nSd"), 1.0)
+    for k, x, c in (("nKS", "Sd", -KILL), ("pKON", "ON", KILL), ("nKLT", "LT", -KILL), ("KSI", "ISd", -KILL), ("nON", "ON", -1.0)):
+        lin(M(k), M(x), c)
     lin(V("W18", 0, 144), V("Wd", 0, 144), 1.0 / OM)
     lin(V("WS", 0, 143), V("Wd", 1, 144), s)
     lin(V("WS", 15, 143, 16), V("Wd", 15, 143, 16), -2048.0)
@@ -339,15 +349,18 @@ def build():
     for b in range(4):
         lo, hi, pb = 512 * b, 512 * b + 512, V("ps%d" % (4 + b), 0, 512)
         ts(V("z0", lo, hi), V("x0", lo, hi), 0.0, AL.is_equal)
-        mm(pb, [(M("I"), V("x0", lo, hi)), (M("nOm"), V("z0", lo, hi))])
-        if b % 2:
-            cp(V("y", lo, hi), pb)
+        if b in (0, 3):
+            mm(pb, [(M("nOm"), V("z0", lo, hi))])
+            tt(V("y", lo, hi), V("x0", lo, hi), pb, AL.add)
         else:
+            mm(pb, [(M("I"), V("x0", lo, hi)), (M("nOm"), V("z0", lo, hi))])
             act(V("y", lo, hi), pb, AF.Identity)
 
     def send(kind, v, ci, a, b):
         sem = "r%s%d_%d" % (kind, v + 1, ci)
-        i = add("g", SENDC, [a], [], (a, b), "send", sem)
+        i = add("g", SENDC + SENDB * max(0, nel(a) - BN) + (0.0 if sends else FIRST), [a], [], (a, b), "send", sem)
+        ops[i]["behind"] = sends[:1]
+        sends.append(i)
         add("n", 0, [], [b], None, "recv", sem, i)
 
     def passes(ci, src, dst, opnd, op, bank, head, late):
@@ -368,7 +381,6 @@ def build():
     one = V("one", 0, BN)
     for v in range(NV):
         last = v == NV - 1
-        floor = 0.0 if last else -OM
         for ci in range(NB):
             c0, g0, R = ci * BN, ci * GW + 16, regions(ci)
             t = lambda k: V(k, c0, c0 + BN)
@@ -377,10 +389,13 @@ def build():
             tag[0] = (v, "g", ci)
             for a in range(0, BN, GSUB):
                 gather(V("G", g0 + 16 * a, g0 + 16 * (a + GSUB)), V("nm", v * C + c0 + a, v * C + c0 + a + GSUB),
-                       vec=c0 + a in (VG if v else VG0))
+                       vec=c0 + a in (VG5 if last else VG if v else VG0))
             P = V("G", g0, g0 + 16 * BN, 16)
             tag[0] = (v, "c", ci)
-            act(R["Pa"], P, AF.Abs)
+            if ci in PT:
+                mm(R["Pa"], [(M("n2"), P), (M("pH"), one), (M("nH"), one), (M("I"), P)])
+            else:
+                act(R["Pa"], P, AF.Abs)
             cnt = passes(ci, "G", "c1", R["Pa"], AL.is_gt, "ps%d" % CNT["c"][ci], [], [(M("Mpar"), th)] if v else [])
             if not PV:
                 mm(R["P"], [(M("I"), P)])
@@ -410,13 +425,16 @@ def build():
             ts(t("pr"), R["pr"], col("g3"), AL.max, col("g5"), AL.add)
             tag[0] = (v, "f", ci)
             mm(R["F"], [(M("I"), xk), (M("p2Om"), t("m"))])
-            ts(V("FB", 2 * c0, 2 * (c0 + BN), 2), R["F"], -2 * OM, AL.add, floor, AL.max)
+            if last:
+                act(V("FB", 2 * c0, 2 * (c0 + BN), 2), R["F"], AF.Relu, -2 * OM)
+            else:
+                ts(V("FB", 2 * c0, 2 * (c0 + BN), 2), R["F"], -2 * OM, AL.add, -OM, AL.max)
             act(V("FB", 2 * c0 + 1, 2 * (c0 + BN), 2), R["B"], AF.Relu if last else AF.Identity, 0.0, 1.0 / (1 - ETA))
             tag[0] = (v, "b", ci)
             for a in range(g0, g0 + 16 * BN, ASUB) if ci in ABSB else []:
                 act(V("Gp", a, a + ASUB), V("G", a, a + ASUB), AF.Abs)
             tag[0] = (v, "m", ci)
-            for grp in BGROUPS:
+            for grp in BGROUPS if v else BGROUP0:
                 if grp[-1] == ci:
                     lo, n = 2 * (v * C + grp[0] * BN), BN * len(grp)
                     if last:
@@ -448,8 +466,8 @@ def build():
             t = lambda k: V(k, c0, c0 + BN)
             Z, thn = V("Zi", v * C + c0, v * C + c0 + BN), state("To", v, ci, 1)
             tag[0] = (v, "l", ci)
-            mm(R["L1"], [(M("SmI"), Z), (M("pKON"), t("isk")), (M("nKON"), t("isk")), (M("ISd"), Z), (M("pKGE"), t("isk")),
-                         (M("nKGE"), t("isk")), (M("Sd"), Z)])
+            mm(R["L1"], [(M("SmI"), Z), (M("pKON"), t("isk")), (M("nKLT"), t("isk")), (M("ISd"), Z), (M("nKGE"), t("isk")),
+                         (M("Sd"), Z)])
             cp(t("L1"), R["L1"])
             tag[0] = (v, "e", ci)
             head = [] if ci in ABSB else [(sel("W18", k), V("G", g0 + k, g0 + 16 * BN, 16)) for k in range(1, 16)]
@@ -459,8 +477,8 @@ def build():
             mm(R["val"], [(M("LT"), t("isk")), (M("Mv"), t("e"))])
             act(t("X"), R["val"], AF.Relu, col("x"))
             nz = R["new"]
-            mm(nz, [(M("I"), t("L1")), (M("nNB"), t("pr")), (M("pK"), t("X")), (M("nK"), t("X")), (M("pNB"), t("pr")),
-                    (M("nSd"), t("L1")), (M("pKS"), t("X")), (M("nKS"), t("X")), (M("Sd"), t("L1"))])
+            mm(nz, [(M("I"), t("L1")), (M("nNB"), t("pr")), (M("pK"), t("X")), (M("KSI"), t("X")), (M("pNB"), t("pr")),
+                    (M("nSd"), t("L1")), (M("nKS"), t("X")), (M("Sd"), t("L1"))])
             act(t("aZ"), nz, AF.Abs)
             if not last:
                 lo = v * C + c0
@@ -474,8 +492,10 @@ def build():
             else:
                 act(t("onm"), t("aZ"), AF.Identity, -1.0)
                 ts(t("omk"), nz, 0.0, AL.is_lt)
-                store(lambda T, c0=c0: T.ynam[:, c0:c0 + BN], t("onm"))
-                store(lambda T, c0=c0: T.ymrk[:, c0:c0 + BN], t("omk"))
+                if ci % 2:
+                    lo, hi = c0 - BN, c0 + BN
+                    store(lambda T, lo=lo, hi=hi: T.ynam[:, lo:hi], V("onm", lo, hi))
+                    store(lambda T, lo=lo, hi=hi: T.ymrk[:, lo:hi], V("omk", lo, hi))
     return ops
 
 
@@ -487,6 +507,7 @@ def plan():
     for i, o in enumerate(ops):
         if o["after"] is not None:
             deps[i].add(o["after"])
+        deps[i].update(o["behind"])
         for x, wr in [(x, False) for x in o["r"]] + [(x, True) for x in o["w"]]:
             for (lo, hi, j, w2, st) in hist.get(x[0], []):
                 if j != i and (wr or w2) and lo < x[2] and x[1] < hi and not (st == x[3] > 1 and (lo - x[1]) % st):
@@ -504,7 +525,8 @@ def plan():
     eng = [o["e"] for o in ops]
     banks = [sorted(set(x[0] for x in o["r"] + o["w"] if x[0] not in SB)) for o in ops]
     pred = [sorted(d) for d in deps]
-    hard = [[j for j in pred[i] if not (ops[i]["cont"] and eng[j] == "p")] for i in range(n)]
+    soft = [set(ops[i]["behind"]) | set(j for j in pred[i] if ops[i]["cont"] and eng[j] == "p") for i in range(n)]
+    hard = [[j for j in pred[i] if j not in soft[i]] for i in range(n)]
     table = [([cost[i] * m.get(ops[i]["ck"], 1.0) for i in range(n)], [extra[i] * m.get("x" + ops[i]["kind"], 1.0) for i in range(n)])
              for m in MODELS + CHECK]
     nm = len(MODELS)
@@ -533,6 +555,46 @@ def plan():
             par[i] = pj
         return end, fin, par
 
+    above = [set() for _ in range(n)]
+    for i in range(n):
+        for j in hard[i]:
+            above[i] |= above[j]
+        hard[i] = [j for j in hard[i] if j not in above[i]]
+        above[i].update(hard[i])
+    slot = {b + e: 8 + 3 * k + x for k, b in enumerate("ps%d" % b for b in range(8)) for x, e in enumerate("vap")}
+    rows = [("vapgsn".index(eng[i]), hard[i], [slot[b + eng[i]] for b in banks[i]],
+             [slot[b + e] for b in banks[i] for e in "vap" if e != eng[i]], table[0][0][i], table[0][1][i], table[1][0][i], table[1][1][i])
+            for i in range(n)]
+
+    def span(order):
+        f0, f1, l0, l1 = [0.0] * n, [0.0] * n, [0.0] * 32, [0.0] * 32
+        for i in order:
+            e, hd, bi, bo, c0, x0, c1, x1 = rows[i]
+            t0, t1 = l0[e], l1[e]
+            for j in hd:
+                if f0[j] > t0:
+                    t0 = f0[j]
+                if f1[j] > t1:
+                    t1 = f1[j]
+            for b in bi:
+                if l0[b] > t0:
+                    t0 = l0[b]
+                if l1[b] > t1:
+                    t1 = l1[b]
+            t0 += c0
+            t1 += c1
+            if e != 5:
+                l0[e], l1[e] = t0, t1
+            t0 += x0
+            t1 += x1
+            f0[i], f1[i] = t0, t1
+            for b in bo:
+                if t0 > l0[b]:
+                    l0[b] = t0
+                if t1 > l1[b]:
+                    l1[b] = t1
+        return (max(f0) + max(f1)) / 2
+
     def chain(w):
         fin, par = w[1:]
         i = max(range(n), key=lambda i: fin[i])
@@ -557,26 +619,29 @@ def plan():
         at = [0.0] * n
         ready = {e: [] for e in "vapgsn"}
         free = {e: 0.0 for e in ready}
-        use = {"ps%d" % b: {} for b in range(8)}
+        lim = {e: {"ps%d" % b: 0.0 for b in range(8)} for e in "vap"}
         order = []
         for i in range(n):
             if not left[i]:
                 ready[eng[i]].append(i)
-
-        def est(i, e):
-            t0 = max(at[i], free[e])
-            for b in banks[i]:
-                for e2, t in use[b].items():
-                    if e2 != e and t > t0:
-                        t0 = t
-            return t0
         known, stale = {}, set(ready)
         while len(order) < n:
             for e in stale:
-                c = [(est(i, e), i) for i in ready[e]]
-                known[e] = (min([t + cs[i] for t, i in c], default=1e18), e, c)
+                c, low, f0 = [], 1e18, free[e]
+                for i in ready[e]:
+                    t = at[i] if at[i] > f0 else f0
+                    for b in banks[i]:
+                        if lim[e][b] > t:
+                            t = lim[e][b]
+                    c.append((t, i))
+                    if t + cs[i] < low:
+                        low = t + cs[i]
+                known[e] = (low, e, c)
             low, e, pick = min(known.values())
-            t, i = max([x for x in pick if x[0] <= low], key=lambda x: prio[x[1]])
+            top = -1e18
+            for t0, j in pick:
+                if t0 <= low and prio[j] > top:
+                    t, i, top = t0, j, prio[j]
             stale = {e, "v", "a", "p"} if banks[i] else {e}
             ready[e].remove(i)
             order.append(i)
@@ -584,9 +649,11 @@ def plan():
                 free[e] = t + cs[i]
             fin = t + cs[i] + ex[i]
             for b in banks[i]:
-                use[b][e] = fin
+                for e2 in "vap":
+                    if e2 != e and fin > lim[e2][b]:
+                        lim[e2][b] = fin
             for j in succ[i]:
-                at[j] = max(at[j], t + cs[i] if ops[j]["cont"] and e == "p" else fin)
+                at[j] = max(at[j], t + cs[i] if i in soft[j] else fin)
                 left[j] -= 1
                 if not left[j]:
                     ready[eng[j]].append(j)
@@ -596,21 +663,29 @@ def plan():
     def squeak(tries, rng):
         tail = [0.0] * n
         for i in range(n - 1, -1, -1):
-            tail[i] = cost[i] + extra[i] + max([tail[j] for j in succ[i]] + [0.0])
+            tail[i] = cost[i] + extra[i] + QUEUE.get(eng[i], 0.0) + max([tail[j] for j in succ[i]] + [0.0])
         name = [ops[i]["id"][1:] if "id" in ops[i] else i for i in range(n)]
-        cur, best, adj, prio = None, None, {}, tail
+        edge = [ops[i]["id"] if ops[i].get("id", [1])[0] in (0, NV - 1) else None for i in range(n)]
+        part = [ops[i]["tag"][1:] if ops[i]["tag"] else "setup" for i in range(n)]
+        cur, best, adj, prio = None, None, {(k[0], int(k[1])): x for k, x in RAISE.items()}, tail
         for it in range(tries):
             new = dict(adj)
             if cur is not None:
+                end, fin, par = cur[1][it % nm]
                 arcs = chain(cur[1][it % nm])
-                for x in range(int(rng.integers(1, 4))):
-                    a, b = arcs[int(rng.integers(len(arcs)))]
+                due = [max([fin[j] for j in hard[b]] + [0.0]) for a, b in arcs]
+                wait = np.array([max(end[a] - t, 0.0) + FLAT for (a, b), t in zip(arcs, due)])
+                for x in rng.choice(len(arcs), int(rng.integers(1, 4)), p=wait / wait.sum()):
+                    a, b = arcs[x]
+                    while par[a] is not None and par[a][1] and end[par[a][0]] > due[x] and rng.random() < 0.5:
+                        a = par[a][0]
                     d = max(0.0, prio[a] - prio[b]) + BUMP * rng.random()
-                    if rng.random() < 0.5:
-                        new[name[a]] = new.get(name[a], 0.0) - d
-                    else:
-                        new[name[b]] = new.get(name[b], 0.0) + d
-            p2 = [tail[i] + new.get(name[i], 0.0) for i in range(n)]
+                    x, d = (a, -d) if rng.random() < 0.5 else (b, d)
+                    k = edge[x] if edge[x] is not None and it > EDGE * tries else name[x]
+                    if part[a] != part[b] and rng.random() < WIDE:
+                        k = part[x]
+                    new[k] = new.get(k, 0.0) + d
+            p2 = [tail[i] + new.get(name[i], 0.0) + new.get(edge[i], 0.0) + new.get(part[i], 0.0) for i in range(n)]
             order = greedy(p2)
             w = [walk(order, mi) for mi in range(nm)]
             val = sum(max(x[1]) for x in w) / nm
@@ -620,28 +695,41 @@ def plan():
                     best = (val, order)
         return best[1]
 
-    def shift(order, a, b, up):
+    tie = [([eng[i]] if eng[i] != "n" else []) + [b + eng[i] for b in banks[i]] for i in range(n)]
+    held = [([eng[i]] if eng[i] != "n" else []) + [b + e for b in banks[i] for e in "vap" if e != eng[i]] for i in range(n)]
+
+    def shift(order, a, b, up, far):
         lo, hi = order.index(a), order.index(b)
         if lo >= hi:
             return None
         seg = order[lo:hi + 1]
-        take = {b if up else a}
-        for i in (reversed(seg) if up else seg):
-            if i in take or any(j in take for j in (succ[i] if up else pred[i])):
+        head, tail = (b, a) if up else (a, b)
+        take, ties, own = {head}, set(), set() if far else set(tie[head])
+        near = succ if up else pred
+        for i in (seg[-2::-1] if up else seg[1:]):
+            if not take.isdisjoint(near[i]) or not ties.isdisjoint(held[i]) or (i != tail and not own.isdisjoint(held[i])):
+                if i == tail:
+                    return None
                 take.add(i)
-        if (a if up else b) in take:
-            return None
+                ties.update(tie[i])
         x, y = [i for i in seg if i in take], [i for i in seg if i not in take]
         return order[:lo] + (x + y if up else y + x) + order[hi + 1:]
 
     def polish(order, moves, rng):
-        cur = [walk(order, mi) for mi in range(nm)]
-        val = sum(max(w[1]) for w in cur) / nm
+        val, cur = span(order), {}
         best = (val, order)
         for it in range(moves):
-            arcs = chain(cur[it % nm])
-            a, b = arcs[int(rng.integers(len(arcs)))]
-            up, alone = rng.random() < 0.5, rng.random() < 0.15
+            if it % nm not in cur:
+                cur[it % nm] = chain(walk(order, it % nm))
+            arcs = cur[it % nm]
+            x = int(rng.integers(len(arcs)))
+            a, b = arcs[x]
+            up, alone, far = rng.random() < 0.5, rng.random() < ALONE, False
+            while rng.random() < FAR:
+                x += 1 if up else -1
+                if not 0 <= x < len(arcs) or (arcs[x][1] != a if up else arcs[x][0] != b):
+                    break
+                a, b, far = (arcs[x][0], b, True) if up else (a, arcs[x][1], True)
             pairs = [(a, b)]
             if not alone and "id" in ops[a] and "id" in ops[b]:
                 ia, ib = ops[a]["id"], ops[b]["id"]
@@ -649,13 +737,12 @@ def plan():
             new = order
             for x, y in pairs:
                 if x is not None and y is not None and eng[x] == eng[a] and eng[y] == eng[b]:
-                    new = shift(new, x, y, up) or new
+                    new = shift(new, x, y, up, far) or new
             if new is order:
                 continue
-            w = [walk(new, mi) for mi in range(nm)]
-            v2 = sum(max(x[1]) for x in w) / nm
+            v2 = span(new)
             if v2 < val - COOL * (1.0 - it / moves) * float(np.log(rng.random())):
-                order, cur, val = new, w, v2
+                order, cur, val = new, {}, v2
                 if val < best[0]:
                     best = (val, order)
         return best[1]
@@ -685,9 +772,7 @@ def plan():
         k = know[e]
         for j in sorted(deps[i], key=lambda j: -done[j]):
             s, c = token[j]
-            if o["cont"] and ops[j]["e"] == "p":
-                continue
-            if k.get(s, 0) < c:
+            if j not in soft[i] and k.get(s, 0) < c:
                 waits[s] = max(waits.get(s, 0), c)
                 for s2, c2 in clock[j].items():
                     if k.get(s2, 0) < c2:
@@ -715,10 +800,7 @@ def rank_program(g, core, T, topo):
     nr = len(T.cores)
     nxt, prv = T.cores[(rank + 1) % nr], T.cores[(rank - 1) % nr]
 
-    def lanes(a, b):
-        eng = topo.engines(a, b)
-        return eng[::max(1, len(eng) // 8)]
-    mask, nout, nin = sum(1 << x for x in lanes(core, nxt)), len(lanes(core, nxt)), len(lanes(prv, core))
+    mask, nout, nin = topo.mask(core, nxt), len(topo.engines(core, nxt)), len(topo.engines(prv, core))
     rid, pid = topo.addr(nxt, core)
     queue = {"v": g.vector, "a": g.scalar, "p": g.tensor, "g": g, "s": g.sync}
 

import numpy as np
from concourse.mybir import AluOpType, ActivationFunctionType

W, C, NV = 2048, 256, 6
NB, BN = 4, 64
GW = 16 * BN + 16
SGROUPS = [[0, 1], [2, 3]]
ZGROUPS = [[0], [1], [2], [3]]
BGROUPS = [[0, 1], [2, 3]]
BGROUP0 = [[0], [1, 2, 3]]
ABSB, ASUB = [1, 2, 3], 256
BATCH = [4, 4, 4, 3]
GSUB, HSUB = 32, 5
VG, VG0, VG5 = [32, 96, 160], [32, 96], [32, 160]
OPB = {"c": [2, 3, 2, 2], "e": [3, 3, 2, 3]}
CNT = {"c": [0, 0, 0, 0], "e": [1, 1, 0, 1]}
MKV, PV, NVEC = False, True, 12
SPLIT, PAIR, PT = 1, [0, 1, 2, 3], []
OM, ETA, KILL, CU, BIG = 2.0 ** 18, 2.0 ** -8, 2.0 ** 40, 4096.0, 8192.0
WIN = 2 * W + 2 * C + 16
GATH, SCAT, PEC, LAT, DMAL, DMAB, COMM, SENDC = 1.56, 3.8, 0.5, 260.0, 2000.0, 0.7, 3000.0, 1000.0
SENDB, FIRST = 2.5, 2500.0
MODELS = [{}, {"ga": 1.2, "sc": 1.2, "xc": 1.3, "xsend": 1.5}]
CHECK = [{}, {"ga": 0.7, "sc": 0.5, "xsend": 1.4}, {"ga": 1.33, "sc": 1.5, "xsend": .8},
         {"xc": 1.5, "xsend": 1.6}, {"ga": 1.33, "sc": 0.6, "xc": .7, "xsend": 1.2, "p": 1.2},
         {"ga": 0.75, "sc": 1.4, "xc": 1.2, "send": 1.5}]
ALONE, FAR = 0.15, 0.6
FLAT, QUEUE, WIDE, RAISE = 100.0, {}, 0.3, {}
TRIES, MOVES, BUMP, HEAT, COOL, EDGE, SEED = 250, 21000, 500.0, 200.0, 150.0, 0.4, 3

BF, HF, F4, I4, U2 = "bfloat16", "float16", "float32", "int32", "uint16"
SB = {
    "y": (WIN, BF), "yo": (WIN, BF), "x0": (W, BF), "z0": (W, BF),
    "nami": (C, I4), "mrki": (C, I4), "owni": (C // 2, I4), "wti": (4, I4), "thri": (8, I4),
    "G": (NB * GW, BF), "Gp": (NB * GW, BF), "c1": (16 * C, BF), "c2": (16 * C, BF),
    "nm": (NV * C, U2), "nmo": (NV * C, U2), "Zi": (NV * C, HF), "Zo": (NV * C, HF), "Ti": (NV * 2 * C, BF), "To": (NV * 2 * C, BF),
    "cl": (C, BF), "isk": (C, BF), "Zk": (C, HF), "xx": (2 * C, BF), "m": (C, BF), "FB": (2 * C, BF), "pr": (C, HF),
    "L1": (C, HF), "e": (C, BF), "X": (C, BF), "aZ": (C, F4), "offk": (32, U2), "offs": (32, U2),
    "a128": (16, BF), "cix": (C, BF), "OwnT": (C, HF), "owe": (C // 2, HF), "owo": (C // 2, HF),
    "onm": (C, F4), "omk": (C, F4), "oct": (C, F4),
    "ta": (C, F4), "tb": (C, F4), "thb": (8, BF), "thc": (8, F4), "wm": (4, I4), "wc": (4, F4),
    "pi": (4, I4), "si": (4, I4), "col": (64, F4), "jj": (16, F4), "MK": (16, F4), "OH": (16, F4),
    "u0": (144, BF), "Wd": (144, BF), "W18": (144, BF), "WS": (144, BF), "WA": (144, BF), "ug": (128, BF), "Eg": (128, BF),
    "one": (BN, BF), "Mc": (8, BF),
}
MB = ["E1", "E", "Rr", "ON", "I", "nOm", "p2Om", "Ie", "Iem", "It", "pK", "KSI", "nKS", "pKON", "nKLT", "nKGE",
      "LT", "Mv", "nh", "Mr", "pA", "nA", "pR", "nR", "D14", "Sd", "nSd", "Sm", "SmI", "ISd", "Mpar", "nON", "Mt0", "Mt1", "Mth",
      "Tc", "Doff", "Gm", "pNB", "nNB", "Gc", "Mpr", "Mdi", "n2", "pH", "nH"]
MH = ["pMw", "nMw"]
SB["MB"], SB["MH"] = (128 * len(MB), BF), (128 * len(MH), HF)
MAT = {k: (b, 128 * i) for b, ks in (("MB", MB), ("MH", MH)) for i, k in enumerate(ks)}
SCRATCH = {k: ("sbuf", [128, n], d) for k, (n, d) in SB.items()}
for _b in range(8):
    SCRATCH["ps%d" % _b] = ("psum", [128, 512], F4)
LOADS = ["nam", "dep0", "dep1", "dep2", "dep3", "mrk", "thr", "pic0", "pic1", "pic2", "pic3", "own", "wt"]
SEMAPHORES = (["qv", "qa", "qp", "qg", "sent", "stored"] + ["ld_" + k for k in LOADS]
              + ["r%s%d_%d" % (k, v, c) for k in "azb" for v in range(1, NV) for c in range(NB)])
AL, AF = AluOpType, ActivationFunctionType


def V(name, lo, hi, step=1, p=None):
    return (name, lo, hi, step, p)


def ap(T, v):
    name, lo, hi, step, p = v
    rows = slice(0, 128) if p is None else slice(p[0], p[1])
    return T[name][rows, lo:hi] if step == 1 else T[name][rows, lo:hi:step]


def nel(v):
    return len(range(v[1], v[2], v[3]))


def isv(x):
    return isinstance(x, tuple)


def two(*vs):
    return all(v[0] in SB and SB[v[0]][1] in (BF, HF, U2) for v in vs)


def regions(ci):
    slot = {"R": 0, "val": 0, "zt": 1, "oa": 1, "mk": 2, "new": 2, "th": 3, "L1": 7, "P": 4, "F": 4, "A": 0, "Tn": 5, "pr": 6}
    out = {k: V("ps%d" % (4 + ci), BN * s, BN * s + BN) for k, s in slot.items()}
    if SPLIT:
        h, q = PAIR[ci] // 2, PAIR[ci] % 2
        out = {k: V("ps%d" % (4 + q), BN * (s + 3 * h), BN * (s + 3 * h) + BN) for k, s in {"Tn": 1, "pr": 2, "F": 3, "P": 3, "A": 3}.items()}
        out.update({k: V("ps%d" % (4 + q), 32 * h + s, 32 * h + s + 24) for k, s in {"zt": 0, "oa": 8}.items()})
        out.update({k: V("ps%d" % (6 + (q if SPLIT == 1 else h)), BN * (s + 4 * (h if SPLIT == 1 else q)), BN * (s + 4 * (h if SPLIT == 1 else q)) + BN)
                    for k, s in {"R": 0, "val": 0, "mk": 1, "new": 1, "L1": 2, "th": 3}.items()})
    out["Pa"] = V("ps%d" % OPB["c"][ci], BN * ci, BN * ci + BN)
    out["B"] = V("ps%d" % OPB["e"][ci], BN * (NB + ci), BN * (NB + ci) + BN)
    return out


def build():
    ops = []
    tag = [None]
    kept, sends = [], []

    def add(eng, cost, reads, writes, fn, kind="c", sem=None, after=None, ck=None):
        ops.append({"e": eng, "cost": cost, "r": [r for r in reads if isv(r)], "w": writes, "fn": fn, "kind": kind, "sem": sem,
                    "after": after, "ck": ck or (kind if kind != "c" else eng), "tag": tag[0], "cont": False, "n": 1, "behind": []})
        return len(ops) - 1

    def a_(T, x):
        return ap(T, x) if isv(x) else x

    def ts(out, in0, s1, op0, s2=None, op1=None):
        n = nel(in0) * (0.5 if two(out, in0) else 1.0)
        if op1 is None:
            f = lambda g, T: g.vector.tensor_scalar(ap(T, out), ap(T, in0), a_(T, s1), None, op0)
        else:
            f = lambda g, T: g.vector.tensor_scalar(ap(T, out), ap(T, in0), a_(T, s1), a_(T, s2), op0, op1)
        add("v", max(64, n), [in0, s1, s2], [out], f)

    def lin(out, in0, a, b=0.0):
        if len(kept) < NVEC:
            kept.append(out)
            return ts(out, in0, a, AL.mult, b, AL.add)
        act(out, in0, AF.Identity, b, a)

    def cp(out, in0):
        n = nel(in0) * (0.5 if two(out, in0) else 1.0)
        add("v", max(64, n), [in0], [out], lambda g, T: g.vector.tensor_copy(ap(T, out), ap(T, in0)))

    def tt(out, in0, in1, op):
        n = nel(in0) * (2.0 if in0[0] in SB and in1[0] in SB else 1.0)
        add("v", max(64, n), [in0, in1], [out], lambda g, T: g.vector.tensor_tensor(ap(T, out), ap(T, in0), ap(T, in1), op))

    def compare(rows, opnd, op):
        f = lambda g, T: [g.vector.tensor_tensor(ap(T, o), ap(T, x), ap(T, opnd), op) for o, x in rows]
        i = add("v", BN * len(rows), [x for o, x in rows] + [opnd], [o for o, x in rows], f)
        ops[i]["n"] = len(rows)

    def ms(out, c):
        add("v", max(64, nel(out) * (0.5 if two(out) else 1.0)), [], [out], lambda g, T: g.vector.memset(ap(T, out), c))

    def act(out, in0, func, bias=0.0, scale=1.0):
        add("a", max(80, nel(in0)), [in0, bias, scale], [out],
            lambda g, T: g.scalar.activation(ap(T, out), ap(T, in0), func, bias=a_(T, bias), scale=a_(T, scale)))

    def gather(out, off, win=V("y", 0, W), vec=False):
        if vec:
            return add("v", 60 + GATH * nel(out), [win, off], [out],
                       lambda g, T: g.vector.tensor_copy(ap(T, out), ap(T, win).indirect(ap(T, off))), ck="ga")
        add("a", 80 + GATH * nel(out), [win, off], [out],
            lambda g, T: g.scalar.activation(ap(T, out), ap(T, win).indirect(ap(T, off)), AF.Identity), ck="ga")

    def mm(out, terms, first=True, last=True, whole=None):
        cost = sum(max(64, nel(r)) for l, r in terms) * PEC + 20

        def f(g, T):
            ins = None
            for i, (l, r) in enumerate(terms):
                ins = g.tensor.matmul(ap(T, out), ap(T, l), ap(T, r), first and i == 0, last and i == len(terms) - 1)
            return ins
        i = add("p", cost, [x for t in terms for x in t], [whole or out], f)
        ops[i]["cont"] = not first

    def iota(out, pat, base, cm):
        if SB[out[0]][1] == I4:
            f = lambda g, T: g.iota(ap(T, out), pat, base, cm)
        else:
            f = lambda g, T: g.iota(ap(T, out), pat, base, cm, allow_small_or_imprecise_dtypes=True)
        add("g", 160 + 2 * nel(out), [], [out], f)

    def asel(out, in0, pat, op, fill, base, cm):
        add("g", 210 + 2 * nel(out), [in0], [out], lambda g, T: g.affine_select(ap(T, out), ap(T, in0), pat, op, fill, base, cm))

    def diag(out, in0, fill):
        asel(out, in0, [[1, 128]], AL.not_equal, fill, 0, -1)

    def load(name, out, src, eng="s"):
        if eng == "g":
            f = lambda g, T: g.dma_start(ap(T, out), src(T), allow_slow_non_contiguous=True)
        else:
            f = lambda g, T: g.sync.dma_start(ap(T, out), src(T))
        add(eng, 100 + DMAB * nel(out), [], [out], f, "dma", "ld_" + name)

    def store(dst, src):
        add("s", 100 + DMAB * nel(src), [src], [], lambda g, T: g.sync.dma_start(dst(T), ap(T, src)), "dma", "stored")

    M = lambda k: V(MAT[k][0], MAT[k][1], MAT[k][1] + 128)
    Ms = lambda k, r: V(MAT[k][0], MAT[k][1] + r, MAT[k][1] + 128, 16)
    sel = lambda k, r: V(k, 15 - r, 143 - r)
    sel2 = lambda k, b: V(k, 14 - 2 * b, 142 - 2 * b)
    names = {}

    def col(k):
        if k not in names:
            names[k] = len(names)
        return V("col", names[k], names[k] + 1)
    MK = lambda j: V("MK", j, j + 1)
    OH = lambda j: V("OH", j, j + 1)
    top8 = (0, 8)

    def state(buf, v, ci, part):
        grp = [x for x in (BGROUP0 if v == (buf == "Ti") else BGROUPS) if ci in x][0]
        lo = 2 * (v * C + grp[0] * BN) + (part * len(grp) + ci - grp[0]) * BN
        return V(buf, lo, lo + BN)

    for b in range(4):
        load("dep%d" % b, V("x0", 512 * b, 512 * b + 512), lambda T, b=b: T.dep[:, 512 * b:512 * b + 512])
    load("nam", V("nami", 0, C), lambda T: T.nam[:])
    load("mrk", V("mrki", 0, C), lambda T: T.mrk[:])
    load("thr", V("thri", 0, NV, 1, top8), lambda T: T.thr[:])
    for j, grp in enumerate(BGROUPS):
        lo, n = grp[0] * BN, len(grp) * BN
        load("pic%d" % j, V("Ti", 2 * lo, 2 * lo + n), lambda T, lo=lo, n=n: T.pic[:, lo:lo + n])
    load("own", V("owni", 0, C // 2), lambda T: T.own[:])
    E0 = V("u0", 15, 143)
    iota(V("u0", 0, 144), [[1, 144]], -15, -1)
    iota(V("pi", 0, 1), [[0, 1]], 0, 1)
    asel(M("E1"), E0, [[16, 8], [0, 16]], AL.is_ge, 200.0, 15, -1)
    asel(M("E"), M("E1"), [[-16, 8], [0, 16]], AL.is_ge, 200.0, 0, 1)
    iota(V("ug", 0, 128, 1, top8), [[1, 8], [0, 16]], 0, -1)
    ts(V("Eg", 0, 128, 1, top8), V("ug", 0, 128, 1, top8), 0.0, AL.is_equal)
    for k, c in (("I", 1.0), ("nOm", -OM), ("p2Om", 2 * OM), ("Ie", 1 - ETA), ("Iem", (ETA - 1) * OM),
                 ("It", -256.0 / OM), ("pK", KILL)) + ((("n2", -2.0), ("pH", 3 * OM * 2 ** 23), ("nH", -3 * OM * 2 ** 23)) if PT else ()):
        ts(M(k), E0, 0.0, AL.is_equal, c, AL.mult)
    cp(col("p"), V("pi", 0, 1))
    ts(V("si", 0, 1), V("pi", 0, 1), 15, AL.bitwise_and)
    s = col("s")
    cp(s, V("si", 0, 1))
    ts(V("si", 1, 2), V("pi", 0, 1), 1, AL.bitwise_and)
    cp(col("odd"), V("si", 1, 2))
    lin(col("ns"), s, -1.0)
    lin(V("jj", 0, 16), V("u0", 15, 31), 1.0, col("p"))
    ts(V("MK", 0, 16), V("jj", 0, 16), s, AL.is_le)
    ts(V("OH", 0, 16), V("jj", 0, 16), s, AL.is_equal)
    ts(V("Wd", 0, 144), V("u0", 0, 144), col("ns"), AL.is_equal)
    ms(V("one", 0, BN), 1.0)
    for ci in range(NB):
        ms(V("G", ci * GW, ci * GW + 16), -OM)
    for k, x, op, c in (("ON", 100.0, AL.is_lt, 1.0), ("Sd", 1.0, AL.is_equal, 1.0), ("Sm", -1.0, AL.is_equal, 1.0),
                        ("nSd", 1.0, AL.is_equal, -1.0), ("nKGE", 0.5, AL.is_lt, -KILL)):
        ts(M(k), M("E"), x, op, c, AL.mult)
    lin(col("isk"), s, -0.5, 0.5)
    lin(col("x"), s, 1.0, -0.5)
    asel(M("LT"), M("ON"), [[1, 128]], AL.is_gt, 0.0, 0, -1)
    lin(M("nh"), M("LT"), -0.5)
    diag(M("Mr"), M("nh"), 0.5)
    load("wt", V("wti", 0, 1), lambda T: T.wt[:], "g")
    diag(M("Mv"), M("LT"), 0.5)
    diag(M("SmI"), M("Sm"), -1.0)
    diag(M("ISd"), M("nSd"), 1.0)
    for k, x, c in (("nKS", "Sd", -KILL), ("pKON", "ON", KILL), ("nKLT", "LT", -KILL), ("KSI", "ISd", -KILL), ("nON", "ON", -1.0)):
        lin(M(k), M(x), c)
    lin(V("W18", 0, 144), V("Wd", 0, 144), 1.0 / OM)
    lin(V("WS", 0, 143), V("Wd", 1, 144), s)
    lin(V("WS", 15, 143, 16), V("Wd", 15, 143, 16), -2048.0)
    lin(col("s8"), col("odd"), -8.0, 16.0)
    lin(col("s16"), s, 8.0, col("s8"))
    lin(V("a128", 0, 16), V("jj", 0, 16), 128.0)
    lin(col("in6"), MK(7), -1.0, MK(1))
    lin(col("sg"), col("odd"), -1.0, 0.5)
    lin(col("par"), col("in6"), col("sg"))
    lin(M("Mpar"), M("ON"), col("par"))
    lin(col("h6"), col("in6"), 0.5)
    lin(V("Mc", 0, 8), Ms("ON", 0), col("h6"))
    lin(col("t0"), col("in6"), CU)
    lin(col("t1"), MK(6), -CU / 2, CU / 2)
    lin(M("Mt0"), M("I"), col("t0"))
    lin(M("Mt1"), M("Sd"), col("t1"))
    tt(M("Mth"), M("Mt0"), M("Mt1"), AL.add)
    lin(col("t2"), col("in6"), CU / 2, -0.5)
    lin(col("t3"), OH(0), BIG, OH(8))
    lin(col("thb"), col("t2"), 1.0, col("t3"))
    lin(col("tc"), OH(0), -256.0)
    lin(M("Tc"), M("ON"), col("tc"))
    lin(col("gc"), OH(7), 16.0)
    lin(M("Gc"), M("ON"), col("gc"))
    lin(col("f0"), OH(0), 2.0, -1.0)
    lin(M("Rr"), M("E"), 1.0, s)
    ts(M("pA"), M("Rr"), 12.0, AL.is_lt, CU, AL.mult)
    lin(M("nA"), M("pA"), -1.0)
    lin(col("lo8"), MK(8), -1.0, 1.0)
    lin(col("lo12"), MK(12), -1.0, 1.0)
    ts(col("un"), col("lo8"), col("lo12"), AL.add, 4 * CU, AL.mult)
    lin(col("u15"), OH(15), 2048.0, col("un"))
    lin(col("mg"), col("u15"), 1.5 * 2 ** 23)
    lin(M("pR"), M("I"), col("mg"))
    lin(M("nR"), M("pR"), -1.0)
    lin(col("r8"), MK(8), -8.0, s)
    ts(col("cr"), col("r8"), col("lo12"), AL.mult, -CU, AL.mult)
    lin(col("o1"), col("un"), -0.5, col("cr"))
    lin(col("o2"), col("lo12"), CU / 2, col("o1"))
    lin(M("Doff"), M("I"), col("o2"))
    lin(col("o3"), OH(14), -0.5)
    lin(col("o4"), OH(15), 1024.0, col("o3"))
    lin(Ms("Doff", 15), Ms("ON", 15), col("o4"))
    ts(col("pa"), MK(8), MK(12), AL.subtract, OH(14), AL.add)
    ts(col("g1"), col("lo12"), OH(14), AL.add, BIG / 2, AL.mult)
    lin(col("g2"), col("pa"), -2048.0, col("g1"))
    lin(col("g6"), OH(15), BIG - 1, col("cr"))
    lin(col("g3"), col("g2"), 1.0, col("g6"))
    ts(col("g4"), OH(12), col("pa"), AL.subtract, 2048.0, AL.mult)
    lin(col("g5"), col("g3"), -1.0, col("g4"))
    lin(M("Gm"), M("pA"), OH(7))
    lin(col("g7"), OH(7), -BIG / 2)
    lin(col("g8"), OH(8), BIG / 2, col("g7"))
    lin(Ms("Gm", 14), Ms("ON", 14), col("g7"))
    lin(Ms("Gm", 15), Ms("ON", 15), col("g8"))
    ts(V("wm", 0, 1), V("wti", 0, 1), W - 1, AL.bitwise_and)
    cp(V("wc", 0, 1), V("wm", 0, 1))
    ts(M("pMw"), sel("Wd", 15), V("wc", 0, 1), AL.mult)
    ts(M("nMw"), M("pMw"), -1.0, AL.mult)
    ts(col("n1"), col("lo12"), col("lo8"), AL.subtract, col("lo8"), AL.subtract)
    lin(col("nb"), OH(12), 4.0, col("n1"))
    ts(col("nb0"), col("nb"), col("lo8"), AL.add, OH(13), AL.subtract)
    lin(col("nb15"), OH(15), 1.0, col("nb"))
    lin(M("pNB"), M("ON"), col("nb"))
    lin(M("nNB"), M("nON"), col("nb"))
    lin(Ms("pNB", 0), Ms("ON", 0), col("nb0"))
    lin(Ms("pNB", 15), Ms("ON", 15), col("nb15"))
    lin(col("wa"), OH(14), 1.0, col("lo8"))
    lin(col("wb"), OH(14), 2.0, col("n1"))
    lin(V("WA", 0, 143), V("Wd", 1, 144), col("wa"))
    lin(V("WA", 15, 143, 16), V("Wd", 15, 143, 16), col("wb"))
    lin(col("oc"), col("odd"), 10240.0, 2047.0)
    lin(col("p1"), col("p"), 1.0, 1.0)
    lin(col("p2"), col("p"), 1.0, 129.0)
    lin(V("cix", 0, 128), E0, 1.0, col("p1"))
    lin(V("cix", 128, 256), E0, 1.0, col("p2"))
    lin(M("D14"), M("I"), OH(14))
    ts(col("d1"), MK(4), MK(8), AL.add, MK(12), AL.add)
    lin(col("d2"), col("d1"), -4.0, 8.0)
    ts(M("Mpr"), M("E"), col("d2"), AL.is_equal)
    lin(col("d3"), MK(8), -8.0)
    ts(M("Mdi"), M("E"), col("d3"), AL.is_equal)
    ts(V("owe", 0, 128), V("owni", 0, 128), 1.0, AL.add, col("lo8"), AL.mult)
    ts(V("owo", 0, 128), V("owni", 0, 128), 1.0, AL.add, MK(8), AL.mult)
    ts(col("o5"), MK(12), MK(8), AL.subtract, 2048.0, AL.mult)
    mm(V("ps1", 128, 256), [(M("Mpr"), V("owe", 0, 128)), (M("Mdi"), V("owe", 0, 128)), (M("D14"), V("cix", 0, C, 2))])
    mm(V("ps1", 256, 384), [(M("Mpr"), V("owo", 0, 128)), (M("Mdi"), V("owo", 0, 128)), (M("D14"), V("cix", 1, C, 2))])
    ts(V("OwnT", 0, C, 2), V("ps1", 128, 256), col("o5"), AL.add)
    ts(V("OwnT", 1, C, 2), V("ps1", 256, 384), col("o5"), AL.add)
    cp(V("thb", 0, NV, 1, top8), V("thri", 0, NV, 1, top8))
    mm(V("ps1", 0, NV), [(V("Eg", 0, 128, 1, top8), V("thb", 0, NV, 1, top8))])
    lin(V("thc", 0, NV), V("ps1", 0, NV), -1.0, 0.5)
    cp(V("nm", 0, C), V("nami", 0, C))
    ts(V("ta", 0, C), V("mrki", 0, C), -2.0, AL.mult, 1.0, AL.add)
    ts(V("tb", 0, C), V("nami", 0, C), 1.0, AL.add)
    tt(V("Zi", 0, C), V("ta", 0, C), V("tb", 0, C), AL.mult)
    for ci in range(NB):
        lin(state("Ti", 0, ci, 1), V("one", 0, BN), col("f0"))
    for b in range(4):
        lo, hi, pb = 512 * b, 512 * b + 512, V("ps%d" % (4 + b), 0, 512)
        ts(V("z0", lo, hi), V("x0", lo, hi), 0.0, AL.is_equal)
        if b in (0, 3):
            mm(pb, [(M("nOm"), V("z0", lo, hi))])
            tt(V("y", lo, hi), V("x0", lo, hi), pb, AL.add)
        else:
            mm(pb, [(M("I"), V("x0", lo, hi)), (M("nOm"), V("z0", lo, hi))])
            act(V("y", lo, hi), pb, AF.Identity)

    def send(kind, v, ci, a, b):
        sem = "r%s%d_%d" % (kind, v + 1, ci)
        i = add("g", SENDC + SENDB * max(0, nel(a) - BN) + (0.0 if sends else FIRST), [a], [], (a, b), "send", sem)
        ops[i]["behind"] = sends[:1]
        sends.append(i)
        add("n", 0, [], [b], None, "recv", sem, i)

    def passes(ci, src, dst, opnd, op, bank, head, late):
        c0, g0 = ci * BN, ci * GW + 16
        cnt, whole = V(bank, 0, BN), V(bank, 0, 512)
        for i in range(0, len(head), HSUB):
            mm(cnt, head[i:i + HSUB], i == 0, False, whole if i == 0 else None)
        i = 1
        for x, w in enumerate(BATCH):
            rows = [(V(dst, 16 * c0 + k * BN, 16 * c0 + (k + 1) * BN), V(src, g0 + k, g0 + 16 * BN, 16)) for k in range(i, i + w)]
            compare(rows, opnd, op)
            opens = i == 1 and not head
            mm(cnt, (list(late) if x == 1 else []) + [(sel("Wd", i + k), rows[k][0]) for k in range(w)], opens, i + w == 16,
               whole if opens else None)
            i += w
        return cnt

    one = V("one", 0, BN)
    for v in range(NV):
        last = v == NV - 1
        for ci in range(NB):
            c0, g0, R = ci * BN, ci * GW + 16, regions(ci)
            t = lambda k: V(k, c0, c0 + BN)
            Z = V("Zi", v * C + c0, v * C + c0 + BN)
            Tp, th, Tn, thn = [state(b, v, ci, j) for b in ("Ti", "To") for j in range(2)]
            tag[0] = (v, "g", ci)
            for a in range(0, BN, GSUB):
                gather(V("G", g0 + 16 * a, g0 + 16 * (a + GSUB)), V("nm", v * C + c0 + a, v * C + c0 + a + GSUB),
                       vec=c0 + a in (VG5 if last else VG if v else VG0))
            P = V("G", g0, g0 + 16 * BN, 16)
            tag[0] = (v, "c", ci)
            if ci in PT:
                mm(R["Pa"], [(M("n2"), P), (M("pH"), one), (M("nH"), one), (M("I"), P)])
            else:
                act(R["Pa"], P, AF.Abs)
            cnt = passes(ci, "G", "c1", R["Pa"], AL.is_gt, "ps%d" % CNT["c"][ci], [], [(M("Mpar"), th)] if v else [])
            if not PV:
                mm(R["P"], [(M("I"), P)])
            tag[0] = (v, "h", ci)
            act(t("cl"), cnt, AF.Sign, V("thc", v, v + 1))
            mm(R["R"], [(M("Mr"), t("cl"))])
            act(t("isk"), R["R"], AF.Relu, col("isk"))
            zt = V(R["zt"][0], R["zt"][1], R["zt"][1] + 8)
            mm(zt, [(M("I"), V("a128", 0, 8))] + [(sel2("WS", b), V("isk", c0 + b, c0 + BN, 8)) for b in range(8)])
            ok = V("offk", 8 * ci, 8 * ci + 8)
            ts(ok, zt, col("s16"), AL.add)
            gather(V("xx", 2 * c0, 2 * (c0 + BN)), ok, V("G", g0 - 16, g0 + 16 * BN))
            xk, Pe = V("xx", 2 * c0, 2 * (c0 + BN), 2), V("xx", 2 * c0 + 1, 2 * (c0 + BN), 2)
            tt(t("m"), xk, P if PV else R["P"], AL.is_gt)
            mm(R["B"], [(M("Ie"), xk), (M("Iem"), t("m"))])
            tag[0] = (v, "o", ci)
            if not MKV:
                mm(R["mk"], [(M("I"), t("isk"))])
            tt(t("Zk"), Z, t("isk") if MKV else R["mk"], AL.mult)
            mm(R["th"], [(M("Mth"), th), (M("nON"), t("Zk"))])
            act(thn, R["th"], AF.Sign, col("thb"))
            tag[0] = (v, "m", ci)
            mm(R["Tn"], [(M("I"), Tp), (M("Tc"), th), (M("It"), Pe)])
            tt(Tn, Pe, R["Tn"], AL.max)
            mm(R["pr"], [(M("Doff"), one), (M("pA"), xk), (M("nMw"), Tn), (M("pR"), one), (M("nR"), one),
                         (M("nA"), xk), (M("pMw"), Tn), (M("I"), t("OwnT")), (sel("Wd", 13), t("Zk")), (M("Gm"), thn)])
            ts(t("pr"), R["pr"], col("g3"), AL.max, col("g5"), AL.add)
            tag[0] = (v, "f", ci)
            mm(R["F"], [(M("I"), xk), (M("p2Om"), t("m"))])
            if last:
                act(V("FB", 2 * c0, 2 * (c0 + BN), 2), R["F"], AF.Relu, -2 * OM)
            else:
                ts(V("FB", 2 * c0, 2 * (c0 + BN), 2), R["F"], -2 * OM, AL.add, -OM, AL.max)
            act(V("FB", 2 * c0 + 1, 2 * (c0 + BN), 2), R["B"], AF.Relu if last else AF.Identity, 0.0, 1.0 / (1 - ETA))
            tag[0] = (v, "b", ci)
            for a in range(g0, g0 + 16 * BN, ASUB) if ci in ABSB else []:
                act(V("Gp", a, a + ASUB), V("G", a, a + ASUB), AF.Abs)
            tag[0] = (v, "m", ci)
            for grp in BGROUPS if v else BGROUP0:
                if grp[-1] == ci:
                    lo, n = 2 * (v * C + grp[0] * BN), BN * len(grp)
                    if last:
                        store(lambda T, a=grp[0] * BN, n=n: T.ypic[:, a:a + n], V("To", lo, lo + n))
                    else:
                        send("b", v, ci, V("To", lo, lo + 2 * n), V("Ti", lo + 2 * C, lo + 2 * C + 2 * n))
            if last:
                tag[0] = (v, "l", ci)
                A = V(R["A"][0], R["A"][1], R["A"][2], 1, top8)
                mm(A, [(V("Mc", 0, 8), thn)])
                act(V("oct", c0, c0 + BN, 1, top8), A, AF.Identity, 3.0)
                ts(V("yo", 512 * ci, 512 * ci + 512), V("y", 512 * ci, 512 * ci + 512), 0.0, AL.max)
        for grp in SGROUPS:
            tag[0] = (v, "s", grp[-1])
            lo, hi = grp[0] * BN, grp[-1] * BN + BN
            oT = regions(grp[-1])["oa"]
            oa = V(oT[0], oT[1], oT[1] + (hi - lo) // 8)
            mm(oa, [(sel2("WA", b), V("pr", lo + b, hi, 8)) for b in range(8)])
            off = V("offs", lo // 8, hi // 8)
            ts(off, oa, col("oc"), AL.add)
            win, fb = V("yo" if last else "y", 0, WIN), V("FB", 2 * lo, 2 * hi)
            add("v", 60 + SCAT * nel(fb), [off, fb], [win],
                lambda g, T, win=win, off=off, fb=fb: g.vector.tensor_copy(ap(T, win).indirect(ap(T, off)), ap(T, fb)), ck="sc")
        if last:
            store(lambda T: T.ydep[:], V("yo", 0, W))
            store(lambda T: T.ycut[:], V("oct", 0, C, 1, top8))
        for ci in range(NB):
            c0, g0, R = ci * BN, ci * GW + 16, regions(ci)
            t = lambda k: V(k, c0, c0 + BN)
            Z, thn = V("Zi", v * C + c0, v * C + c0 + BN), state("To", v, ci, 1)
            tag[0] = (v, "l", ci)
            mm(R["L1"], [(M("SmI"), Z), (M("pKON"), t("isk")), (M("nKLT"), t("isk")), (M("ISd"), Z), (M("nKGE"), t("isk")),
                         (M("Sd"), Z)])
            cp(t("L1"), R["L1"])
            tag[0] = (v, "e", ci)
            head = [] if ci in ABSB else [(sel("W18", k), V("G", g0 + k, g0 + 16 * BN, 16)) for k in range(1, 16)]
            cnt = passes(ci, "Gp" if ci in ABSB else "G", "c2", R["B"], AL.is_lt, "ps%d" % CNT["e"][ci], head, [(M("Gc"), thn)])
            tag[0] = (v, "t", ci)
            act(t("e"), cnt, AF.Sign, -17.5)
            mm(R["val"], [(M("LT"), t("isk")), (M("Mv"), t("e"))])
            act(t("X"), R["val"], AF.Relu, col("x"))
            nz = R["new"]
            mm(nz, [(M("I"), t("L1")), (M("nNB"), t("pr")), (M("pK"), t("X")), (M("KSI"), t("X")), (M("pNB"), t("pr")),
                    (M("nSd"), t("L1")), (M("nKS"), t("X")), (M("Sd"), t("L1"))])
            act(t("aZ"), nz, AF.Abs)
            if not last:
                lo = v * C + c0
                ts(V("nmo", lo, lo + BN), t("aZ"), -1.0, AL.add)
                send("a", v, ci, V("nmo", lo, lo + BN), V("nm", lo + C, lo + C + BN))
                cp(V("Zo", lo, lo + BN), nz)
                for grp in ZGROUPS:
                    if grp[-1] == ci:
                        lo, hi = v * C + grp[0] * BN, v * C + c0 + BN
                        send("z", v, ci, V("Zo", lo, hi), V("Zi", lo + C, hi + C))
            else:
                act(t("onm"), t("aZ"), AF.Identity, -1.0)
                ts(t("omk"), nz, 0.0, AL.is_lt)
                if ci % 2:
                    lo, hi = c0 - BN, c0 + BN
                    store(lambda T, lo=lo, hi=hi: T.ynam[:, lo:hi], V("onm", lo, hi))
                    store(lambda T, lo=lo, hi=hi: T.ymrk[:, lo:hi], V("omk", lo, hi))
    return ops


def plan():
    ops = build()
    n = len(ops)
    deps = [set() for _ in range(n)]
    hist = {}
    for i, o in enumerate(ops):
        if o["after"] is not None:
            deps[i].add(o["after"])
        deps[i].update(o["behind"])
        for x, wr in [(x, False) for x in o["r"]] + [(x, True) for x in o["w"]]:
            for (lo, hi, j, w2, st) in hist.get(x[0], []):
                if j != i and (wr or w2) and lo < x[2] and x[1] < hi and not (st == x[3] > 1 and (lo - x[1]) % st):
                    deps[i].add(j)
        for x in o["w"]:
            hist[x[0]] = [h for h in hist.get(x[0], []) if not (x[1] <= h[0] and h[1] <= x[2] and x[3] == 1 and x[4] is None)]
        for x, wr in [(x, False) for x in o["r"]] + [(x, True) for x in o["w"]]:
            hist.setdefault(x[0], []).append((x[1], x[2], i, wr, x[3]))
    extra = [DMAL if o["kind"] == "dma" else COMM if o["kind"] == "send" else LAT for o in ops]
    succ = [[] for _ in range(n)]
    for i in range(n):
        for j in deps[i]:
            succ[j].append(i)
    cost = [o["cost"] for o in ops]
    eng = [o["e"] for o in ops]
    banks = [sorted(set(x[0] for x in o["r"] + o["w"] if x[0] not in SB)) for o in ops]
    pred = [sorted(d) for d in deps]
    soft = [set(ops[i]["behind"]) | set(j for j in pred[i] if ops[i]["cont"] and eng[j] == "p") for i in range(n)]
    hard = [[j for j in pred[i] if j not in soft[i]] for i in range(n)]
    table = [([cost[i] * m.get(ops[i]["ck"], 1.0) for i in range(n)], [extra[i] * m.get("x" + ops[i]["kind"], 1.0) for i in range(n)])
             for m in MODELS + CHECK]
    nm = len(MODELS)

    def walk(order, mi):
        cs, ex = table[mi]
        end, fin, par = [0.0] * n, [0.0] * n, [None] * n
        last, use = {}, {}
        for i in order:
            e = eng[i]
            j = last.get(e)
            t0, pj = (end[j], (j, True)) if j is not None else (0.0, None)
            for j in hard[i]:
                if fin[j] > t0:
                    t0, pj = fin[j], (j, False)
            for b in banks[i]:
                u = use.setdefault(b, {})
                for e2, j in u.items():
                    if e2 != e and fin[j] > t0:
                        t0, pj = fin[j], (j, True)
                u[e] = i
            if e != "n":
                last[e] = i
            end[i] = t0 + cs[i]
            fin[i] = end[i] + ex[i]
            par[i] = pj
        return end, fin, par

    above = [set() for _ in range(n)]
    for i in range(n):
        for j in hard[i]:
            above[i] |= above[j]
        hard[i] = [j for j in hard[i] if j not in above[i]]
        above[i].update(hard[i])
    slot = {b + e: 8 + 3 * k + x for k, b in enumerate("ps%d" % b for b in range(8)) for x, e in enumerate("vap")}
    rows = [("vapgsn".index(eng[i]), hard[i], [slot[b + eng[i]] for b in banks[i]],
             [slot[b + e] for b in banks[i] for e in "vap" if e != eng[i]], table[0][0][i], table[0][1][i], table[1][0][i], table[1][1][i])
            for i in range(n)]

    def span(order):
        f0, f1, l0, l1 = [0.0] * n, [0.0] * n, [0.0] * 32, [0.0] * 32
        for i in order:
            e, hd, bi, bo, c0, x0, c1, x1 = rows[i]
            t0, t1 = l0[e], l1[e]
            for j in hd:
                if f0[j] > t0:
                    t0 = f0[j]
                if f1[j] > t1:
                    t1 = f1[j]
            for b in bi:
                if l0[b] > t0:
                    t0 = l0[b]
                if l1[b] > t1:
                    t1 = l1[b]
            t0 += c0
            t1 += c1
            if e != 5:
                l0[e], l1[e] = t0, t1
            t0 += x0
            t1 += x1
            f0[i], f1[i] = t0, t1
            for b in bo:
                if t0 > l0[b]:
                    l0[b] = t0
                if t1 > l1[b]:
                    l1[b] = t1
        return (max(f0) + max(f1)) / 2

    def chain(w):
        fin, par = w[1:]
        i = max(range(n), key=lambda i: fin[i])
        arcs = []
        while par[i] is not None:
            if par[i][1]:
                arcs.append((par[i][0], i))
            i = par[i][0]
        return arcs

    twin, seen = {}, {}
    for i in range(n):
        tg = ops[i]["tag"]
        if tg is not None:
            seen[tg] = seen.get(tg, 0) + 1
            twin[tg + (seen[tg],)] = i
            ops[i]["id"] = tg + (seen[tg],)

    def greedy(prio):
        cs, ex = table[0]
        left = [len(d) for d in pred]
        at = [0.0] * n
        ready = {e: [] for e in "vapgsn"}
        free = {e: 0.0 for e in ready}
        lim = {e: {"ps%d" % b: 0.0 for b in range(8)} for e in "vap"}
        order = []
        for i in range(n):
            if not left[i]:
                ready[eng[i]].append(i)
        known, stale = {}, set(ready)
        while len(order) < n:
            for e in stale:
                c, low, f0 = [], 1e18, free[e]
                for i in ready[e]:
                    t = at[i] if at[i] > f0 else f0
                    for b in banks[i]:
                        if lim[e][b] > t:
                            t = lim[e][b]
                    c.append((t, i))
                    if t + cs[i] < low:
                        low = t + cs[i]
                known[e] = (low, e, c)
            low, e, pick = min(known.values())
            top = -1e18
            for t0, j in pick:
                if t0 <= low and prio[j] > top:
                    t, i, top = t0, j, prio[j]
            stale = {e, "v", "a", "p"} if banks[i] else {e}
            ready[e].remove(i)
            order.append(i)
            if e != "n":
                free[e] = t + cs[i]
            fin = t + cs[i] + ex[i]
            for b in banks[i]:
                for e2 in "vap":
                    if e2 != e and fin > lim[e2][b]:
                        lim[e2][b] = fin
            for j in succ[i]:
                at[j] = max(at[j], t + cs[i] if i in soft[j] else fin)
                left[j] -= 1
                if not left[j]:
                    ready[eng[j]].append(j)
                    stale.add(eng[j])
        return order

    def squeak(tries, rng):
        tail = [0.0] * n
        for i in range(n - 1, -1, -1):
            tail[i] = cost[i] + extra[i] + QUEUE.get(eng[i], 0.0) + max([tail[j] for j in succ[i]] + [0.0])
        name = [ops[i]["id"][1:] if "id" in ops[i] else i for i in range(n)]
        edge = [ops[i]["id"] if ops[i].get("id", [1])[0] in (0, NV - 1) else None for i in range(n)]
        part = [ops[i]["tag"][1:] if ops[i]["tag"] else "setup" for i in range(n)]
        cur, best, adj, prio = None, None, {(k[0], int(k[1])): x for k, x in RAISE.items()}, tail
        for it in range(tries):
            new = dict(adj)
            if cur is not None:
                end, fin, par = cur[1][it % nm]
                arcs = chain(cur[1][it % nm])
                due = [max([fin[j] for j in hard[b]] + [0.0]) for a, b in arcs]
                wait = np.array([max(end[a] - t, 0.0) + FLAT for (a, b), t in zip(arcs, due)])
                for x in rng.choice(len(arcs), int(rng.integers(1, 4)), p=wait / wait.sum()):
                    a, b = arcs[x]
                    while par[a] is not None and par[a][1] and end[par[a][0]] > due[x] and rng.random() < 0.5:
                        a = par[a][0]
                    d = max(0.0, prio[a] - prio[b]) + BUMP * rng.random()
                    x, d = (a, -d) if rng.random() < 0.5 else (b, d)
                    k = edge[x] if edge[x] is not None and it > EDGE * tries else name[x]
                    if part[a] != part[b] and rng.random() < WIDE:
                        k = part[x]
                    new[k] = new.get(k, 0.0) + d
            p2 = [tail[i] + new.get(name[i], 0.0) + new.get(edge[i], 0.0) + new.get(part[i], 0.0) for i in range(n)]
            order = greedy(p2)
            w = [walk(order, mi) for mi in range(nm)]
            val = sum(max(x[1]) for x in w) / nm
            if cur is None or val < cur[0] - HEAT * (1.0 - it / tries) * float(np.log(rng.random())):
                cur, adj, prio = (val, w), new, p2
                if best is None or val < best[0]:
                    best = (val, order)
        return best[1]

    tie = [([eng[i]] if eng[i] != "n" else []) + [b + eng[i] for b in banks[i]] for i in range(n)]
    held = [([eng[i]] if eng[i] != "n" else []) + [b + e for b in banks[i] for e in "vap" if e != eng[i]] for i in range(n)]

    def shift(order, a, b, up, far):
        lo, hi = order.index(a), order.index(b)
        if lo >= hi:
            return None
        seg = order[lo:hi + 1]
        head, tail = (b, a) if up else (a, b)
        take, ties, own = {head}, set(), set() if far else set(tie[head])
        near = succ if up else pred
        for i in (seg[-2::-1] if up else seg[1:]):
            if not take.isdisjoint(near[i]) or not ties.isdisjoint(held[i]) or (i != tail and not own.isdisjoint(held[i])):
                if i == tail:
                    return None
                take.add(i)
                ties.update(tie[i])
        x, y = [i for i in seg if i in take], [i for i in seg if i not in take]
        return order[:lo] + (x + y if up else y + x) + order[hi + 1:]

    def polish(order, moves, rng):
        val, cur = span(order), {}
        best = (val, order)
        for it in range(moves):
            if it % nm not in cur:
                cur[it % nm] = chain(walk(order, it % nm))
            arcs = cur[it % nm]
            x = int(rng.integers(len(arcs)))
            a, b = arcs[x]
            up, alone, far = rng.random() < 0.5, rng.random() < ALONE, False
            while rng.random() < FAR:
                x += 1 if up else -1
                if not 0 <= x < len(arcs) or (arcs[x][1] != a if up else arcs[x][0] != b):
                    break
                a, b, far = (arcs[x][0], b, True) if up else (a, arcs[x][1], True)
            pairs = [(a, b)]
            if not alone and "id" in ops[a] and "id" in ops[b]:
                ia, ib = ops[a]["id"], ops[b]["id"]
                pairs = [(twin.get((ia[0] + d,) + ia[1:]), twin.get((ib[0] + d,) + ib[1:])) for d in range(-NV, NV)]
            new = order
            for x, y in pairs:
                if x is not None and y is not None and eng[x] == eng[a] and eng[y] == eng[b]:
                    new = shift(new, x, y, up, far) or new
            if new is order:
                continue
            v2 = span(new)
            if v2 < val - COOL * (1.0 - it / moves) * float(np.log(rng.random())):
                order, cur, val = new, {}, v2
                if val < best[0]:
                    best = (val, order)
        return best[1]

    rng = np.random.default_rng(SEED)
    order = polish(squeak(TRIES, rng), MOVES, rng)
    end, done = walk(order, 0)[:2]
    lastuse = {}
    for i in order:
        for b in banks[i]:
            for e2, j in lastuse.get(b, {}).items():
                if e2 != eng[i]:
                    deps[i].add(j)
            lastuse.setdefault(b, {})[eng[i]] = i
    count = {}
    token = [None] * n
    clock = [None] * n
    know = {e: {} for e in "vapgs"}
    steps = []
    for i in order:
        o = ops[i]
        e = o["e"]
        if o["kind"] == "recv":
            token[i], clock[i] = (o["sem"], 1), {o["sem"]: 1}
            continue
        waits = {}
        k = know[e]
        for j in sorted(deps[i], key=lambda j: -done[j]):
            s, c = token[j]
            if j not in soft[i] and k.get(s, 0) < c:
                waits[s] = max(waits.get(s, 0), c)
                for s2, c2 in clock[j].items():
                    if k.get(s2, 0) < c2:
                        k[s2] = c2
        s = o["sem"] if o["kind"] == "dma" else "sent" if o["kind"] == "send" else "q" + e
        count[s] = count.get(s, 0) + o["n"]
        token[i] = (s, count[s])
        clock[i] = dict(k)
        clock[i][s] = count[s]
        steps.append((i, sorted(waits.items())))
    return {"ops": ops, "steps": steps, "count": count, "start": [end[i] - cost[i] for i in range(n)],
            "score": [max(walk(order, mi)[1]) for mi in range(len(table))], "order": order, "deps": deps, "pure": pred, "extra": extra}


PLAN = {}


def rank_program(g, core, T, topo):
    rank = T.rank_of(core)
    if rank is None:
        return
    if "p" not in PLAN:
        PLAN["p"] = plan()
    p = PLAN["p"]
    nr = len(T.cores)
    nxt, prv = T.cores[(rank + 1) % nr], T.cores[(rank - 1) % nr]

    mask, nout, nin = topo.mask(core, nxt), len(topo.engines(core, nxt)), len(topo.engines(prv, core))
    rid, pid = topo.addr(nxt, core)
    queue = {"v": g.vector, "a": g.scalar, "p": g.tensor, "g": g, "s": g.sync}

    def unit(s):
        return 1 if s[0] == "q" else nin if s[0] == "r" else nout if s == "sent" else 16
    for i, waits in p["steps"]:
        o = p["ops"][i]
        q = queue[o["e"]]
        for s, c in waits:
            q.wait_ge(T.sem[s], c * unit(s))
        if o["kind"] == "send":
            g.remote_dma(ap(T, o["fn"][1]), ap(T, o["fn"][0]), T.sem[o["sem"]], T.sem["sent"], pid, rid, mask)
        elif o["kind"] == "dma":
            o["fn"](g, T).then_inc(T.sem[o["sem"]], 16)
        else:
            r = o["fn"](g, T)
            for ins in r if isinstance(r, list) else [r]:
                ins.then_inc(T.sem["q" + o["e"]], 1)
    for s, c in sorted(p["count"].items()):
        if not s.startswith("ld_"):
            g.wait_ge(T.sem[s], c * unit(s))
